import numpy as np, ml_dtypes
CORES = [25,29,65,69,153,157,193,197]
N = 8
import mx_ref
BF = ml_dtypes.bfloat16
def gcols(t, e):
    v = np.concatenate([t.reshape(8, 16, -1, 4), np.zeros((8, 16, 1, 4), BF)], axis=2)
    return np.ascontiguousarray(np.stack([v[g][:, e[g]] for g in range(8)])).reshape(128, -1)
def tile(rs):
    return np.stack(rs, axis=2).reshape(128, -1).astype(BF)
def pick(q, e):
    c = np.concatenate([q[0].reshape(128, -1, 4), np.zeros((128, 1, 4), np.uint8)], axis=1); s = np.concatenate([q[1], np.ones((16, 1), np.uint8)], axis=1)
    return (np.ascontiguousarray(c[:, e].reshape(128, -1)), np.ascontiguousarray(s[:, e]))
def join(*qs):
    return (np.concatenate([q[0] for q in qs], axis=1), np.concatenate([q[1] for q in qs], axis=1))
def put(q, e, v):
    c, s = q[0].reshape(128, -1, 4).copy(), q[1].copy(); c[:, e] = v[0].reshape(128, -1, 4); s[:, e] = v[1]
    return (c.reshape(128, -1), s)
def pk(c, s):
    return (np.ascontiguousarray(c), mx_ref.live(s))
def emit(q):
    return q[0], q[1]
def packed(v, rng):
    q = [mx_ref.quantize(np.ascontiguousarray(v[r])) for r in range(N)]
    return np.stack([a for a, b in q]), np.stack([mx_ref.plane(b, rng) for a, b in q])
def f(rng, *shape):
    return mx_ref.flush((rng.standard_normal(shape, dtype=np.float32) * np.exp2(rng.integers(-2, 3, shape[:-1] + (1,)))).astype(BF))
def wide(rng, *shape, cols=0):
    v = rng.standard_normal(shape, dtype=np.float32) * np.exp2(rng.integers(-12, 13, shape)).astype(np.float32)
    if cols: v *= np.repeat(np.exp2(rng.integers(-cols, cols + 1, shape[:-2] + (1, shape[-1] // 4))) * (rng.random(shape[:-2] + (1, shape[-1] // 4)) > 0.0625), 4, axis=-1).astype(np.float32)
    return mx_ref.flush(v.astype(BF))
C, K, R = 192, 24, 2
STEP = [4, 3]
def runs(p):
    here, beside = [], []
    for g in range(8):
        a, s = p[16 * g] + np.float32(0.0), p[16 * g + 1] + np.float32(0.0)
        b = np.append(0, np.sort(1 + np.argsort(-s[1:], kind="stable")[:K - 1]))
        n = np.diff(np.append(b, C))
        e = []
        for i in range(K):
            k = b[i] + np.argsort(-a[b[i]:b[i] + n[i]], kind="stable")[:2]
            e += [(-a[k[0]], k[0], 0, i), (-a[k[-1]], k[-1], 1, i)]
        e = [(q[1], b[q[3]], n[q[3]]) for q in sorted(e)]
        h, m = [], []
        for (k, i, l), (k2, i2, l2) in zip(e, e[1:] + e[:1]):
            o = np.arange(l)
            h.append(i + (k - i + o) % l)
            m.append(i2 + (k2 - i2 + o) % l2)
        here.append(np.concatenate(h))
        beside.append(np.concatenate(m))
    return np.stack(here), np.stack(beside)
def big(v):
    v = v.astype(np.float32)
    v[np.abs(v) < np.float32(2.0 ** -16)] = 0
    return v.astype(BF)
def numbers_of(rng):
    return {"x": big(f(rng, N, 128, 4 * C)), "u": np.array(f(rng, N, 128, 512)), "v": np.array(f(rng, N, 128, 512))}
def weights(rng, still=[]):
    w = np.array(f(rng, N, 128, 2048)).reshape(N, 8, 16, 4, 8, 16, 4)
    for i in still:
        w[:, :, i] = 0
        w[:, :, :, :, :, i] = 0
    c, p = packed(w.reshape(N, 128, 2048), rng)
    return {"wc": c, "ws": p}
def signs(rng):
    return np.stack([rng.permutation(8) % 2 * 2.0 - 1.0 for r in range(N)])
def setup_inputs(rng):
    return {**numbers_of(rng), **weights(rng)}
def setup_inputs_ties(rng):
    d = numbers_of(rng)
    e = rng.permutation(N)
    x = d["x"].reshape(N, 8, 16, C, 4)
    for r in range(N):
        k = np.zeros(C, int) if r == e[0] else rng.permutation(C) % 3
        a = x[r][:, :8, :3].copy()
        a[:, :, 2] = 0
        x[r][:, :8] = a[:, :, k]
    x[e[1]] = 0
    u = d["u"].reshape(N, 8, 16, 8, 16, 4)
    k = u.copy()
    u[:, :, :, :, :2] = 0
    for g in range(8): u[:, g, :8, g, :2] = k[:, g, :8, g, :2]
    return {"x": x.reshape(N, 128, 4 * C), "u": u.reshape(N, 128, 512), "v": d["v"], **weights(rng, range(8))}
def setup_inputs_near(rng):
    d = numbers_of(rng)
    x = np.zeros((N, 8, 16, C, 4), np.float32)
    u = d["u"].reshape(N, 128, 128, 4)
    u[:, :, ::16] = 0
    u[:, :, 1::16] = 0
    kind, c = rng.permutation(N) % 4, [signs(rng), signs(rng)]
    j = np.arange(C)
    for r in range(N):
        size = 1.0 if kind[r] < 2 else 2.0 ** -4
        k = 1.0 if kind[r] == 0 else 2.0 ** -30
        l = C // 2 if kind[r] == 3 else C
        for row in range(2):
            if row == 0: i = (j + rng.integers(0, C, (8, 1))) % l
            else:
                i = (j + 8 * rng.integers(0, C // 8, (8, 1))) % l
                i = i % 8 * (l // 8) + i // 8
            s = i if kind[r] == 3 else (i + 1 - row) // 2
            z = ((s[:, :, None] >> np.arange(8)) & 1) * np.exp2(np.arange(8) - 23.0) * size
            if kind[r] < 2:
                x[r, :, row, :, 0] = c[row][r][:, None]
                for g in rng.permutation(8)[:4]: x[r, g, row, rng.integers(1, C), 0] *= np.float32(2.0 ** 30)
            if kind[r] == 3: x[r, :, row, :, 0] = (8 + j // (C // 2)) * 2.0 ** -30
            x[r, :, 8 + 2 * row] = z[:, :, :4]
            x[r, :, 9 + 2 * row] = z[:, :, 4:]
            for h in range(0, 128, 16):
                u[r, h + row, h + row, 0] = k
                u[r, h + 8 + 2 * row:h + 10 + 2 * row, h + row] = k
        x[r, :, 12:] = rng.integers(4, 8, (8, 4, C, 4)) * 2.0 ** -20 * size
    return {"x": x.reshape(N, 128, 4 * C).astype(BF), "u": u.reshape(N, 128, 512), "v": d["v"], **weights(rng, range(12))}
def setup_inputs_huge(rng):
    d = numbers_of(rng)
    c = np.stack([rng.permutation(C) % 2 * 2.0 - 1.0 for r in range(N)])
    c[rng.permutation(N) < N // 2] = -1
    x = 2.0 ** 30 * (0.6 + 0.2 * rng.random((N, 128, C, 4))) * c[:, None, :, None]
    u = d["u"].reshape(N, 128, 8, 16, 4)
    a = 2.0 ** 30 * (1 - 0.1 * rng.random((N, 128, 8, 2, 4))) * np.stack([signs(rng), signs(rng)], axis=2)[:, None, :, :, None]
    u[:, :, :, :2] = a.astype(np.float32).astype(BF)
    w = np.zeros((N, 128, 4, 128, 4), np.float32)
    i = np.arange(128)
    for b in range(4): w[:, i, b, i, b] = -1
    wc, ws = packed(w.reshape(N, 128, 2048).astype(BF), rng)
    return {"x": x.astype(np.float32).reshape(N, 128, 4 * C).astype(BF), "u": u.reshape(N, 128, 512), "v": d["v"], "wc": wc, "ws": ws}
def setup_inputs_cuts(rng):
    d = numbers_of(rng)
    x = d["x"].reshape(N, 8, 16, C, 4)
    u = d["u"].reshape(N, 128, 128, 4)
    x[:, :, 0] = 0
    u[:, :, 1::16] = 0
    u[:, ::16, ::16, 1] = 0
    for h in range(0, 128, 16):
        u[:, h, h + 1, 0] = 1
        u[:, h, h, 1] = 1024
    m = np.arange(1, K)
    end = [C - 1, C - K, C - K + K // 2 - 1]
    for r in range(N):
        way = [m, C - m, np.where(m < K // 2, m, C - K + m), 2 * m, 3 * m, C // K * m, 1 + rng.permutation(C - 1)[:K - 1], np.append([1, C - 1], 2 + rng.permutation(C - 3)[:K - 3])]
        top, last = rng.permutation(8) % 2, rng.permutation(3)
        for g, i in enumerate(rng.permutation(8)):
            s = -1.0 * rng.integers(0, 3, C)
            s[way[i]] = rng.integers(8, 16, K - 1) * 0.125
            s[0] = 4.0 if top[g] else -4.0
            x[r, g, 0, :, 0] = s.astype(np.float32).astype(BF)
            if i < 3 and last[i] < 2:
                x[r, g, 0, end[i], 1] = 64
                if last[i] == 1: x[r, g, 0, end[i] - 1 - int(rng.integers(C - K)), 1] = 128
    return {"x": x.reshape(N, 128, 4 * C), "u": u.reshape(N, 128, 512), "v": d["v"], **weights(rng, [0])}
def setup_inputs_spread(rng):
    d = setup_inputs(rng)
    d["x"] = big(wide(rng, N, 128, 4 * C, cols=6))
    return d
def check_inputs(d):
    b = []
    for k in ("x", "u", "v"):
        a = np.abs(d[k].astype(np.float32))
        if not (np.isfinite(a).all() and ((a == 0) | (a >= 2.0 ** -30) & (a <= 2.0 ** 30)).all()): b.append("a value of " + k)
    if ((d["wc"] & 0x7F) == 0x7F).any(): b.append("a code of wc that is no number")
    z = np.zeros((128, 4, 4), np.float32)
    z[:, 1] = 2.0 ** -30
    z[:, 2] = 2.0 ** 30
    c, s = emit(mx_ref.quantize(z.reshape(128, 16).astype(BF)))
    for r in range(N):
        p = mx_ref.live(d["ws"][r])
        if not ((p == s[0, 0]) | (p >= s[0, 1]) & (p <= s[0, 2])).all(): b.append("a scale of ws")
    return b
def reference(x, u, v, wc, ws):
    qu = [mx_ref.quantize(u[r]) for r in range(N)]
    lay = [pk(wc[r], ws[r]) for r in range(N)]
    now = [x[r] for r in range(N)]
    for t in range(R):
        at, made = [], []
        for r in range(N):
            e, h = runs(mx_ref.matmul(qu[r], mx_ref.quantize(now[r])))
            z = ((gcols(now[r], e).astype(np.float32) + gcols(now[r], h).astype(np.float32)) * np.float32(0.5)).astype(BF)
            at.append(e)
            made.append(mx_ref.quantize(z))
        for r in range(N):
            q = join(pick(made[r], np.arange(C)), pick(made[r ^ STEP[t]], np.arange(C, 2 * C)))
            h = tile([mx_ref.matmul(pick(lay[r], np.arange(128 * b, 128 * b + 128)), q) * np.float32(0.03125) for b in range(4)])
            back = np.argsort(at[r], axis=1, kind="stable")
            s = gcols(h, back[:, ::2]).astype(np.float32) + gcols(h, back[:, 1::2]).astype(np.float32)
            now[r] = (s * np.float32(0.5) + now[r].astype(np.float32)).astype(BF)
    y, ol = np.zeros((N, 128, C), np.float32), np.zeros((N, 8, 2 * C), np.float32)
    oc, osc = np.zeros((N, 128, 4 * C), np.uint8), np.zeros((N, 16, C), np.uint8)
    for r in range(N):
        q = mx_ref.quantize(now[r])
        y[r] = mx_ref.matmul(mx_ref.quantize(v[r]), q)
        ol[r] = at[r]
        oc[r], osc[r] = emit(q)
    return {"y": y, "ol": ol, "oc": oc, "osc": osc}

@@ -1,0 +1,621 @@
+from concourse.bass import DstId, RemoteDMATransfer
+from concourse.mybir import dt, AluOpType, ActivationFunctionType
+
+C = 192
+STEP = [4, 3]
+CORES_ALL = 256
+BIG = 2.0 ** 96
+PEN = 2.0 ** 90
+F32, BF, I32, U16, U8, MX = "float32", "bfloat16", "int32", "uint16", "uint8", "float8_e4m3fn_x4"
+OPT = {"scan_planes": (2, 3), "vevac": (0, 1, 2), "sc": (0, 1, 10, 11),
+       "wake": 130.0, "cy": 1.0, "ga": 1.5, "far": (4000.0, 7000.0), "load": 2400.0}
+PLAN = []
+
+
+def _sb(n, d):
+    return ("sbuf", [128, n], d)
+
+
+SCRATCH = {
+    "X0": _sb(768, BF), "X1": _sb(768, BF), "X2": _sb(768, BF), "XH": _sb(768, BF),
+    "ut": _sb(512, BF), "vt": _sb(512, BF),
+    "uq": _sb(128, MX), "us": _sb(128, U8), "vq": _sb(128, MX), "vs": _sb(128, U8),
+    "usq": _sb(128, MX), "uss": _sb(128, U8), "ukq": _sb(128, MX), "uks": _sb(128, U8),
+    "wq": _sb(512, MX), "wp": _sb(512, U8),
+    "xq0": _sb(192, MX), "xs0": _sb(192, U8), "xq1": _sb(192, MX), "xs1": _sb(192, U8), "xq2": _sb(192, MX), "xs2": _sb(192, U8),
+    "Za": _sb(768, BF), "Zb": _sb(768, BF), "Ga": _sb(768, BF), "Gb": _sb(768, BF),
+    "zaq": _sb(192, MX), "zas": _sb(192, U8),
+    "zq0": _sb(192, MX), "zs0": _sb(192, U8), "zq1": _sb(192, MX), "zs1": _sb(192, U8),
+    "lq0": _sb(192, MX), "ls0": _sb(192, U8), "lq1": _sb(192, MX), "ls1": _sb(192, U8),
+    "rq": _sb(96, MX), "rs": _sb(192, U8),
+    "HH": _sb(1536, BF), "HQ": _sb(768, BF), "HS": _sb(768, F32), "SQ": _sb(4 * 576, BF), "SO": _sb(4 * 576, BF),
+    "yo": _sb(192, F32), "fo": _sb(384, F32),
+    "ci": _sb(32, I32), "cf": _sb(32, F32), "uo": _sb(16, U16),
+    "cmod": _sb(192, F32), "D": _sb(192, F32), "R": _sb(192, F32), "keep": _sb(192, BF), "iof": _sb(192, F32),
+    "io5": _sb(192, BF), "lur": _sb(192, BF), "lus": _sb(192, BF), "one": _sb(192, BF), "k3": _sb(576, BF),
+    "thr": _sb(144, F32), "k144": _sb(144, BF), "tmpc": _sb(192, F32), "tmpd": _sb(192, F32), "tmpe": _sb(144, F32),
+    "c48": _sb(256, F32), "cw": _sb(96, F32),
+    "sm": _sb(192, F32), "hold": _sb(192, F32), "eq": _sb(192, BF), "ne": _sb(192, BF),
+    "TT": _sb(12 * 192, BF), "SUM": _sb(12 * 96, BF), "U": _sb(6 * 200, BF), "junk": _sb(14 * 200, BF), "acc": _sb(48, F32),
+    "RK": _sb(12, U16), "aS": _sb(400, F32), "r": _sb(192, BF), "pen": _sb(192, BF), "tid": _sb(192, BF),
+    "FW": _sb(400, F32), "rec": _sb(192, BF), "ev": _sb(192, BF), "KW": _sb(592, BF), "OE": _sb(8, U16),
+    "e48": _sb(22 * 56, F32), "d144": _sb(144, F32), "c144": _sb(144, BF), "s144": _sb(144, BF), "RE": _sb(4, U16),
+    "srt": _sb(5 * 56, F32), "sI": _sb(96, I32), "bm": _sb(48, F32), "OL": _sb(4, U16),
+    "XW": _sb(224, F32), "MW": _sb(224, F32), "GW": _sb(128, F32), "VV": _sb(128, I32),
+    "wi": _sb(4 * 64, I32), "wf": _sb(9 * 64, F32), "FG": _sb(64, U16),
+    "bI": _sb(48, I32), "bm2": _sb(24, F32), "OP": _sb(4, U16), "ZW": _sb(96, F32), "ZM": _sb(96, F32), "G2": _sb(48, F32),
+    "V2": _sb(64, I32), "pi": _sb(96, I32), "pf": _sb(128, F32), "PQ": _sb(32, U16),
+}
+for _b in range(8):
+    SCRATCH["ps%d" % _b] = ("psum", [128, 512], F32)
+SEMAPHORES = ["V", "S", "P", "G", "arr0", "arr1", "sent", "hop"] + ["d%d" % _i for _i in range(16)]
+
+
+def _routes(T, topo):
+    cores = list(T.cores)
+    used = set(cores)
+    out = {}
+    for t, s in enumerate(STEP):
+        for r, c in enumerate(cores):
+            d = cores[r ^ s]
+            if topo.may_write(c, d):
+                out[(t, r)] = (d, None)
+                continue
+            near = [k for k in topo.cores_of(c) if k not in used and topo.may_write(k, d) and topo.die(k) == topo.die(c)][:2]
+            used.update(near)
+            far = [k for k in range(CORES_ALL) if k not in used and topo.mates(k, d) and topo.may_write(c, k)
+                   and topo.may_write(k, d) and topo.die(k) == topo.die(c)][:1]
+            used.update(far)
+            out[(t, r)] = (d, near + far)
+    return out
+
+
+def _bits(engs):
+    m = 0
+    for e in engs:
+        m |= 1 << e
+    return m
+
+
+def _relay(g, core, T, topo, routes):
+    for (t, r), (d, via) in routes.items():
+        if via is None or core not in via:
+            continue
+        k = via.index(core)
+        src = T.cores[r]
+        rid, pid = topo.addr(d, core)
+        m = topo.mask(core, d)
+        n = len(topo.engines(core, d))
+        if k < 2:
+            g.wait_ge(T.sem.hop, len(topo.engines(src, core)) // 2)
+            g.remote_dma(T["lq%d" % t][:, 96 * k:96 * k + 96].bitcast(dt.uint8), T.rq[:].bitcast(dt.uint8),
+                         T.sem["arr%d" % t], T.sem.sent, pid, rid, m)
+        else:
+            g.wait_ge(T.sem.hop, len(topo.engines(src, core)))
+            g.remote_dma(T["ls%d" % t][:], T.rs[:], T.sem["arr%d" % t], T.sem.sent, pid, rid, m)
+        g.wait_ge(T.sem.sent, n)
+
+
+def _deps(ops):
+    seen = {}
+    deps = []
+    for i, (q, fn, rd, wr, kind, cost) in enumerate(ops):
+        d = set()
+        for (n, lo, hi, s) in rd:
+            for (j, a, b, s2, w) in seen.get(n, []):
+                if n.startswith("ps"):
+                    if w or ops[j][0] != q:
+                        d.add(j)
+                elif w and a < hi and lo < b and not (s == s2 and (a - lo) % s):
+                    d.add(j)
+        for (n, lo, hi, s) in wr:
+            for (j, a, b, s2, w) in seen.get(n, []):
+                if n.startswith("ps") or (a < hi and lo < b and not (s == s2 and (a - lo) % s)):
+                    d.add(j)
+        for (n, lo, hi, s) in wr:
+            if s == 1:
+                seen[n] = [e for e in seen.get(n, []) if not (lo <= e[1] and e[2] <= hi)]
+            seen.setdefault(n, []).append((i, lo, hi, s, True))
+        for (n, lo, hi, s) in rd:
+            seen.setdefault(n, []).append((i, lo, hi, s, False))
+        d.discard(i)
+        deps.append(d)
+    return deps
+
+
+def _order(ops, deps):
+    n, wake = len(ops), OPT["wake"]
+    pre = [set(d) for d in deps]
+    sends = []
+    for i, o in enumerate(ops):
+        if o[4] is not None and o[4][0] == "remote":
+            if sends:
+                pre[i].add(sends[-1])
+            sends.append(i)
+        if o[4] is not None and o[4][0] == "arrive":
+            pre[i].add(sends[-1])
+    tail = [0.0] * n
+    for i in range(n - 1, -1, -1):
+        tail[i] += ops[i][5]
+        for j in pre[i]:
+            tail[j] = max(tail[j], tail[i] + wake)
+    busy = {}
+    start, end = [0.0] * n, [0.0] * n
+    for i in sorted(range(n), key=lambda k: (-tail[k], k)):
+        q, kind = ops[i][0], ops[i][4]
+        t = max([0.0] + [end[j] + wake for j in pre[i]])
+        hold = 80.0 if kind is not None and kind[0] == "dma" else ops[i][5]
+        for (a, b) in sorted(busy.setdefault(q, [])):
+            if t + hold <= a:
+                break
+            t = max(t, b)
+        busy[q].append((t, t + hold))
+        start[i], end[i] = t, t + ops[i][5]
+    return sorted(range(n), key=lambda k: (start[k], k))
+
+
+def _emit(g, T, ops, last):
+    queue = {"V": g.vector, "S": g.scalar, "P": g.tensor, "G": g, "Y": g.sync}
+    deps = _deps(ops)
+    order = _order(ops, deps)
+    PLAN[:] = [ops, deps, order]
+    pos = {i: k for k, i in enumerate(order)}
+    clock = {q: {} for q in queue}
+    after, waits, signal = {}, {}, set()
+    for i in order:
+        q, kind = ops[i][0], ops[i][4]
+        if kind is not None and kind[0] == "arrive":
+            after[i] = {}
+            continue
+        ck = clock[q]
+        w = []
+        for j in sorted(deps[i], key=lambda k: -pos[k]):
+            key = ops[j][0] if ops[j][4] is None else ("x", j)
+            if ck.get(key, -1) >= pos[j]:
+                continue
+            w.append(j)
+            signal.add(j)
+            for k2, v2 in after[j].items():
+                if ck.get(k2, -1) < v2:
+                    ck[k2] = v2
+            ck[key] = pos[j]
+        waits[i] = w
+        after[i] = dict(ck)
+    count = {q: 0 for q in queue}
+    mark = {}
+    ndma = 0
+    for i in order:
+        q, fn, kind = ops[i][0], ops[i][1], ops[i][4]
+        if kind is not None and kind[0] == "arrive":
+            mark[i] = (kind[1], kind[2])
+            continue
+        for j in waits[i]:
+            queue[q].wait_ge(T.sem[mark[j][0]], mark[j][1])
+        ins = fn()
+        if kind is None:
+            if i in signal:
+                count[q] += 1
+                mark[i] = (q, count[q])
+                ins.then_inc(T.sem[q], 1)
+        elif kind[0] == "dma":
+            mark[i] = ("d%d" % ndma, 16)
+            ins.then_inc(T.sem["d%d" % ndma], 16)
+            ndma += 1
+    for q in ("V", "S", "P", "G"):
+        if count[q]:
+            g.wait_ge(T.sem[q], count[q])
+    for s, n in last:
+        g.wait_ge(T.sem[s], n)
+    for k in range(ndma):
+        g.wait_ge(T.sem["d%d" % k], 16)
+
+
+def rank_program(g, core, T, topo):
+    routes = _routes(T, topo)
+    rank = T.rank_of(core)
+    if rank is None:
+        _relay(g, core, T, topo, routes)
+        return
+    A = AluOpType
+    ACT = ActivationFunctionType
+    ops = []
+    cy, ga = OPT["cy"], OPT["ga"]
+
+    def v(name, a=0, b=None, s=1):
+        if b is None:
+            b = SCRATCH[name][1][1]
+        ap = T[name][:, a:b] if s == 1 else T[name][:, a:b:s]
+        return (ap, [(name, a, b, s)], len(range(a, b, s)), SCRATCH[name][2], False)
+
+    def col(name, j):
+        return v(name, j, j + 1)
+
+    def ind(w, o):
+        return (w[0].indirect(o[0]), w[1] + o[1], 16 * o[2], w[3], True)
+
+    def ap(x):
+        return x[0] if isinstance(x, tuple) else x
+
+    def regs(*xs):
+        out = []
+        for x in xs:
+            if isinstance(x, tuple):
+                out += x[1]
+        return out
+
+    def price(n, first, sides, full=1.0):
+        if first[4]:
+            return 50.0 + n * ga * cy
+        if full == 1.0 and all(s[3] in (BF, U16) for s in sides):
+            full = 0.5
+        return max(64.0, n * full) * cy
+
+    def tt(o, a, b, op):
+        two = 1.01 if a[1][0][0].startswith("ps") else 2.0
+        ops.append(("V", lambda: g.vector.tensor_tensor(o[0], a[0], b[0], op), regs(a, b), o[1], None, price(o[2], a, [], two)))
+
+    def ts(o, a, s1, op0, s2=None, op1=None):
+        c = price(o[2], a, [o, a])
+        if op1 is None:
+            ops.append(("V", lambda: g.vector.tensor_scalar(o[0], a[0], ap(s1), None, op0), regs(a, s1), o[1], None, c))
+        else:
+            ops.append(("V", lambda: g.vector.tensor_scalar(o[0], a[0], ap(s1), ap(s2), op0, op1), regs(a, s1, s2), o[1], None, c))
+
+    def cp(o, a):
+        ops.append(("V", lambda: g.vector.tensor_copy(o[0], a[0]), regs(a), o[1], None, price(o[2], a, [o, a])))
+
+    def scatter(w, off, a):
+        ops.append(("V", lambda: g.vector.tensor_copy(w[0].indirect(off[0]), a[0]), regs(a, off), w[1], None, 50.0 + 3.5 * cy * a[2]))
+
+    def scan(o, d0, d1, init, op0, op1):
+        ops.append(("V", lambda: g.vector.tensor_tensor_scan(o[0], d0[0], d1[0], ap(init), op0, op1), regs(d0, d1, init), o[1],
+                    None, price(o[2], d0, [o, d0, d1])))
+
+    def fill(o, c):
+        ops.append(("V", lambda: g.vector.memset(o[0], c), [], o[1], None, price(o[2], o, [o])))
+
+    def recip(o, a):
+        ops.append(("V", lambda: g.vector.reciprocal(o[0], a[0]), regs(a), o[1], None, 190.0 + 6 * cy * o[2]))
+
+    def quant(q, s, a):
+        ops.append(("V", lambda: g.vector.quantize_mx(q[0], s[0], a[0]), regs(a), regs(q, s), None, 12.0 + 0.26 * a[2]))
+
+    def act(o, a, f=ACT.Copy, bias=None, scale=None, acc=None):
+        kw = {}
+        if bias is not None:
+            kw["bias"] = ap(bias)
+        if scale is not None:
+            kw["scale"] = scale
+        if acc is not None:
+            kw["accum_out"] = acc[0]
+        c = price(o[2], a, [], 1.01) + (20.0 if acc is not None else 0.0)
+        ops.append(("S", lambda: g.scalar.activation(o[0], a[0], f, **kw), regs(a, bias), regs(o, acc), None, c))
+
+    def mm(o, lq, ls, rq, rs):
+        ops.append(("P", lambda: g.tensor.matmul_mx(o[0], lq[0], ls[0], rq[0], rs[0], True, True), regs(lq, ls, rq, rs), o[1],
+                    None, 170.0))
+
+    def iota(o, pat, base, ch=0):
+        c = 130.0 + 2 * cy * o[2]
+        if o[3] == I32:
+            ops.append(("G", lambda: g.iota(o[0], pat, base, ch), [], o[1], None, c))
+        else:
+            ops.append(("G", lambda: g.iota(o[0], pat, base, ch, allow_small_or_imprecise_dtypes=True), [], o[1], None, c))
+
+    def dma(q, o, a, rd, wr):
+        e = g.sync if q == "Y" else g.scalar
+        ops.append((q, lambda: e.dma_start(o, a), rd, wr, ("dma",), OPT["load"]))
+
+    def u8(x):
+        return x[0].bitcast(dt.uint8)
+
+    def u32(x):
+        return (x[0].bitcast(dt.uint32), x[1], x[2], x[3], False)
+
+    dma("Y", T.X0[:], T.x[:], [], v("X0")[1])
+    dma("S", T.ut[:], T.u[:], [], v("ut")[1])
+    dma("Y", u8(v("wq")), T.wc[:], [], v("wq")[1])
+    dma("Y", T.wp[:], T.ws[:], [], v("wp")[1])
+    dma("Y", T.vt[:], T.v[:], [], v("vt")[1])
+
+    sc, planes = OPT["sc"], OPT["scan_planes"]
+    iota(v("ci", 0, 1), [[0, 1]], 0, 1)
+    iota(v("cmod"), [[0, 12], [1, 16]], 0)
+    iota(v("ci", 8, 24), [[-1, 2], [16, 8]], 1)
+    iota(v("iof"), [[1, 192]], 0)
+    iota(v("cf", 4, 7), [[8, 3]], 1)
+    iota(v("tmpe"), [[-16, 3], [1, 48]], 0)
+    iota(v("cf", 12, 16), [[-16, 2], [256, 2]], 15)
+    iota(v("cf", 20, 22), [[-16, 2]], 15)
+    iota(v("tmpd", 0, 64), [[0, 2], [16, 32]], -512)
+    iota(v("tmpd", 64, 96), [[0, 2], [16, 16]], 0)
+    pm = col("cf", 0)
+    fill(v("TT", 0, 12 * 192, 192), 0.0)
+    ts(col("ci", 1), col("ci", 0), 15, A.bitwise_and)
+    fill(col("FW", 0), -BIG)
+    fill(v("FW", 192, 208), -BIG)
+    cp(pm, col("ci", 1))
+    cp(v("uo"), v("ci", 8, 24))
+    ts(v("tmpc"), v("cmod"), pm, A.is_equal)
+    fill(v("aS", 192, 208), 0.0)
+    fill(v("keep"), 1.0)
+    fill(v("keep", 0, 192, 16), 0.0)
+    fill(v("R"), BIG)
+    fill(v("R", 16, 192, 16), -BIG)
+    act(v("D"), v("tmpc"), ACT.Identity, -BIG, 2 * BIG)
+    fill(v("KW", 0, 16), 0.0)
+    fill(v("one"), PEN)
+    for k, i in enumerate(sc):
+        if 16 * i + 16 < C:
+            fill(col("U", 200 * k + 192), -(16.0 * i + 15))
+    fill(v("lus"), -PEN)
+    fill(v("lus", 0, 23), 0.0)
+    fill(v("lur"), BIG)
+    fill(v("lur", 0, 23), -BIG)
+    act(v("io5"), v("iof"), ACT.Copy, None, 1.0 / 512)
+    ts(col("ci", 2), col("ci", 1), 1, A.logical_shift_right)
+    ts(col("ci", 3), col("ci", 1), 1, A.bitwise_and)
+    ts(col("cf", 1), col("ci", 2), 0.5, A.add)
+    ts(col("cf", 2), col("ci", 3), 201.0, A.mult, 95.0, A.add)
+    act(col("cf", 3), pm, ACT.Identity, 0.5, 16.0)
+    ts(v("thr"), v("tmpe"), pm, A.is_lt, -1e-30, A.mult)
+    act(v("cf", 8, 11), v("cf", 4, 7), ACT.Identity, col("cf", 1))
+    act(v("cf", 16, 20), v("cf", 12, 16), ACT.Identity, col("cf", 3))
+    act(v("cf", 22, 24), v("cf", 20, 22), ACT.Identity, col("cf", 3))
+    fill(v("k144"), 1.0)
+    fill(v("k144", 0, 144, 48), 0.0)
+    if planes:
+        fill(v("k3"), 1.0)
+        fill(v("k3", 0, 576, 3), 0.0)
+    act(v("cw"), v("tmpd", 0, 96), ACT.Identity, pm)
+    act(v("c48", 0, 48), v("iof", 0, 48), ACT.Copy, None, 65536.0)
+    fill(v("c48", 48, 96), 1024.0)
+    fill(v("c48", 96, 144), 0.0)
+    act(v("c48", 144, 168), v("iof", 0, 24), ACT.Identity, 65536.0, 2.0 ** 18)
+    act(v("c48", 168, 192), v("iof", 0, 24), ACT.Copy, None, 256.0)
+    fill(v("e48", 5 * 56, 5 * 56 + 2), -1.0)
+    fill(v("srt", 3 * 56, 4 * 56), 0.0)
+    fill(col("srt", 4 * 56), 512.0)
+    fill(v("XW"), 0.0)
+    fill(v("MW"), 0.0)
+    fill(v("ZW"), 0.0)
+    fill(v("ZM"), 0.0)
+    fill(v("wi", 3 * 64, 4 * 64), 0)
+
+    quant(v("uq"), v("us"), v("ut"))
+    quant(v("xq0"), v("xs0"), v("X0"))
+    quant(v("vq"), v("vs"), v("vt"))
+    cp(u32(v("usq")), ind(u32(v("uq")), v("uo", 0, 8)))
+    act(v("uss"), ind(v("us"), v("uo", 0, 8)))
+    cp(u32(v("ukq")), ind(u32(v("uq")), v("uo", 8, 16)))
+    act(v("uks"), ind(v("us"), v("uo", 8, 16)))
+
+    def e48(k, a=0, b=48, s=1):
+        return v("e48", 56 * k + a, 56 * k + b, s)
+
+    def srt(k, a=0, b=48):
+        return v("srt", 56 * k + a, 56 * k + b)
+
+    def wf(k, a=0, b=64):
+        return v("wf", 64 * k + a, 64 * k + b)
+
+    def wi(k, a=0, b=64):
+        return v("wi", 64 * k + a, 64 * k + b)
+
+    last = []
+    sent = [0]
+    for t in range(2):
+        X, Xn = "X%d" % t, "X%d" % (t + 1)
+        xq, xs = v("xq%d" % t), v("xs%d" % t)
+        sV, sS, aP = "ps0", "ps1", "ps2"
+        mm(v(sV, 0, C), v("usq"), v("uss"), xq, xs)
+        mm(v(sS, 0, C), v("usq"), v("uss"), xq, xs)
+        mm(v(aP, 0, C), v("ukq"), v("uks"), xq, xs)
+        tt(v("sm"), v(sV, 0, C), v("D"), A.min)
+        act(v("aS", 0, C), v(aP, 0, C))
+        scan(v("hold"), v("R"), v("sm"), col("D", 0), A.min, A.max)
+        tt(v("eq"), v(sV, 0, C), v("hold"), A.is_equal)
+        scan(v("ne"), v("keep"), v("eq"), 0.0, A.mult, A.subtract)
+        for i in range(12):
+            if i in sc:
+                continue
+            o, m = 192 * i, 16 * i + 16
+            ts(v("TT", o + 1, o + m), v(sV, 1, m), col("hold", m - 1), A.is_ge)
+            if m < C:
+                ts(v("TT", o + m, o + C), v(sV, m, C), col("hold", m - 1), A.is_gt)
+            scan(v("SUM", 96 * i, 96 * i + 96), v("TT", o, o + 96), v("TT", o + 96, o + C), col("ne", m - 1), A.add, A.add)
+        for k, i in enumerate(sc):
+            o, m = 200 * k, 16 * i + 16
+            act(v("U", o + 1, o + C), v(sS, 1, C), ACT.Sign, col("hold", m - 1), -1.0)
+            act(v("junk", o + 1, o + m), v("U", o + 1, o + m), ACT.Relu, None, None, col("acc", k))
+            if m < C:
+                act(v("junk", o + m, o + C + 1), v("U", o + m, o + C + 1), ACT.Relu, None, -1.0, col("acc", 6 + k))
+            act(col("acc", 12 + k), col("acc", k), ACT.Identity, col("ne", m - 1), -1.0)
+            act(col("SUM", 96 * i + 95), col("acc", 12 + k), ACT.Identity, col("acc", 6 + k) if m < C else 191.0)
+        cp(v("RK"), v("SUM", 95, 12 * 96, 96))
+        st = v("pen")
+        cp(v("r"), ind(v("lur"), v("RK")))
+        act(st, ind(v("lus"), v("RK")))
+        scan(v("FW", 1, C), v(aP, 0, C - 1), v("r", 1, C), -BIG, A.max, A.min)
+        scan(v("tid"), st, v("one"), 0.0, A.add, A.add)
+        tt(v("aS", 201, 393), v(aP, 0, C), st, A.add)
+        scan(v("FW", 201, 393), v(aP, 0, C), v("FW", 0, C), -BIG, A.max, A.min)
+        for j in range(3):
+            act(v("junk", 200 * (6 + j), 200 * (6 + j) + C), v("tid"), ACT.Sign, col("cf", 8 + j), -1.0 / PEN, col("acc", 18 + j))
+        for b in range(4):
+            act(v("XH", C * b, C * b + C), v(X, b, 768, 4), ACT.Copy, None, 0.5)
+        tt(v("rec"), v(aP, 0, C), v("FW", 0, C), A.is_gt)
+        tt(v("ev"), v(aP, 0, C), v("FW", 200, 392), A.is_gt)
+        scan(v("KW", 16, 208), v("rec"), v("io5"), 0.0, A.add, A.min)
+        oe, on = v("OE", 0, 3), v("OE", 4, 7)
+        ts(oe, v("acc", 18, 21), 0.5, A.mult, col("cf", 2), A.add)
+        ts(on, v("acc", 18, 21), 0.5, A.mult, 95.0, A.add)
+        act(e48(1), ind(v("aS", 0, 393), oe))
+        tt(e48(0), ind(v("aS", 0, 393), oe), v("D", 0, 48), A.min)
+        tt(e48(3), ind(v("FW", 0, 393), oe), v("D", 0, 48), A.min)
+        scan(v("KW", 208, 400), v("ev"), v("io5"), 0.0, A.add, A.min)
+        act(e48(5, 2, 50), ind(v("iof"), on))
+        scan(v("KW", 400, 592), v("ev"), v("KW", 15, 207), 0.0, A.add, A.min)
+        tt(e48(2), ind(v("FW", 0, 393), oe), e48(1), A.max)
+        act(e48(6), ind(v("KW", 16, 208), on))
+        act(e48(7), ind(v("KW", 208, 400), on))
+        act(e48(9), e48(5), ACT.Identity, 256.0, 256.0)
+        act(e48(10), e48(5), ACT.Identity, 1.0 / 512, 1.0 / 512)
+        tt(e48(8), e48(5, 2, 50), e48(5), A.subtract)
+        tt(e48(11), ind(v("KW", 400, 592), on), e48(7), A.add)
+        for j in range(3):
+            scan(e48(4, 16 * j, 16 * j + 16), e48(0, 16 * j, 16 * j + 16), e48(3, 16 * j, 16 * j + 16), -BIG, A.max, A.max)
+        tt(e48(6, 1, 48, 2), e48(11, 1, 48, 2), e48(6, 1, 48, 2), A.subtract)
+        for j in range(3):
+            ts(v("d144", 48 * j, 48 * j + 48), e48(2), e48(4, 16 * j + 15, 16 * j + 16), A.subtract)
+        tt(e48(12), e48(6), e48(10), A.subtract)
+        for j in range(3):
+            tt(v("c144", 48 * j, 48 * j + 48), v("d144", 48 * j, 48 * j + 48), v("thr", 48 * j, 48 * j + 48), A.is_gt)
+        act(e48(13), e48(12), ACT.Relu, None, 512.0)
+        tt(e48(14), e48(9), e48(8), A.add)
+        scan(v("s144"), v("k144"), v("c144"), 0.0, A.mult, A.add)
+        re = v("RE", 0, 3)
+        cp(re, v("s144", 47, 144, 48))
+        scatter(srt(0), re, e48(8))
+        scatter(srt(1), re, e48(14))
+        scan(srt(3, 1, 49), srt(0), v("c48", 96, 144), 0.0, A.add, A.max)
+        scatter(srt(2), re, e48(13))
+        scan(srt(4, 1, 49), v("c48", 48, 96), srt(0), 512.0, A.add, A.subtract)
+        for j in range(4):
+            act(v("junk", 1800 + 56 * j, 1848 + 56 * j), srt(3), ACT.Sign, col("cf", 16 + j), -1.0, col("acc", 22 + j))
+        cp(v("sI", 0, 48), srt(3))
+        tt(v("XW", 1, 48), srt(1, 1, 48), v("c48", 0, 47), A.add)
+        act(col("XW", 48), srt(1, 0, 1), ACT.Identity, 47.0 * 65536)
+        ts(v("sI", 48, 96), v("sI", 0, 48), 15, A.bitwise_and)
+        tt(v("XW", 57, 105), srt(1), v("c48", 0, 48), A.add)
+        tt(v("XW", 113, 160), srt(2, 1, 48), srt(4, 0, 47), A.add)
+        ts(v("bm"), v("sI", 48, 96), pm, A.is_le, 2.0 ** 25, A.mult)
+        act(col("XW", 160), srt(2, 0, 1), ACT.Identity, srt(4, 47, 48))
+        tt(v("XW", 169, 217), srt(2), srt(4), A.add)
+        ts(v("OL"), v("acc", 22, 26), 0.5, A.mult, 24.0, A.add)
+        for a in range(4):
+            scan(v("MW", 56 * a + 1, 56 * a + 49), v("bm"), v("XW", 56 * a + 1, 56 * a + 49), 0.0, A.add, A.min)
+            act(v("GW", 32 * a, 32 * a + 32), ind(v("XW", 56 * a, 56 * a + 56), v("OL", 2, 4)))
+            tt(v("VV", 32 * a, 32 * a + 32), ind(v("MW", 56 * a, 56 * a + 56), v("OL", 0, 2)), v("GW", 32 * a, 32 * a + 32), A.max)
+
+        ts(wi(0, 0, 32), v("VV", 0, 32), 255, A.bitwise_and)
+        cp(wf(0, 0, 24), wi(0, 0, 24))
+        recip(wf(1, 0, 24), wf(0, 0, 24))
+        act(wf(2, 0, 24), wf(0, 0, 24), ACT.Identity, 0.5, -0.5)
+        ts(wi(2), v("VV", 64, 128), 1023, A.bitwise_and)
+        ts(wi(0, 32, 64), v("VV", 32, 64), 255, A.bitwise_and)
+        tt(wf(3, 0, 56), wi(2, 0, 56), v("cw", 0, 56), A.add)
+        ts(wi(1), v("VV", 0, 64), 8, A.logical_shift_right, 255, A.bitwise_and)
+        tt(wf(5, 0, 24), wf(3, 0, 24), wf(2, 0, 24), A.add)
+        tt(wi(3, 32, 56), wf(3, 32, 56), wi(0, 32, 56), A.is_ge)
+        tt(wf(6, 0, 24), wf(5, 0, 24), wf(1, 0, 24), A.mult)
+        tt(wf(4, 0, 56), wf(3, 0, 56), wi(1, 0, 56), A.add)
+        cp(wi(3, 0, 24), wf(6, 0, 24))
+        for h in (32, 0):
+            tt(wf(7, h, h + 24), wi(3, h, h + 24), wi(0, h, h + 24), A.mult)
+            tt(wf(8, h, h + 24), wf(4, h, h + 24), wf(7, h, h + 24), A.subtract)
+            cp(v("FG", h, h + 24), wf(8, h, h + 24))
+
+        def zhalf(Z, Gt, o):
+            for b in range(4):
+                w = v("XH", C * b, C * b + C)
+                act(v(Gt, C * b, C * b + C), ind(w, v("FG", 32 + o, 44 + o)))
+                tt(v(Z, b, 768, 4), ind(w, v("FG", o, o + 12)), v(Gt, C * b, C * b + C), A.add)
+
+        zhalf("Zb", "Gb", 12)
+        zq, zs = "zq%d" % t, "zs%d" % t
+        quant(v(zq), v(zs), v("Zb"))
+        d, via = routes[(t, rank)]
+        arr = T.sem["arr%d" % t]
+        if via is None:
+            rid, pid = topo.addr(d, core)
+            m, n = topo.mask(core, d), len(topo.engines(core, d))
+            ops.append(("G", lambda zq=zq, t=t, rid=rid, pid=pid, m=m, arr=arr: g.remote_dma(
+                u8(v("lq%d" % t)), u8(v(zq)), arr, T.sem.sent, pid, rid, m), v(zq)[1], [], ("remote",), 500.0))
+            ops.append(("G", lambda zs=zs, t=t, rid=rid, pid=pid, m=m, arr=arr: g.remote_dma(
+                T["ls%d" % t][:], T[zs][:], arr, T.sem.sent, pid, rid, m), v(zs)[1], [], ("remote",), 500.0))
+            sent[0] += 2 * n
+        else:
+            en = topo.engines(core, via[0])
+            h = len(en) // 2
+            trs = []
+            for k in range(2):
+                rid, pid = topo.addr(via[k], core)
+                trs.append(RemoteDMATransfer(dst_ids=[DstId(rid=rid, pnc=pid)], dma_engine_mask=_bits(en[h * k:h * k + h]),
+                                             remote_sem=T.sem.hop, src=u8(v(zq, 96 * k, 96 * k + 96)), dst=u8(v("rq"))))
+            rid, pid = topo.addr(via[2], core)
+            m = topo.mask(core, via[2])
+            ops.append(("G", lambda trs=trs: g.remote_dma_fused(trs, local_sem=T.sem.sent), v(zq)[1], [], ("remote",), 500.0))
+            ops.append(("G", lambda zs=zs, rid=rid, pid=pid, m=m: g.remote_dma(
+                T.rs[:], T[zs][:], T.sem.hop, T.sem.sent, pid, rid, m), v(zs)[1], [], ("remote",), 500.0))
+            sent[0] += 2 * h + len(topo.engines(core, via[2]))
+        back = routes[(t, rank ^ STEP[t])][1]
+        total = 2 * len(topo.engines(d, core)) if back is None else sum(len(topo.engines(k, core)) for k in back)
+        ops.append(("X", None, [], v("lq%d" % t)[1] + v("ls%d" % t)[1], ("arrive", "arr%d" % t, total), OPT["far"][t]))
+
+        zhalf("Za", "Ga", 0)
+        quant(v("zaq"), v("zas"), v("Za"))
+        for b in range(4):
+            mm(v("ps%d" % b, 0, C), v("wq", 128 * b, 128 * b + 128), v("wp", 128 * b, 128 * b + 128), v("zaq"), v("zas"))
+            act(v("HH", 384 * b, 384 * b + C), v("ps%d" % b, 0, C), ACT.Copy, None, 2.0 ** -6)
+
+        act(e48(16), ind(srt(3, 0, 56), re))
+        act(e48(15), e48(5), ACT.Identity, 1.0)
+        tt(e48(17), e48(13), e48(15), A.add)
+        cp(v("bI", 0, 24), e48(15, 0, 48, 2))
+        for j in range(2):
+            act(v("junk", 2100 + 56 * j, 2124 + 56 * j), e48(15, 0, 48, 2), ACT.Sign, col("cf", 22 + j), -1.0, col("acc", 26 + j))
+        tt(e48(18), e48(16), e48(17), A.subtract)
+        ts(v("bI", 24, 48), v("bI", 0, 24), 15, A.bitwise_and)
+        tt(v("ZW", 65, 89), e48(8, 0, 48, 2), v("c48", 168, 192), A.add)
+        act(e48(19), e48(18), ACT.Copy, None, 256.0)
+        ts(v("bm2"), v("bI", 24, 48), pm, A.is_le, 2.0 ** 25, A.mult)
+        ts(v("OP", 0, 4, 2), v("acc", 26, 28), 0.5, A.mult, 12.0, A.add)
+        tt(e48(20), e48(19), e48(17), A.add)
+        for w in range(2):
+            tt(v("ZW", 32 * w + 1, 32 * w + 25), e48(20, w, 48, 2), v("c48", 144, 168), A.add)
+        for a in (2, 0, 1):
+            act(v("G2", 16 * a, 16 * a + 16), ind(v("ZW", 32 * a, 32 * a + 32), v("OP", 2, 3)))
+            scan(v("ZM", 32 * a + 1, 32 * a + 25), v("bm2"), v("ZW", 32 * a + 1, 32 * a + 25), 0.0, A.add, A.min)
+        for k, a in ((2, 2), (3, 2), (0, 0), (1, 1)):
+            tt(v("V2", 16 * k, 16 * k + 16), ind(v("ZM", 32 * a, 32 * a + 32), v("OP", 0, 1)), v("G2", 16 * a, 16 * a + 16), A.max)
+        ts(v("pi", 0, 64), v("V2"), 255, A.bitwise_and)
+        ts(v("pi", 64, 96), v("V2", 0, 32), 8, A.logical_shift_right, 1023, A.bitwise_and)
+        tt(v("pf", 0, 32), v("cw", 64, 96), v("pi", 0, 32), A.is_lt)
+        tt(v("pf", 32, 64), v("pi", 64, 96), v("cw", 64, 96), A.add)
+        tt(v("pf", 64, 96), v("pf", 0, 32), v("pi", 32, 64), A.mult)
+        tt(v("pf", 96, 128), v("pf", 32, 64), v("pf", 64, 96), A.add)
+        ts(v("PQ"), v("pf", 96, 128), -256.0, A.add)
+        if t == 1:
+            act(v("fo"), ind(v("iof"), v("FG", 32, 56)))
+            dma("Y", T.ol[:], T.fo[0:128:16, :], v("fo")[1], [])
+
+        for b in range(4):
+            mm(v("ps%d" % (4 + b), 0, C), v("wq", 128 * b, 128 * b + 128), v("wp", 128 * b, 128 * b + 128),
+               v("lq%d" % t), v("ls%d" % t))
+            hw = v("HH", 384 * b, 384 * b + 384)
+            if b in OPT["vevac"]:
+                ts(v("HH", 384 * b + C, 384 * b + 384), v("ps%d" % (4 + b), 0, C), 2.0 ** -6, A.mult)
+            else:
+                act(v("HH", 384 * b + C, 384 * b + 384), v("ps%d" % (4 + b), 0, C), ACT.Copy, None, 2.0 ** -6)
+            if b in planes:
+                o = 576 * b
+                act(v("SQ", o + 2, o + 576, 3), v(X, b, 768, 4))
+                act(v("SQ", o, o + 576, 3), ind(hw, v("PQ", 0, 12)))
+                act(v("SQ", o + 1, o + 576, 3), ind(hw, v("PQ", 16, 28)))
+                scan(v("SO", o, o + 576), v("k3"), v("SQ", o, o + 576), 0.0, A.mult, A.add)
+                cp(v(Xn, b, 768, 4), v("SO", o + 2, o + 576, 3))
+            else:
+                act(v("HQ", C * b, C * b + C), ind(hw, v("PQ", 16, 28)))
+                tt(v("HS", C * b, C * b + C), ind(hw, v("PQ", 0, 12)), v("HQ", C * b, C * b + C), A.add)
+                tt(v(Xn, b, 768, 4), v("HS", C * b, C * b + C), v(X, b, 768, 4), A.add)
+        quant(v("xq%d" % (t + 1)), v("xs%d" % (t + 1)), v(Xn))
+
+    mm(v("ps0", 0, C), v("vq"), v("vs"), v("xq2"), v("xs2"))
+    dma("Y", T.oc[:], u8(v("xq2")), v("xq2")[1], [])
+    cp(v("yo"), v("ps0", 0, C))
+    for k in range(4):
+        dma("S", T.osc[4 * k:4 * k + 4, :], T.xs2[32 * k:32 * k + 4, :], v("xs2")[1], [])
+    dma("Y", T.y[:], T.yo[:], v("yo")[1], [])
+    last.append(("sent", sent[0]))
+    _emit(g, T, ops, last)

@@ -5,11 +5,12 @@ C = 192
 STEP = [4, 3]
 CORES_ALL = 256
 BIG = 2.0 ** 96
-PEN = 2.0 ** 90
+U = 65536.0
+HALF = 8.5
+ROUND = 1.5 * 2.0 ** 48
 F32, BF, I32, U16, U8, MX = "float32", "bfloat16", "int32", "uint16", "uint8", "float8_e4m3fn_x4"
-OPT = {"scan_planes": (2, 3), "vevac": (0, 1, 2), "sc": (0, 1, 10, 11),
-       "wake": 130.0, "cy": 1.0, "ga": 1.5, "far": (4000.0, 7000.0), "load": 2400.0}
-PLAN = []
+OPT = {"state": ("VVSS", "SVSV", "VVSS", "SVSV"), "sc": (7, 12), "vsub": (0,),
+       "wake": 220.0, "cy": 0.83, "ga": 1.5, "far": (3000.0, 5000.0), "load": 1500.0}
 
 
 def _sb(n, d):
@@ -32,19 +33,21 @@ SCRATCH = {
     "yo": _sb(192, F32), "fo": _sb(384, F32),
     "ci": _sb(32, I32), "cf": _sb(32, F32), "uo": _sb(16, U16),
     "cmod": _sb(192, F32), "D": _sb(192, F32), "R": _sb(192, F32), "keep": _sb(192, BF), "iof": _sb(192, F32),
-    "io5": _sb(192, BF), "lur": _sb(192, BF), "lus": _sb(192, BF), "one": _sb(192, BF), "k3": _sb(576, BF),
-    "thr": _sb(144, F32), "k144": _sb(144, BF), "tmpc": _sb(192, F32), "tmpd": _sb(192, F32), "tmpe": _sb(144, F32),
-    "c48": _sb(256, F32), "cw": _sb(96, F32),
+    "dn": _sb(192, BF), "lur": _sb(192, BF), "neg": _sb(192, BF), "k3": _sb(576, BF),
+    "thr": _sb(144, F32), "k144": _sb(144, BF), "tmpc": _sb(192, F32), "tmpd": _sb(96, F32), "tmpe": _sb(144, F32),
+    "zero": _sb(48, F32), "cw": _sb(96, F32), "cx": _sb(64, F32),
+    "lun": _sb(192, BF), "D3": _sb(96, F32), "R3": _sb(72, F32),
+    "nr": _sb(192, BF), "M1": _sb(192, F32), "x3": _sb(96, F32), "sA": _sb(56, F32), "sB": _sb(96, F32),
     "sm": _sb(192, F32), "hold": _sb(192, F32), "eq": _sb(192, BF), "ne": _sb(192, BF),
-    "TT": _sb(12 * 192, BF), "SUM": _sb(12 * 96, BF), "U": _sb(6 * 200, BF), "junk": _sb(14 * 200, BF), "acc": _sb(48, F32),
-    "RK": _sb(12, U16), "aS": _sb(400, F32), "r": _sb(192, BF), "pen": _sb(192, BF), "tid": _sb(192, BF),
-    "FW": _sb(400, F32), "rec": _sb(192, BF), "ev": _sb(192, BF), "KW": _sb(592, BF), "OE": _sb(8, U16),
-    "e48": _sb(22 * 56, F32), "d144": _sb(144, F32), "c144": _sb(144, BF), "s144": _sb(144, BF), "RE": _sb(4, U16),
-    "srt": _sb(5 * 56, F32), "sI": _sb(96, I32), "bm": _sb(48, F32), "OL": _sb(4, U16),
-    "XW": _sb(224, F32), "MW": _sb(224, F32), "GW": _sb(128, F32), "VV": _sb(128, I32),
-    "wi": _sb(4 * 64, I32), "wf": _sb(9 * 64, F32), "FG": _sb(64, U16),
-    "bI": _sb(48, I32), "bm2": _sb(24, F32), "OP": _sb(4, U16), "ZW": _sb(96, F32), "ZM": _sb(96, F32), "G2": _sb(48, F32),
-    "V2": _sb(64, I32), "pi": _sb(96, I32), "pf": _sb(128, F32), "PQ": _sb(32, U16),
+    "TT": _sb(12 * 192, BF), "SUM": _sb(12 * 96, BF), "SG": _sb(6 * 200, BF), "junk": _sb(14 * 200, BF), "acc": _sb(48, F32),
+    "RK": _sb(12, U16), "aS": _sb(192, F32), "r": _sb(192, BF), "tid": _sb(192, BF),
+    "FW": _sb(400, F32), "rec": _sb(192, BF), "ev": _sb(192, BF), "KW": _sb(592, BF), "OE": _sb(2, U16),
+    "e": _sb(24 * 72, F32), "d144": _sb(144, F32), "c144": _sb(144, BF), "s144": _sb(144, BF), "RE": _sb(4, U16),
+    "srt": _sb(3 * 56, F32), "sI": _sb(96, I32), "bm": _sb(48, F32), "OL": _sb(2, U16),
+    "XW": _sb(112, F32), "MW": _sb(112, F32), "GW": _sb(80, F32), "VV": _sb(64, I32),
+    "wi": _sb(5 * 64, I32), "wf": _sb(10 * 64, F32), "FG": _sb(64, U16),
+    "bI": _sb(48, I32), "bm2": _sb(24, F32), "OP": _sb(2, U16), "ZW": _sb(64, F32), "ZM": _sb(64, F32), "G2": _sb(48, F32),
+    "V2": _sb(32, I32), "pi": _sb(96, I32), "pf": _sb(160, F32), "PQ": _sb(32, U16),
 }
 for _b in range(8):
     SCRATCH["ps%d" % _b] = ("psum", [128, 512], F32)
@@ -101,23 +104,23 @@ def _deps(ops):
     deps = []
     for i, (q, fn, rd, wr, kind, cost) in enumerate(ops):
         d = set()
-        for (n, lo, hi, s) in rd:
-            for (j, a, b, s2, w) in seen.get(n, []):
+        rd = [(n, _bits(range(lo, hi, s))) for (n, lo, hi, s) in rd]
+        wr = [(n, _bits(range(lo, hi, s))) for (n, lo, hi, s) in wr]
+        for (n, m) in rd:
+            for (j, m2, w) in seen.get(n, []):
                 if n.startswith("ps"):
                     if w or ops[j][0] != q:
                         d.add(j)
-                elif w and a < hi and lo < b and not (s == s2 and (a - lo) % s):
+                elif w and m & m2:
                     d.add(j)
-        for (n, lo, hi, s) in wr:
-            for (j, a, b, s2, w) in seen.get(n, []):
-                if n.startswith("ps") or (a < hi and lo < b and not (s == s2 and (a - lo) % s)):
+        for (n, m) in wr:
+            for (j, m2, w) in seen.get(n, []):
+                if n.startswith("ps") or m & m2:
                     d.add(j)
-        for (n, lo, hi, s) in wr:
-            if s == 1:
-                seen[n] = [e for e in seen.get(n, []) if not (lo <= e[1] and e[2] <= hi)]
-            seen.setdefault(n, []).append((i, lo, hi, s, True))
-        for (n, lo, hi, s) in rd:
-            seen.setdefault(n, []).append((i, lo, hi, s, False))
+        for (n, m) in wr:
+            seen[n] = [e for e in seen.get(n, []) if e[1] & ~m] + [(i, m, True)]
+        for (n, m) in rd:
+            seen.setdefault(n, []).append((i, m, False))
         d.discard(i)
         deps.append(d)
     return deps
@@ -158,7 +161,6 @@ def _emit(g, T, ops, last):
     queue = {"V": g.vector, "S": g.scalar, "P": g.tensor, "G": g, "Y": g.sync}
     deps = _deps(ops)
     order = _order(ops, deps)
-    PLAN[:] = [ops, deps, order]
     pos = {i: k for k, i in enumerate(order)}
     clock = {q: {} for q in queue}
     after, waits, signal = {}, {}, set()
@@ -291,6 +293,9 @@ def rank_program(g, core, T, topo):
         c = price(o[2], a, [], 1.01) + (20.0 if acc is not None else 0.0)
         ops.append(("S", lambda: g.scalar.activation(o[0], a[0], f, **kw), regs(a, bias), regs(o, acc), None, c))
 
+    def affine(o, a, scale, bias):
+        act(o, a, ACT.Identity, bias, scale)
+
     def mm(o, lq, ls, rq, rs):
         ops.append(("P", lambda: g.tensor.matmul_mx(o[0], lq[0], ls[0], rq[0], rs[0], True, True), regs(lq, ls, rq, rs), o[1],
                     None, 170.0))
@@ -312,75 +317,77 @@ def rank_program(g, core, T, topo):
     def u32(x):
         return (x[0].bitcast(dt.uint32), x[1], x[2], x[3], False)
 
+    def e(k, a=0, b=48, s=1):
+        return v("e", 72 * k + a, 72 * k + b, s)
+
+    def srt(k, a=0, b=48):
+        return v("srt", 56 * k + a, 56 * k + b)
+
+    def wf(k, a, b):
+        return v("wf", 64 * k + a, 64 * k + b)
+
+    def wi(k, a=0, b=64):
+        return v("wi", 64 * k + a, 64 * k + b)
+
     dma("Y", T.X0[:], T.x[:], [], v("X0")[1])
     dma("S", T.ut[:], T.u[:], [], v("ut")[1])
     dma("Y", u8(v("wq")), T.wc[:], [], v("wq")[1])
     dma("Y", T.wp[:], T.ws[:], [], v("wp")[1])
     dma("Y", T.vt[:], T.v[:], [], v("vt")[1])
 
-    sc, planes = OPT["sc"], OPT["scan_planes"]
+    s0, s1 = OPT["sc"]
     iota(v("ci", 0, 1), [[0, 1]], 0, 1)
     iota(v("cmod"), [[0, 12], [1, 16]], 0)
     iota(v("ci", 8, 24), [[-1, 2], [16, 8]], 1)
     iota(v("iof"), [[1, 192]], 0)
-    iota(v("cf", 4, 7), [[8, 3]], 1)
     iota(v("tmpe"), [[-16, 3], [1, 48]], 0)
-    iota(v("cf", 12, 16), [[-16, 2], [256, 2]], 15)
-    iota(v("cf", 20, 22), [[-16, 2]], 15)
-    iota(v("tmpd", 0, 64), [[0, 2], [16, 32]], -512)
-    iota(v("tmpd", 64, 96), [[0, 2], [16, 16]], 0)
+    iota(v("tmpd", 0, 64), [[0, 2], [16, 32]], -16 - C)
+    iota(v("tmpd", 64, 96), [[0, 2], [16, 16]], -16 - 96)
     pm = col("cf", 0)
     fill(v("TT", 0, 12 * 192, 192), 0.0)
     ts(col("ci", 1), col("ci", 0), 15, A.bitwise_and)
-    fill(col("FW", 0), -BIG)
-    fill(v("FW", 192, 208), -BIG)
+    fill(v("FW", 0, 400, 207), -BIG)
     cp(pm, col("ci", 1))
     cp(v("uo"), v("ci", 8, 24))
     ts(v("tmpc"), v("cmod"), pm, A.is_equal)
-    fill(v("aS", 192, 208), 0.0)
     fill(v("keep"), 1.0)
     fill(v("keep", 0, 192, 16), 0.0)
     fill(v("R"), BIG)
     fill(v("R", 16, 192, 16), -BIG)
-    act(v("D"), v("tmpc"), ACT.Identity, -BIG, 2 * BIG)
-    fill(v("KW", 0, 16), 0.0)
-    fill(v("one"), PEN)
-    for k, i in enumerate(sc):
+    affine(v("D"), v("tmpc"), 2 * BIG, -BIG)
+    fill(col("KW", 15), 256 * U)
+    fill(v("neg"), -BIG)
+    for i in range(s0, s1):
         if 16 * i + 16 < C:
-            fill(col("U", 200 * k + 192), -(16.0 * i + 15))
-    fill(v("lus"), -PEN)
-    fill(v("lus", 0, 23), 0.0)
+            fill(col("SG", 200 * (i - s0) + C), -(16.0 * i + 15))
+        else:
+            fill(col("acc", 6 + i - s0), C - 1.0)
     fill(v("lur"), BIG)
     fill(v("lur", 0, 23), -BIG)
-    act(v("io5"), v("iof"), ACT.Copy, None, 1.0 / 512)
-    ts(col("ci", 2), col("ci", 1), 1, A.logical_shift_right)
-    ts(col("ci", 3), col("ci", 1), 1, A.bitwise_and)
-    ts(col("cf", 1), col("ci", 2), 0.5, A.add)
-    ts(col("cf", 2), col("ci", 3), 201.0, A.mult, 95.0, A.add)
-    act(col("cf", 3), pm, ACT.Identity, 0.5, 16.0)
-    ts(v("thr"), v("tmpe"), pm, A.is_lt, -1e-30, A.mult)
-    act(v("cf", 8, 11), v("cf", 4, 7), ACT.Identity, col("cf", 1))
-    act(v("cf", 16, 20), v("cf", 12, 16), ACT.Identity, col("cf", 3))
-    act(v("cf", 22, 24), v("cf", 20, 22), ACT.Identity, col("cf", 3))
+    act(v("lun"), v("lur"), ACT.Copy, None, -1.0)
+    for w in range(3):
+        act(v("D3", w, 96, 3), v("D", min(w, 1), 64, 2))
+    fill(v("R3"), BIG)
+    fill(v("R3", 24, 72, 24), -BIG)
+    affine(col("cf", 1), pm, -U, (7.5 - C) * U)
+    cp(col("sA", 0), col("cf", 1))
+    affine(v("dn"), v("iof"), -U, 256 * U)
+    ts(v("thr"), v("tmpe"), pm, A.is_lt, 1e-30, A.mult)
+    for j in range(2):
+        affine(col("cf", 8 + j), pm, 1.0, 16 * j + 1.5)
+        affine(col("cf", 16 + j), pm, 16 * U, (256 * j - C - 0.5 + HALF) * U)
+    affine(col("cf", 22), pm, 16 * U, -97.5 * U)
     fill(v("k144"), 1.0)
     fill(v("k144", 0, 144, 48), 0.0)
-    if planes:
-        fill(v("k3"), 1.0)
-        fill(v("k3", 0, 576, 3), 0.0)
-    act(v("cw"), v("tmpd", 0, 96), ACT.Identity, pm)
-    act(v("c48", 0, 48), v("iof", 0, 48), ACT.Copy, None, 65536.0)
-    fill(v("c48", 48, 96), 1024.0)
-    fill(v("c48", 96, 144), 0.0)
-    act(v("c48", 144, 168), v("iof", 0, 24), ACT.Identity, 65536.0, 2.0 ** 18)
-    act(v("c48", 168, 192), v("iof", 0, 24), ACT.Copy, None, 256.0)
-    fill(v("e48", 5 * 56, 5 * 56 + 2), -1.0)
-    fill(v("srt", 3 * 56, 4 * 56), 0.0)
-    fill(col("srt", 4 * 56), 512.0)
-    fill(v("XW"), 0.0)
-    fill(v("MW"), 0.0)
-    fill(v("ZW"), 0.0)
-    fill(v("ZM"), 0.0)
-    fill(v("wi", 3 * 64, 4 * 64), 0)
+    fill(v("k3"), 1.0)
+    fill(v("k3", 0, 576, 3), 0.0)
+    affine(v("cw"), v("tmpd"), 1.0, pm)
+    act(v("cx", 0, 32), v("cw", 0, 32))
+    fill(v("zero"), 0.0)
+    fill(e(5, 0, 2), -97 * U)
+    fill(srt(2, 0, 56), (HALF - C) * U)
+    for name in ("XW", "MW", "GW", "ZW", "ZM", "G2"):
+        fill(v(name), -256 * U)
 
     quant(v("uq"), v("us"), v("ut"))
     quant(v("xq0"), v("xs0"), v("X0"))
@@ -389,18 +396,6 @@ def rank_program(g, core, T, topo):
     act(v("uss"), ind(v("us"), v("uo", 0, 8)))
     cp(u32(v("ukq")), ind(u32(v("uq")), v("uo", 8, 16)))
     act(v("uks"), ind(v("us"), v("uo", 8, 16)))
-
-    def e48(k, a=0, b=48, s=1):
-        return v("e48", 56 * k + a, 56 * k + b, s)
-
-    def srt(k, a=0, b=48):
-        return v("srt", 56 * k + a, 56 * k + b)
-
-    def wf(k, a=0, b=64):
-        return v("wf", 64 * k + a, 64 * k + b)
-
-    def wi(k, a=0, b=64):
-        return v("wi", 64 * k + a, 64 * k + b)
 
     last = []
     sent = [0]
@@ -411,110 +406,116 @@ def rank_program(g, core, T, topo):
         mm(v(sV, 0, C), v("usq"), v("uss"), xq, xs)
         mm(v(sS, 0, C), v("usq"), v("uss"), xq, xs)
         mm(v(aP, 0, C), v("ukq"), v("uks"), xq, xs)
-        tt(v("sm"), v(sV, 0, C), v("D"), A.min)
-        act(v("aS", 0, C), v(aP, 0, C))
-        scan(v("hold"), v("R"), v("sm"), col("D", 0), A.min, A.max)
-        tt(v("eq"), v(sV, 0, C), v("hold"), A.is_equal)
-        scan(v("ne"), v("keep"), v("eq"), 0.0, A.mult, A.subtract)
+        for (a, b) in ((16 * s0, C), (0, 16 * s0)):
+            tt(v("sm", a, b), v(sV, a, b), v("D", a, b), A.min)
+            scan(v("hold", a, b), v("R", a, b), v("sm", a, b), -BIG if a else col("D", 0), A.min, A.max)
+            tt(v("eq", a, b), v(sV, a, b), v("hold", a, b), A.is_equal)
+            scan(v("ne", a, b), v("keep", a, b), v("eq", a, b), 0.0, A.mult, A.subtract)
+        ts(v("SG", 0, 200 * (s1 - s0), 200), v("ne", 16 * s0 + 15, 16 * s1, 16), -1.0, A.mult)
         for i in range(12):
-            if i in sc:
+            m = 16 * i + 16
+            if s0 <= i < s1:
+                k = i - s0
+                o = 200 * k
+                act(v("SG", o + 1, o + C), v(sS, 1, C), ACT.Sign, col("hold", m - 1), -1.0)
+                act(v("junk", o, o + m), v("SG", o, o + m), ACT.Relu, None, None, col("acc", k))
+                if m < C:
+                    act(v("junk", o + m, o + C + 1), v("SG", o + m, o + C + 1), ACT.Relu, None, -1.0, col("acc", 6 + k))
                 continue
-            o, m = 192 * i, 16 * i + 16
+            o = 192 * i
             ts(v("TT", o + 1, o + m), v(sV, 1, m), col("hold", m - 1), A.is_ge)
             if m < C:
                 ts(v("TT", o + m, o + C), v(sV, m, C), col("hold", m - 1), A.is_gt)
             scan(v("SUM", 96 * i, 96 * i + 96), v("TT", o, o + 96), v("TT", o + 96, o + C), col("ne", m - 1), A.add, A.add)
-        for k, i in enumerate(sc):
-            o, m = 200 * k, 16 * i + 16
-            act(v("U", o + 1, o + C), v(sS, 1, C), ACT.Sign, col("hold", m - 1), -1.0)
-            act(v("junk", o + 1, o + m), v("U", o + 1, o + m), ACT.Relu, None, None, col("acc", k))
-            if m < C:
-                act(v("junk", o + m, o + C + 1), v("U", o + m, o + C + 1), ACT.Relu, None, -1.0, col("acc", 6 + k))
-            act(col("acc", 12 + k), col("acc", k), ACT.Identity, col("ne", m - 1), -1.0)
-            act(col("SUM", 96 * i + 95), col("acc", 12 + k), ACT.Identity, col("acc", 6 + k) if m < C else 191.0)
+        tt(v("SUM", 96 * s0 + 95, 96 * s1, 96), v("acc", 6, 6 + s1 - s0), v("acc", 0, s1 - s0), A.subtract)
         cp(v("RK"), v("SUM", 95, 12 * 96, 96))
-        st = v("pen")
-        cp(v("r"), ind(v("lur"), v("RK")))
-        act(st, ind(v("lus"), v("RK")))
+        cp(v("r", 0, 96), ind(v("lur"), v("RK", 0, 6)))
+        act(v("r", 96, C), ind(v("lur"), v("RK", 6, 12)))
         scan(v("FW", 1, C), v(aP, 0, C - 1), v("r", 1, C), -BIG, A.max, A.min)
-        scan(v("tid"), st, v("one"), 0.0, A.add, A.add)
-        tt(v("aS", 201, 393), v(aP, 0, C), st, A.add)
-        scan(v("FW", 201, 393), v(aP, 0, C), v("FW", 0, C), -BIG, A.max, A.min)
-        for j in range(3):
-            act(v("junk", 200 * (6 + j), 200 * (6 + j) + C), v("tid"), ACT.Sign, col("cf", 8 + j), -1.0 / PEN, col("acc", 18 + j))
+        scan(v("tid"), v("r"), v("neg"), 0.0, A.add, A.add)
+        scan(v("FW", 208, 400), v(aP, 0, C), v("FW", 0, C), -BIG, A.max, A.min)
+        act(v("nr"), ind(v("lun"), v("RK")))
+        scan(v("M1"), v("r"), v(aP, 0, C), -BIG, A.min, A.max)
+        tt(v("aS"), v(aP, 0, C), v("nr"), A.min)
+        for j in range(2):
+            act(v("junk", 200 * (6 + j), 200 * (6 + j) + C), v("tid"), ACT.Sign, col("cf", 8 + j), 0.5 / BIG, col("acc", 18 + j))
         for b in range(4):
             act(v("XH", C * b, C * b + C), v(X, b, 768, 4), ACT.Copy, None, 0.5)
-        tt(v("rec"), v(aP, 0, C), v("FW", 0, C), A.is_gt)
-        tt(v("ev"), v(aP, 0, C), v("FW", 200, 392), A.is_gt)
-        scan(v("KW", 16, 208), v("rec"), v("io5"), 0.0, A.add, A.min)
-        oe, on = v("OE", 0, 3), v("OE", 4, 7)
-        ts(oe, v("acc", 18, 21), 0.5, A.mult, col("cf", 2), A.add)
-        ts(on, v("acc", 18, 21), 0.5, A.mult, 95.0, A.add)
-        act(e48(1), ind(v("aS", 0, 393), oe))
-        tt(e48(0), ind(v("aS", 0, 393), oe), v("D", 0, 48), A.min)
-        tt(e48(3), ind(v("FW", 0, 393), oe), v("D", 0, 48), A.min)
-        scan(v("KW", 208, 400), v("ev"), v("io5"), 0.0, A.add, A.min)
-        act(e48(5, 2, 50), ind(v("iof"), on))
-        scan(v("KW", 400, 592), v("ev"), v("KW", 15, 207), 0.0, A.add, A.min)
-        tt(e48(2), ind(v("FW", 0, 393), oe), e48(1), A.max)
-        act(e48(6), ind(v("KW", 16, 208), on))
-        act(e48(7), ind(v("KW", 208, 400), on))
-        act(e48(9), e48(5), ACT.Identity, 256.0, 256.0)
-        act(e48(10), e48(5), ACT.Identity, 1.0 / 512, 1.0 / 512)
-        tt(e48(8), e48(5, 2, 50), e48(5), A.subtract)
-        tt(e48(11), ind(v("KW", 400, 592), on), e48(7), A.add)
+        tt(v("rec"), v(aP, 0, C), v("FW", 0, C), A.is_le)
+        tt(v("ev"), v(aP, 0, C), v("FW", 207, 399), A.is_le)
+        scan(v("KW", 16, 208), v("rec"), v("dn"), 0.0, A.mult, A.max)
+        on = v("OE")
+        ts(on, v("acc", 18, 20), 0.5, A.mult, 95.0, A.add)
+        scan(v("KW", 208, 400), v("ev"), v("dn"), 0.0, A.mult, A.max)
+        scan(v("KW", 400, 592), v("ev"), v("KW", 15, 207), 0.0, A.mult, A.max)
+        rows = (v("M1"), v("FW", 208, 400), v("aS"))
+        act(e(1, 0, 32), ind(rows[2], on))
+        act(e(2, 0, 64, 2), ind(rows[0], on))
+        for w in range(3):
+            tt(v("x3", w, 96, 3), ind(rows[w], on), v("D3", w, 96, 3), A.min)
+        tt(e(2, 1, 64, 2), ind(rows[1], on), e(1, 0, 32), A.max)
+        scan(e(21, 0, 72), v("R3"), v("x3", 0, 72), -BIG, A.min, A.max)
         for j in range(3):
-            scan(e48(4, 16 * j, 16 * j + 16), e48(0, 16 * j, 16 * j + 16), e48(3, 16 * j, 16 * j + 16), -BIG, A.max, A.max)
-        tt(e48(6, 1, 48, 2), e48(11, 1, 48, 2), e48(6, 1, 48, 2), A.subtract)
-        for j in range(3):
-            ts(v("d144", 48 * j, 48 * j + 48), e48(2), e48(4, 16 * j + 15, 16 * j + 16), A.subtract)
-        tt(e48(12), e48(6), e48(10), A.subtract)
-        for j in range(3):
-            tt(v("c144", 48 * j, 48 * j + 48), v("d144", 48 * j, 48 * j + 48), v("thr", 48 * j, 48 * j + 48), A.is_gt)
-        act(e48(13), e48(12), ACT.Relu, None, 512.0)
-        tt(e48(14), e48(9), e48(8), A.add)
+            dj, own = v("d144", 48 * j, 48 * j + 48), e(21, 24 * j + 23, 24 * j + 24)
+            if j in OPT["vsub"]:
+                ts(dj, e(2), own, A.subtract, -1.0, A.mult)
+            else:
+                affine(dj, e(2), -1.0, own)
+            tt(v("c144", 48 * j, 48 * j + 48), dj, v("thr", 48 * j, 48 * j + 48), A.is_lt)
         scan(v("s144"), v("k144"), v("c144"), 0.0, A.mult, A.add)
         re = v("RE", 0, 3)
         cp(re, v("s144", 47, 144, 48))
-        scatter(srt(0), re, e48(8))
-        scatter(srt(1), re, e48(14))
-        scan(srt(3, 1, 49), srt(0), v("c48", 96, 144), 0.0, A.add, A.max)
-        scatter(srt(2), re, e48(13))
-        scan(srt(4, 1, 49), v("c48", 48, 96), srt(0), 512.0, A.add, A.subtract)
-        for j in range(4):
-            act(v("junk", 1800 + 56 * j, 1848 + 56 * j), srt(3), ACT.Sign, col("cf", 16 + j), -1.0, col("acc", 22 + j))
-        cp(v("sI", 0, 48), srt(3))
-        tt(v("XW", 1, 48), srt(1, 1, 48), v("c48", 0, 47), A.add)
-        act(col("XW", 48), srt(1, 0, 1), ACT.Identity, 47.0 * 65536)
-        ts(v("sI", 48, 96), v("sI", 0, 48), 15, A.bitwise_and)
-        tt(v("XW", 57, 105), srt(1), v("c48", 0, 48), A.add)
-        tt(v("XW", 113, 160), srt(2, 1, 48), srt(4, 0, 47), A.add)
-        ts(v("bm"), v("sI", 48, 96), pm, A.is_le, 2.0 ** 25, A.mult)
-        act(col("XW", 160), srt(2, 0, 1), ACT.Identity, srt(4, 47, 48))
-        tt(v("XW", 169, 217), srt(2), srt(4), A.add)
-        ts(v("OL"), v("acc", 22, 26), 0.5, A.mult, 24.0, A.add)
-        for a in range(4):
-            scan(v("MW", 56 * a + 1, 56 * a + 49), v("bm"), v("XW", 56 * a + 1, 56 * a + 49), 0.0, A.add, A.min)
-            act(v("GW", 32 * a, 32 * a + 32), ind(v("XW", 56 * a, 56 * a + 56), v("OL", 2, 4)))
-            tt(v("VV", 32 * a, 32 * a + 32), ind(v("MW", 56 * a, 56 * a + 56), v("OL", 0, 2)), v("GW", 32 * a, 32 * a + 32), A.max)
+        for w in range(2):
+            affine(e(5, 2 + w, 66, 2), ind(v("iof"), on), U, -96 * U)
+        act(e(6, 0, 64, 2), ind(v("KW", 16, 208), on))
+        tt(e(8), e(5), e(5, 2, 50), A.subtract)
+        tt(e(7, 0, 32), ind(v("KW", 400, 592), on), e(6, 0, 64, 2), A.subtract)
+        tt(e(6, 1, 64, 2), ind(v("KW", 208, 400), on), e(7, 0, 32), A.add)
+        affine(e(9), e(5), 1.0, -159 * U)
+        act(e(10), e(5, 2, 50), ACT.Copy, None, 1.0 / U)
+        affine(e(11), e(5), 255.0 / U, 97.0 * 256 - HALF * U)
+        tt(e(12), e(6), e(9), A.add)
+        tt(e(15), e(10), e(11), A.add)
+        act(e(13), e(12), ACT.Relu, None, -1.0)
+        tt(e(14), e(15), e(13), A.subtract)
+        scatter(srt(0), re, e(8))
+        scan(srt(2, 1, 49), v("zero"), srt(0), (HALF - C) * U, A.add, A.subtract)
+        scan(v("sA", 1, 48), v("zero", 0, 47), srt(0, 0, 47), col("cf", 1), A.add, A.subtract)
+        scatter(srt(1), re, e(14))
+        affine(v("sB", 0, 48), srt(2), 32.0, ROUND)
+        affine(v("sB", 48, 96), v("sA", 0, 48), 32.0, ROUND)
+        tt(v("bm"), v("sB", 0, 48), v("sB", 48, 96), A.subtract)
+        for j in range(2):
+            act(v("junk", 1800 + 56 * j, 1848 + 56 * j), srt(2), ACT.Sign, col("cf", 16 + j), -1.0, col("acc", 22 + j))
+        tt(v("XW", 1, 49), srt(2, 1, 49), srt(1), A.add)
+        affine(v("XW", 57, 104), v("XW", 2, 49), 1.0, srt(0, 0, 1))
+        affine(col("XW", 104), srt(1, 0, 1), 1.0, (C + HALF) * U)
+        affine(col("acc", 30), srt(0, 0, 1), 1.0 / U, 0.5)
+        affine(v("cx", 32, 64), v("cw", 32, 64), 1.0, col("acc", 30))
+        ts(v("OL"), v("acc", 22, 24), 0.5, A.mult, 24.0, A.add)
+        for a in range(2):
+            scan(v("MW", 56 * a + 1, 56 * a + 49), v("bm"), v("XW", 56 * a + 1, 56 * a + 49), -256 * U, A.add, A.min)
+            act(v("GW", 40 * a + 1, 40 * a + 33), ind(v("XW", 56 * a, 56 * a + 56), v("OL")))
+            tt(v("VV", 32 * a, 32 * a + 32), ind(v("MW", 56 * a, 56 * a + 56), v("OL")), v("GW", 40 * a, 40 * a + 32), A.max)
 
-        ts(wi(0, 0, 32), v("VV", 0, 32), 255, A.bitwise_and)
-        cp(wf(0, 0, 24), wi(0, 0, 24))
-        recip(wf(1, 0, 24), wf(0, 0, 24))
-        act(wf(2, 0, 24), wf(0, 0, 24), ACT.Identity, 0.5, -0.5)
-        ts(wi(2), v("VV", 64, 128), 1023, A.bitwise_and)
-        ts(wi(0, 32, 64), v("VV", 32, 64), 255, A.bitwise_and)
-        tt(wf(3, 0, 56), wi(2, 0, 56), v("cw", 0, 56), A.add)
-        ts(wi(1), v("VV", 0, 64), 8, A.logical_shift_right, 255, A.bitwise_and)
-        tt(wf(5, 0, 24), wf(3, 0, 24), wf(2, 0, 24), A.add)
-        tt(wi(3, 32, 56), wf(3, 32, 56), wi(0, 32, 56), A.is_ge)
-        tt(wf(6, 0, 24), wf(5, 0, 24), wf(1, 0, 24), A.mult)
-        tt(wf(4, 0, 56), wf(3, 0, 56), wi(1, 0, 56), A.add)
-        cp(wi(3, 0, 24), wf(6, 0, 24))
-        for h in (32, 0):
-            tt(wf(7, h, h + 24), wi(3, h, h + 24), wi(0, h, h + 24), A.mult)
-            tt(wf(8, h, h + 24), wf(4, h, h + 24), wf(7, h, h + 24), A.subtract)
-            cp(v("FG", h, h + 24), wf(8, h, h + 24))
+        ts(wi(0), v("VV"), 255, A.bitwise_and)
+        ts(wi(1), v("VV"), 16, A.arith_shift_right)
+        cp(wf(0, 33, 57), wi(0, 33, 57))
+        recip(wf(1, 33, 57), wf(0, 33, 57))
+        ts(wi(2), v("VV"), 8, A.logical_shift_right, 255, A.bitwise_and)
+        tt(wf(2, 1, 57), v("cx", 1, 57), wi(1, 1, 57), A.subtract)
+        act(wf(3, 1, 25), wf(2, 1, 25), ACT.Relu, None, -512.0)
+        tt(wf(4, 1, 25), wf(2, 1, 25), wi(2, 1, 25), A.add)
+        tt(wf(5, 1, 25), wf(3, 1, 25), wi(0, 1, 25), A.min)
+        tt(wf(6, 1, 25), wf(4, 1, 25), wf(5, 1, 25), A.add)
+        cp(v("FG", 32, 56), wf(6, 1, 25))
+        tt(wf(3, 33, 57), wf(2, 33, 57), wi(0, 1, 25), A.add)
+        tt(wf(5, 33, 57), wf(3, 33, 57), wf(1, 33, 57), A.mult)
+        tt(wf(4, 33, 57), wf(3, 33, 57), wi(2, 33, 57), A.add)
+        ts(wi(3, 33, 57), wf(5, 33, 57), -0.5, A.add)
+        tt(wf(6, 33, 57), wi(3, 33, 57), wi(0, 33, 57), A.mult)
+        tt(wf(7, 33, 57), wf(4, 33, 57), wf(6, 33, 57), A.subtract)
+        ts(v("FG", 0, 24), wf(7, 33, 57), -0.5, A.add)
 
         def zhalf(Z, Gt, o):
             for b in range(4):
@@ -559,33 +560,31 @@ def rank_program(g, core, T, topo):
             mm(v("ps%d" % b, 0, C), v("wq", 128 * b, 128 * b + 128), v("wp", 128 * b, 128 * b + 128), v("zaq"), v("zas"))
             act(v("HH", 384 * b, 384 * b + C), v("ps%d" % b, 0, C), ACT.Copy, None, 2.0 ** -6)
 
-        act(e48(16), ind(srt(3, 0, 56), re))
-        act(e48(15), e48(5), ACT.Identity, 1.0)
-        tt(e48(17), e48(13), e48(15), A.add)
-        cp(v("bI", 0, 24), e48(15, 0, 48, 2))
-        for j in range(2):
-            act(v("junk", 2100 + 56 * j, 2124 + 56 * j), e48(15, 0, 48, 2), ACT.Sign, col("cf", 22 + j), -1.0, col("acc", 26 + j))
-        tt(e48(18), e48(16), e48(17), A.subtract)
+        affine(e(16), ind(srt(2, 0, 56), re), 256.0 / U, (C - HALF) * 256.0)
+        affine(e(17), e(5), 2.0 - 1.0 / U, 2 * U)
+        act(e(18), e(12), ACT.Relu, None, -2.0)
+        tt(e(19), e(10), e(17), A.add)
+        tt(e(20), e(19), e(18), A.add)
+        ts(v("bI", 0, 24), e(5, 0, 48, 2), 1.0 / U, A.mult, 97.0, A.add)
         ts(v("bI", 24, 48), v("bI", 0, 24), 15, A.bitwise_and)
-        tt(v("ZW", 65, 89), e48(8, 0, 48, 2), v("c48", 168, 192), A.add)
-        act(e48(19), e48(18), ACT.Copy, None, 256.0)
-        ts(v("bm2"), v("bI", 24, 48), pm, A.is_le, 2.0 ** 25, A.mult)
-        ts(v("OP", 0, 4, 2), v("acc", 26, 28), 0.5, A.mult, 12.0, A.add)
-        tt(e48(20), e48(19), e48(17), A.add)
+        ts(v("bm2"), v("bI", 24, 48), pm, A.is_le, 512 * U, A.mult)
+        act(v("junk", 2100, 2124), e(5, 0, 48, 2), ACT.Sign, col("cf", 22), -1.0, col("acc", 26))
+        op = v("OP", 0, 1)
+        ts(op, col("acc", 26), 0.5, A.mult, 12.0, A.add)
         for w in range(2):
-            tt(v("ZW", 32 * w + 1, 32 * w + 25), e48(20, w, 48, 2), v("c48", 144, 168), A.add)
-        for a in (2, 0, 1):
-            act(v("G2", 16 * a, 16 * a + 16), ind(v("ZW", 32 * a, 32 * a + 32), v("OP", 2, 3)))
-            scan(v("ZM", 32 * a + 1, 32 * a + 25), v("bm2"), v("ZW", 32 * a + 1, 32 * a + 25), 0.0, A.add, A.min)
-        for k, a in ((2, 2), (3, 2), (0, 0), (1, 1)):
-            tt(v("V2", 16 * k, 16 * k + 16), ind(v("ZM", 32 * a, 32 * a + 32), v("OP", 0, 1)), v("G2", 16 * a, 16 * a + 16), A.max)
-        ts(v("pi", 0, 64), v("V2"), 255, A.bitwise_and)
-        ts(v("pi", 64, 96), v("V2", 0, 32), 8, A.logical_shift_right, 1023, A.bitwise_and)
-        tt(v("pf", 0, 32), v("cw", 64, 96), v("pi", 0, 32), A.is_lt)
-        tt(v("pf", 32, 64), v("pi", 64, 96), v("cw", 64, 96), A.add)
-        tt(v("pf", 64, 96), v("pf", 0, 32), v("pi", 32, 64), A.mult)
-        tt(v("pf", 96, 128), v("pf", 32, 64), v("pf", 64, 96), A.add)
-        ts(v("PQ"), v("pf", 96, 128), -256.0, A.add)
+            tt(v("ZW", 32 * w + 1, 32 * w + 25), e(20, w, 48, 2), e(16, w, 48, 2), A.add)
+            act(v("G2", 24 * w + 1, 24 * w + 17), ind(v("ZW", 32 * w, 32 * w + 32), op))
+            scan(v("ZM", 32 * w + 1, 32 * w + 25), v("bm2"), v("ZW", 32 * w + 1, 32 * w + 25), -256 * U, A.add, A.min)
+            tt(v("V2", 16 * w, 16 * w + 16), ind(v("ZM", 32 * w, 32 * w + 32), op), v("G2", 24 * w, 24 * w + 16), A.max)
+        ts(v("pi", 0, 32), v("V2"), 17, A.arith_shift_right)
+        ts(v("pi", 32, 64), v("V2"), 255, A.bitwise_and)
+        ts(v("pi", 64, 96), v("V2"), 8, A.logical_shift_right, 511, A.bitwise_and)
+        tt(v("pf", 0, 32), v("cw", 64, 96), v("pi", 0, 32), A.subtract)
+        act(v("pf", 32, 64), v("pf", 0, 32), ACT.Relu, None, -512.0)
+        tt(v("pf", 64, 96), v("pf", 0, 32), v("pi", 64, 96), A.add)
+        tt(v("pf", 96, 128), v("pf", 32, 64), v("pi", 32, 64), A.min)
+        tt(v("pf", 128, 160), v("pf", 64, 96), v("pf", 96, 128), A.add)
+        cp(v("PQ", 0, 28), v("pf", 129, 157))
         if t == 1:
             act(v("fo"), ind(v("iof"), v("FG", 32, 56)))
             dma("Y", T.ol[:], T.fo[0:128:16, :], v("fo")[1], [])
@@ -594,19 +593,21 @@ def rank_program(g, core, T, topo):
             mm(v("ps%d" % (4 + b), 0, C), v("wq", 128 * b, 128 * b + 128), v("wp", 128 * b, 128 * b + 128),
                v("lq%d" % t), v("ls%d" % t))
             hw = v("HH", 384 * b, 384 * b + 384)
-            if b in OPT["vevac"]:
+            how = OPT["state"][b]
+            move = {"V": cp, "S": act}
+            if how[0] == "V":
                 ts(v("HH", 384 * b + C, 384 * b + 384), v("ps%d" % (4 + b), 0, C), 2.0 ** -6, A.mult)
             else:
                 act(v("HH", 384 * b + C, 384 * b + 384), v("ps%d" % (4 + b), 0, C), ACT.Copy, None, 2.0 ** -6)
-            if b in planes:
+            if len(how) > 2:
                 o = 576 * b
                 act(v("SQ", o + 2, o + 576, 3), v(X, b, 768, 4))
-                act(v("SQ", o, o + 576, 3), ind(hw, v("PQ", 0, 12)))
-                act(v("SQ", o + 1, o + 576, 3), ind(hw, v("PQ", 16, 28)))
+                move[how[1]](v("SQ", o, o + 576, 3), ind(hw, v("PQ", 0, 12)))
+                move[how[2]](v("SQ", o + 1, o + 576, 3), ind(hw, v("PQ", 16, 28)))
                 scan(v("SO", o, o + 576), v("k3"), v("SQ", o, o + 576), 0.0, A.mult, A.add)
-                cp(v(Xn, b, 768, 4), v("SO", o + 2, o + 576, 3))
+                move[how[3]](v(Xn, b, 768, 4), v("SO", o + 2, o + 576, 3))
             else:
-                act(v("HQ", C * b, C * b + C), ind(hw, v("PQ", 16, 28)))
+                move[how[1]](v("HQ", C * b, C * b + C), ind(hw, v("PQ", 16, 28)))
                 tt(v("HS", C * b, C * b + C), ind(hw, v("PQ", 0, 12)), v("HQ", C * b, C * b + C), A.add)
                 tt(v(Xn, b, 768, 4), v("HS", C * b, C * b + C), v(X, b, 768, 4), A.add)
         quant(v("xq%d" % (t + 1)), v("xs%d" % (t + 1)), v(Xn))

@@ -8,9 +8,11 @@ BIG = 2.0 ** 96
 U = 65536.0
 HALF = 8.5
 ROUND = 1.5 * 2.0 ** 48
+WHOLE = 1.5 * 2.0 ** 23
 F32, BF, I32, U16, U8, MX = "float32", "bfloat16", "int32", "uint16", "uint8", "float8_e4m3fn_x4"
-OPT = {"state": ("VVSS", "SVSV", "VVSS", "SVSV"), "sc": (7, 12), "vsub": (0,),
-       "wake": 220.0, "cy": 0.83, "ga": 1.5, "far": (3000.0, 5000.0), "load": 1500.0}
+OPT = {"cuts": ((112, 192), (0, 112)), "irec": True, "state": ("VVSS", "SHSV2", "VVSS", "SVSV"), "sc": (7, 12), "vsub": (0,), "passes": 12000, "paces": ((1.0, 235.0), (1.3, 260.0)), "slack": 60.0, "near": 8, "hand": 2, "zf": "SSSS", "own": "VSVS",
+       "wake": 235.0, "cy": 0.83, "ga": 1.5, "far": (2000.0, 4000.0), "load": 1500.0}
+ORDERS = {}
 
 
 def _sb(n, d):
@@ -29,21 +31,23 @@ SCRATCH = {
     "zq0": _sb(192, MX), "zs0": _sb(192, U8), "zq1": _sb(192, MX), "zs1": _sb(192, U8),
     "lq0": _sb(192, MX), "ls0": _sb(192, U8), "lq1": _sb(192, MX), "ls1": _sb(192, U8),
     "rq": _sb(96, MX), "rs": _sb(192, U8),
-    "HH": _sb(1536, BF), "HQ": _sb(768, BF), "HS": _sb(768, F32), "SQ": _sb(4 * 576, BF), "SO": _sb(4 * 576, BF),
+    "HH": _sb(1536, BF), "SQ": _sb(4 * 576, BF), "SO": _sb(4 * 576, BF),
     "yo": _sb(192, F32), "fo": _sb(384, F32),
     "ci": _sb(32, I32), "cf": _sb(32, F32), "uo": _sb(16, U16),
     "cmod": _sb(192, F32), "D": _sb(192, F32), "R": _sb(192, F32), "keep": _sb(192, BF), "iof": _sb(192, F32),
     "dn": _sb(192, BF), "lur": _sb(192, BF), "neg": _sb(192, BF), "k3": _sb(576, BF),
-    "thr": _sb(144, F32), "k144": _sb(144, BF), "tmpc": _sb(192, F32), "tmpd": _sb(96, F32), "tmpe": _sb(144, F32),
+    "thr": _sb(144, F32), "k144": _sb(144, BF), "tmpd": _sb(96, F32), "tmpe": _sb(144, F32),
     "zero": _sb(48, F32), "cw": _sb(96, F32), "cx": _sb(64, F32),
     "lun": _sb(192, BF), "D3": _sb(96, F32), "R3": _sb(72, F32),
     "nr": _sb(192, BF), "M1": _sb(192, F32), "x3": _sb(96, F32), "sA": _sb(56, F32), "sB": _sb(96, F32),
+    "cu": _sb(24, F32), "f0": _sb(72, F32), "f1": _sb(72, F32), "f2": _sb(72, F32),
+    "g0": _sb(144, F32), "g1": _sb(144, F32), "g2": _sb(144, F32),
     "sm": _sb(192, F32), "hold": _sb(192, F32), "eq": _sb(192, BF), "ne": _sb(192, BF),
     "TT": _sb(12 * 192, BF), "SUM": _sb(12 * 96, BF), "SG": _sb(6 * 200, BF), "junk": _sb(14 * 200, BF), "acc": _sb(48, F32),
     "RK": _sb(12, U16), "aS": _sb(192, F32), "r": _sb(192, BF), "tid": _sb(192, BF),
     "FW": _sb(400, F32), "rec": _sb(192, BF), "ev": _sb(192, BF), "KW": _sb(592, BF), "OE": _sb(2, U16),
     "e": _sb(24 * 72, F32), "d144": _sb(144, F32), "c144": _sb(144, BF), "s144": _sb(144, BF), "RE": _sb(4, U16),
-    "srt": _sb(3 * 56, F32), "sI": _sb(96, I32), "bm": _sb(48, F32), "OL": _sb(2, U16),
+    "srt": _sb(3 * 56, F32), "bm": _sb(48, F32), "OL": _sb(2, U16),
     "XW": _sb(112, F32), "MW": _sb(112, F32), "GW": _sb(80, F32), "VV": _sb(64, I32),
     "wi": _sb(5 * 64, I32), "wf": _sb(10 * 64, F32), "FG": _sb(64, U16),
     "bI": _sb(48, I32), "bm2": _sb(24, F32), "OP": _sb(2, U16), "ZW": _sb(64, F32), "ZM": _sb(64, F32), "G2": _sb(48, F32),
@@ -87,10 +91,10 @@ def _relay(g, core, T, topo, routes):
         k = via.index(core)
         src = T.cores[r]
         rid, pid = topo.addr(d, core)
-        m = topo.mask(core, d)
-        n = len(topo.engines(core, d))
+        en = topo.engines(core, d)[::OPT["hand"]]
+        m, n = _bits(en), len(en)
         if k < 2:
-            g.wait_ge(T.sem.hop, len(topo.engines(src, core)) // 2)
+            g.wait_ge(T.sem.hop, OPT["near"] // 2)
             g.remote_dma(T["lq%d" % t][:, 96 * k:96 * k + 96].bitcast(dt.uint8), T.rq[:].bitcast(dt.uint8),
                          T.sem["arr%d" % t], T.sem.sent, pid, rid, m)
         else:
@@ -126,7 +130,7 @@ def _deps(ops):
     return deps
 
 
-def _order(ops, deps):
+def _order(ops, deps, rows_of, other):
     n, wake = len(ops), OPT["wake"]
     pre = [set(d) for d in deps]
     sends = []
@@ -142,25 +146,98 @@ def _order(ops, deps):
         tail[i] += ops[i][5]
         for j in pre[i]:
             tail[j] = max(tail[j], tail[i] + wake)
-    busy = {}
-    start, end = [0.0] * n, [0.0] * n
-    for i in sorted(range(n), key=lambda k: (-tail[k], k)):
-        q, kind = ops[i][0], ops[i][4]
-        t = max([0.0] + [end[j] + wake for j in pre[i]])
-        hold = 80.0 if kind is not None and kind[0] == "dma" else ops[i][5]
-        for (a, b) in sorted(busy.setdefault(q, [])):
-            if t + hold <= a:
-                break
-            t = max(t, b)
-        busy[q].append((t, t + hold))
-        start[i], end[i] = t, t + ops[i][5]
-    return sorted(range(n), key=lambda k: (start[k], k))
+        for (j, k) in rows_of:
+            if k == i:
+                tail[j] = max(tail[j], tail[i])
+
+    def lay(rank, before):
+        busy = {}
+        start, end = [0.0] * n, [0.0] * n
+        for i in sorted(range(n), key=rank):
+            q, kind = ops[i][0], ops[i][4]
+            t = max([0.0] + [end[j] + wake for j in before[i]])
+            hold = 80.0 if kind is not None and kind[0] == "dma" else ops[i][5]
+            slots = busy.setdefault(q, [])
+            for (a, b) in slots:
+                if t + hold <= a:
+                    break
+                t = max(t, b)
+            slots.append((t, t + hold))
+            slots.sort()
+            start[i], end[i] = t, t + ops[i][5]
+        return start, end
+
+    start = lay(lambda k: (-tail[k], k), pre)[0]
+    order = sorted(range(n), key=lambda k: (start[k], k))
+    pre = [sorted(p) for p in pre]
+    dmas = {i for i in range(n) if ops[i][4] is not None and ops[i][4][0] == "dma"}
+
+    def play(order, moved):
+        total, held = 0.0, []
+        for (f, w) in OPT["paces"]:
+            end, why, free, prev = [0.0] * n, [None] * n, {}, {}
+            for i in order:
+                o = other[i] if i in moved else ops[i]
+                q = o[0]
+                t, y = free.get(q, 0.0), (prev.get(q), True)
+                for j in pre[i]:
+                    if end[j] + w > t:
+                        t, y = end[j] + w, (j, False)
+                end[i] = t + (o[5] * f if o[4] is None else o[5])
+                why[i], free[q], prev[q] = y, t + 80.0 if i in dmas else end[i], i
+            i = max(range(n), key=lambda k: end[k])
+            total += end[i]
+            while i is not None:
+                if why[i][1] and why[i][0] is not None:
+                    held.append((why[i][0], i))
+                i = why[i][0]
+        return total, held
+
+    post = [[] for _ in range(n)]
+    for i in range(n):
+        for j in pre[i]:
+            post[j].append(i)
+    moved = frozenset()
+    now, held = play(order, moved)
+    best = (now, order, moved)
+    seed = 1
+    for _ in range(OPT["passes"]):
+        seed = (seed * 1103515245 + 12345) % 2 ** 31
+        j, i = held[(seed >> 8) % len(held)]
+        a, b = order.index(j), order.index(i)
+        between = order[a:b + 1]
+        swap = moved
+        if seed >> 27 & 3 == 0 and (i in other or j in other):
+            swap, trial = moved ^ {i if i in other and (seed >> 26 & 1 or j not in other) else j}, between
+        elif seed >> 29 & 1:
+            group = {i}
+            for k in reversed(between):
+                if k in group:
+                    group.update(pre[k])
+            trial = [k for k in between if k in group] + [k for k in between if k not in group]
+        else:
+            group = {j}
+            for k in between:
+                if k in group:
+                    group.update(post[k])
+            trial = [k for k in between if k not in group] + [k for k in between if k in group]
+        trial = order[:a] + trial + order[b + 1:]
+        t, h = play(trial, swap)
+        if t <= now + OPT["slack"] * (1.0 - _ / OPT["passes"]) * (seed >> 4 & 255) / 255.0:
+            now, held, order, moved = t, h, trial, swap
+            if t < best[0]:
+                best = (t, trial, swap)
+    return best[1:]
 
 
-def _emit(g, T, ops, last):
+def _emit(g, T, ops, last, rows_of, other):
     queue = {"V": g.vector, "S": g.scalar, "P": g.tensor, "G": g, "Y": g.sync}
     deps = _deps(ops)
-    order = _order(ops, deps)
+    shape = tuple((o[0], o[5]) for o in ops)
+    if shape not in ORDERS:
+        ORDERS[shape] = _order(ops, deps, rows_of, other)
+    order, moved = ORDERS[shape]
+    ops = [other[i] if i in moved else o for i, o in enumerate(ops)]
     pos = {i: k for k, i in enumerate(order)}
     clock = {q: {} for q in queue}
     after, waits, signal = {}, {}, set()
@@ -221,6 +298,8 @@ def rank_program(g, core, T, topo):
     A = AluOpType
     ACT = ActivationFunctionType
     ops = []
+    rows_of = []
+    other = {}
     cy, ga = OPT["cy"], OPT["ga"]
 
     def v(name, a=0, b=None, s=1):
@@ -282,7 +361,7 @@ def rank_program(g, core, T, topo):
     def quant(q, s, a):
         ops.append(("V", lambda: g.vector.quantize_mx(q[0], s[0], a[0]), regs(a), regs(q, s), None, 12.0 + 0.26 * a[2]))
 
-    def act(o, a, f=ACT.Copy, bias=None, scale=None, acc=None):
+    def act(o, a, f=ACT.Copy, bias=None, scale=None, acc=None, first="S"):
         kw = {}
         if bias is not None:
             kw["bias"] = ap(bias)
@@ -290,8 +369,21 @@ def rank_program(g, core, T, topo):
             kw["scale"] = scale
         if acc is not None:
             kw["accum_out"] = acc[0]
-        c = price(o[2], a, [], 1.01) + (20.0 if acc is not None else 0.0)
+        c = price(o[2], a, [], 1.01) + (20.0 if acc is not None else 0.0) + (15.0 if a[4] else 0.0)
+        if acc is None and f != ACT.Sign:
+            if f == ACT.Relu:
+                ts(o, a, scale, A.mult, 0.0, A.max)
+            elif bias is not None:
+                ts(o, a, scale, A.mult, bias, A.add)
+            elif scale is not None:
+                ts(o, a, scale, A.mult)
+            else:
+                cp(o, a)
+            on_vector = ops.pop()
+            other[len(ops)] = on_vector
         ops.append(("S", lambda: g.scalar.activation(o[0], a[0], f, **kw), regs(a, bias), regs(o, acc), None, c))
+        if first == "V":
+            other[len(ops) - 1], ops[-1] = ops[-1], other[len(ops) - 1]
 
     def affine(o, a, scale, bias):
         act(o, a, ACT.Identity, bias, scale)
@@ -329,8 +421,11 @@ def rank_program(g, core, T, topo):
     def wi(k, a=0, b=64):
         return v("wi", 64 * k + a, 64 * k + b)
 
+    move = {q: lambda o, a, q=q: act(o, a, first=q) for q in "VS"}
+    out_of = {q: lambda o, a, q=q: act(o, a, ACT.Copy, None, 2.0 ** -6, first=q) for q in "VS"}
+
+    dma("Y", T.ut[:], T.u[:], [], v("ut")[1])
     dma("Y", T.X0[:], T.x[:], [], v("X0")[1])
-    dma("S", T.ut[:], T.u[:], [], v("ut")[1])
     dma("Y", u8(v("wq")), T.wc[:], [], v("wq")[1])
     dma("Y", T.wp[:], T.ws[:], [], v("wp")[1])
     dma("Y", T.vt[:], T.v[:], [], v("vt")[1])
@@ -349,12 +444,12 @@ def rank_program(g, core, T, topo):
     fill(v("FW", 0, 400, 207), -BIG)
     cp(pm, col("ci", 1))
     cp(v("uo"), v("ci", 8, 24))
-    ts(v("tmpc"), v("cmod"), pm, A.is_equal)
+    ts(v("D"), v("cmod"), pm, A.is_equal, 2 * BIG, A.mult)
+    ts(v("D"), v("D"), -BIG, A.add)
     fill(v("keep"), 1.0)
     fill(v("keep", 0, 192, 16), 0.0)
     fill(v("R"), BIG)
     fill(v("R", 16, 192, 16), -BIG)
-    affine(v("D"), v("tmpc"), 2 * BIG, -BIG)
     fill(col("KW", 15), 256 * U)
     fill(v("neg"), -BIG)
     for i in range(s0, s1):
@@ -382,7 +477,15 @@ def rank_program(g, core, T, topo):
     fill(v("k3"), 1.0)
     fill(v("k3", 0, 576, 3), 0.0)
     affine(v("cw"), v("tmpd"), 1.0, pm)
-    act(v("cx", 0, 32), v("cw", 0, 32))
+    act(v("f1", 2, 72, 3), v("cw", 1, 25))
+    affine(v("cu"), v("cw", 1, 25), U, U)
+    fill(v("f0"), 1.0)
+    fill(v("f0", 0, 72, 3), 0.0)
+    fill(v("g0"), 1.0)
+    fill(v("g0", 0, 144, 6), 0.0)
+    fill(v("g0", 3, 144, 6), -1.0)
+    fill(v("g1"), WHOLE)
+    fill(v("g1", 1, 144, 6), -0.5)
     fill(v("zero"), 0.0)
     fill(e(5, 0, 2), -97 * U)
     fill(srt(2, 0, 56), (HALF - C) * U)
@@ -406,12 +509,12 @@ def rank_program(g, core, T, topo):
         mm(v(sV, 0, C), v("usq"), v("uss"), xq, xs)
         mm(v(sS, 0, C), v("usq"), v("uss"), xq, xs)
         mm(v(aP, 0, C), v("ukq"), v("uks"), xq, xs)
-        for (a, b) in ((16 * s0, C), (0, 16 * s0)):
+        for (a, b) in OPT["cuts"]:
             tt(v("sm", a, b), v(sV, a, b), v("D", a, b), A.min)
             scan(v("hold", a, b), v("R", a, b), v("sm", a, b), -BIG if a else col("D", 0), A.min, A.max)
             tt(v("eq", a, b), v(sV, a, b), v("hold", a, b), A.is_equal)
             scan(v("ne", a, b), v("keep", a, b), v("eq", a, b), 0.0, A.mult, A.subtract)
-        ts(v("SG", 0, 200 * (s1 - s0), 200), v("ne", 16 * s0 + 15, 16 * s1, 16), -1.0, A.mult)
+        act(v("SG", 0, 200 * (s1 - s0), 200), v("ne", 16 * s0 + 15, 16 * s1, 16), ACT.Copy, None, -1.0, first="V")
         for i in range(12):
             m = 16 * i + 16
             if s0 <= i < s1:
@@ -427,9 +530,10 @@ def rank_program(g, core, T, topo):
             if m < C:
                 ts(v("TT", o + m, o + C), v(sV, m, C), col("hold", m - 1), A.is_gt)
             scan(v("SUM", 96 * i, 96 * i + 96), v("TT", o, o + 96), v("TT", o + 96, o + C), col("ne", m - 1), A.add, A.add)
-        tt(v("SUM", 96 * s0 + 95, 96 * s1, 96), v("acc", 6, 6 + s1 - s0), v("acc", 0, s1 - s0), A.subtract)
-        cp(v("RK"), v("SUM", 95, 12 * 96, 96))
-        cp(v("r", 0, 96), ind(v("lur"), v("RK", 0, 6)))
+        for k in range(s1 - s0):
+            ts(col("RK", s0 + k), col("acc", 6 + k), col("acc", k), A.subtract)
+        cp(v("RK", 0, s0), v("SUM", 95, s0 * 96, 96))
+        act(v("r", 0, 96), ind(v("lur"), v("RK", 0, 6)), first="V")
         act(v("r", 96, C), ind(v("lur"), v("RK", 6, 12)))
         scan(v("FW", 1, C), v(aP, 0, C - 1), v("r", 1, C), -BIG, A.max, A.min)
         scan(v("tid"), v("r"), v("neg"), 0.0, A.add, A.add)
@@ -457,10 +561,7 @@ def rank_program(g, core, T, topo):
         scan(e(21, 0, 72), v("R3"), v("x3", 0, 72), -BIG, A.min, A.max)
         for j in range(3):
             dj, own = v("d144", 48 * j, 48 * j + 48), e(21, 24 * j + 23, 24 * j + 24)
-            if j in OPT["vsub"]:
-                ts(dj, e(2), own, A.subtract, -1.0, A.mult)
-            else:
-                affine(dj, e(2), -1.0, own)
+            act(dj, e(2), ACT.Identity, own, -1.0, first="S" if j else "V")
             tt(v("c144", 48 * j, 48 * j + 48), dj, v("thr", 48 * j, 48 * j + 48), A.is_lt)
         scan(v("s144"), v("k144"), v("c144"), 0.0, A.mult, A.add)
         re = v("RE", 0, 3)
@@ -482,8 +583,8 @@ def rank_program(g, core, T, topo):
         scan(srt(2, 1, 49), v("zero"), srt(0), (HALF - C) * U, A.add, A.subtract)
         scan(v("sA", 1, 48), v("zero", 0, 47), srt(0, 0, 47), col("cf", 1), A.add, A.subtract)
         scatter(srt(1), re, e(14))
-        affine(v("sB", 0, 48), srt(2), 32.0, ROUND)
-        affine(v("sB", 48, 96), v("sA", 0, 48), 32.0, ROUND)
+        act(v("sB", 0, 48), srt(2), ACT.Identity, ROUND, 32.0, first="V")
+        act(v("sB", 48, 96), v("sA", 0, 48), ACT.Identity, ROUND, 32.0, first="V")
         tt(v("bm"), v("sB", 0, 48), v("sB", 48, 96), A.subtract)
         for j in range(2):
             act(v("junk", 1800 + 56 * j, 1848 + 56 * j), srt(2), ACT.Sign, col("cf", 16 + j), -1.0, col("acc", 22 + j))
@@ -500,28 +601,28 @@ def rank_program(g, core, T, topo):
 
         ts(wi(0), v("VV"), 255, A.bitwise_and)
         ts(wi(1), v("VV"), 16, A.arith_shift_right)
-        cp(wf(0, 33, 57), wi(0, 33, 57))
-        recip(wf(1, 33, 57), wf(0, 33, 57))
+        cp(v("g0", 4, 144, 6), wi(0, 33, 57))
+        recip(v("g0", 1, 144, 6), wi(0, 33, 57) if OPT["irec"] else v("g0", 4, 144, 6))
         ts(wi(2), v("VV"), 8, A.logical_shift_right, 255, A.bitwise_and)
-        tt(wf(2, 1, 57), v("cx", 1, 57), wi(1, 1, 57), A.subtract)
-        act(wf(3, 1, 25), wf(2, 1, 25), ACT.Relu, None, -512.0)
-        tt(wf(4, 1, 25), wf(2, 1, 25), wi(2, 1, 25), A.add)
-        tt(wf(5, 1, 25), wf(3, 1, 25), wi(0, 1, 25), A.min)
-        tt(wf(6, 1, 25), wf(4, 1, 25), wf(5, 1, 25), A.add)
-        cp(v("FG", 32, 56), wf(6, 1, 25))
-        tt(wf(3, 33, 57), wf(2, 33, 57), wi(0, 1, 25), A.add)
-        tt(wf(5, 33, 57), wf(3, 33, 57), wf(1, 33, 57), A.mult)
-        tt(wf(4, 33, 57), wf(3, 33, 57), wi(2, 33, 57), A.add)
-        ts(wi(3, 33, 57), wf(5, 33, 57), -0.5, A.add)
-        tt(wf(6, 33, 57), wi(3, 33, 57), wi(0, 33, 57), A.mult)
-        tt(wf(7, 33, 57), wf(4, 33, 57), wf(6, 33, 57), A.subtract)
-        ts(v("FG", 0, 24), wf(7, 33, 57), -0.5, A.add)
+        tt(wf(3, 1, 25), v("VV", 1, 25), v("cu"), A.is_ge)
+        tt(v("f1", 0, 72, 3), wf(3, 1, 25), wi(0, 1, 25), A.mult)
+        tt(v("f1", 1, 72, 3), wi(2, 1, 25), wi(1, 1, 25), A.subtract)
+        scan(v("f2"), v("f0"), v("f1"), 0.0, A.mult, A.add)
+        cp(v("FG", 32, 56), v("f2", 2, 72, 3))
+        tt(wf(2, 33, 57), v("cx", 33, 57), wi(1, 33, 57), A.subtract)
+        ts(v("g1", 4, 144, 6), wi(2, 33, 57), -0.5, A.add)
+        for k in (0, 5):
+            tt(v("g1", k, 144, 6), wf(2, 33, 57), wi(0, 1, 25), A.add)
+        scan(v("g2"), v("g0"), v("g1"), 0.0, A.mult, A.add)
+        cp(v("FG", 0, 24), v("g2", 5, 144, 6))
 
         def zhalf(Z, Gt, o):
             for b in range(4):
                 w = v("XH", C * b, C * b + C)
-                act(v(Gt, C * b, C * b + C), ind(w, v("FG", 32 + o, 44 + o)))
+                move[OPT["zf"][b] if o else "S"](v(Gt, C * b, C * b + C), ind(w, v("FG", 32 + o, 44 + o)))
                 tt(v(Z, b, 768, 4), ind(w, v("FG", o, o + 12)), v(Gt, C * b, C * b + C), A.add)
+                if b:
+                    rows_of.extend([(len(ops) - 4, len(ops) - 2), (len(ops) - 3, len(ops) - 1)])
 
         zhalf("Zb", "Gb", 12)
         zq, zs = "zq%d" % t, "zs%d" % t
@@ -537,7 +638,7 @@ def rank_program(g, core, T, topo):
                 T["ls%d" % t][:], T[zs][:], arr, T.sem.sent, pid, rid, m), v(zs)[1], [], ("remote",), 500.0))
             sent[0] += 2 * n
         else:
-            en = topo.engines(core, via[0])
+            en = topo.engines(core, via[0])[:OPT["near"]]
             h = len(en) // 2
             trs = []
             for k in range(2):
@@ -551,14 +652,14 @@ def rank_program(g, core, T, topo):
                 T.rs[:], T[zs][:], T.sem.hop, T.sem.sent, pid, rid, m), v(zs)[1], [], ("remote",), 500.0))
             sent[0] += 2 * h + len(topo.engines(core, via[2]))
         back = routes[(t, rank ^ STEP[t])][1]
-        total = 2 * len(topo.engines(d, core)) if back is None else sum(len(topo.engines(k, core)) for k in back)
+        total = 2 * len(topo.engines(d, core)) if back is None else sum(len(topo.engines(k, core)[::OPT["hand"]]) for k in back)
         ops.append(("X", None, [], v("lq%d" % t)[1] + v("ls%d" % t)[1], ("arrive", "arr%d" % t, total), OPT["far"][t]))
 
         zhalf("Za", "Ga", 0)
         quant(v("zaq"), v("zas"), v("Za"))
         for b in range(4):
             mm(v("ps%d" % b, 0, C), v("wq", 128 * b, 128 * b + 128), v("wp", 128 * b, 128 * b + 128), v("zaq"), v("zas"))
-            act(v("HH", 384 * b, 384 * b + C), v("ps%d" % b, 0, C), ACT.Copy, None, 2.0 ** -6)
+            out_of[OPT["own"][b]](v("HH", 384 * b, 384 * b + C), v("ps%d" % b, 0, C))
 
         affine(e(16), ind(srt(2, 0, 56), re), 256.0 / U, (C - HALF) * 256.0)
         affine(e(17), e(5), 2.0 - 1.0 / U, 2 * U)
@@ -594,29 +695,27 @@ def rank_program(g, core, T, topo):
                v("lq%d" % t), v("ls%d" % t))
             hw = v("HH", 384 * b, 384 * b + 384)
             how = OPT["state"][b]
-            move = {"V": cp, "S": act}
-            if how[0] == "V":
-                ts(v("HH", 384 * b + C, 384 * b + 384), v("ps%d" % (4 + b), 0, C), 2.0 ** -6, A.mult)
-            else:
-                act(v("HH", 384 * b + C, 384 * b + 384), v("ps%d" % (4 + b), 0, C), ACT.Copy, None, 2.0 ** -6)
-            if len(how) > 2:
-                o = 576 * b
-                act(v("SQ", o + 2, o + 576, 3), v(X, b, 768, 4))
-                move[how[1]](v("SQ", o, o + 576, 3), ind(hw, v("PQ", 0, 12)))
-                move[how[2]](v("SQ", o + 1, o + 576, 3), ind(hw, v("PQ", 16, 28)))
-                scan(v("SO", o, o + 576), v("k3"), v("SQ", o, o + 576), 0.0, A.mult, A.add)
-                move[how[3]](v(Xn, b, 768, 4), v("SO", o + 2, o + 576, 3))
-            else:
-                move[how[1]](v("HQ", C * b, C * b + C), ind(hw, v("PQ", 16, 28)))
-                tt(v("HS", C * b, C * b + C), ind(hw, v("PQ", 0, 12)), v("HQ", C * b, C * b + C), A.add)
-                tt(v(Xn, b, 768, 4), v("HS", C * b, C * b + C), v(X, b, 768, 4), A.add)
+            out_of[how[0]](v("HH", 384 * b + C, 384 * b + 384), v("ps%d" % (4 + b), 0, C))
+            o = 576 * b
+            act(v("SQ", o + 2, o + 576, 3), v(X, b, 768, 4))
+            for w in range(2):
+                if how[1 + w] == "H":
+                    for k, q in enumerate("VS"):
+                        move[q](v("SQ", o + w + 288 * k, o + 288 * k + 288, 3), ind(hw, v("PQ", 16 * w + 6 * k, 16 * w + 6 * k + 6)))
+                else:
+                    move[how[1 + w]](v("SQ", o + w, o + 576, 3), ind(hw, v("PQ", 16 * w, 16 * w + 12)))
+            parts = 2 if len(how) > 4 else 1
+            for k in range(parts):
+                a, n = 576 * k // parts, 576 // parts
+                scan(v("SO", o + a, o + a + n), v("k3", 0, n), v("SQ", o + a, o + a + n), 0.0, A.mult, A.add)
+                move[how[3]](v(Xn, b + 4 * a // 3, 4 * (a + n) // 3, 4), v("SO", o + a + 2, o + a + n, 3))
         quant(v("xq%d" % (t + 1)), v("xs%d" % (t + 1)), v(Xn))
 
     mm(v("ps0", 0, C), v("vq"), v("vs"), v("xq2"), v("xs2"))
     dma("Y", T.oc[:], u8(v("xq2")), v("xq2")[1], [])
-    cp(v("yo"), v("ps0", 0, C))
+    act(v("yo"), v("ps0", 0, C), first="V")
     for k in range(4):
         dma("S", T.osc[4 * k:4 * k + 4, :], T.xs2[32 * k:32 * k + 4, :], v("xs2")[1], [])
     dma("Y", T.y[:], T.yo[:], v("yo")[1], [])
     last.append(("sent", sent[0]))
-    _emit(g, T, ops, last)
+    _emit(g, T, ops, last, rows_of, other)

@@ -9,9 +9,16 @@ U = 65536.0
 HALF = 8.5
 ROUND = 1.5 * 2.0 ** 48
 WHOLE = 1.5 * 2.0 ** 23
+EVEN = 1.5 * 2.0 ** 24
+LOW = -200 * U
+PAD = 64
 F32, BF, I32, U16, U8, MX = "float32", "bfloat16", "int32", "uint16", "uint8", "float8_e4m3fn_x4"
-OPT = {"cuts": ((112, 192), (0, 112)), "irec": True, "state": ("VVSS", "SHSV2", "VVSS", "SVSV"), "sc": (7, 12), "vsub": (0,), "passes": 12000, "paces": ((1.0, 235.0), (1.3, 260.0)), "slack": 60.0, "near": 8, "hand": 2, "zf": "SSSS", "own": "VSVS",
-       "wake": 235.0, "cy": 0.83, "ga": 1.5, "far": (2000.0, 4000.0), "load": 1500.0}
+OPT = {"send": (((192, 256), (256, 384)), ((192, 256), (256, 384))), "own": (((0, 192),), ((0, 192),)),
+       "runs": (((0, 128), (128, 192)), ((0, 192),)), "cuts": (((112, 192), (0, 112)), ((80, 128), (0, 80), (128, 192))),
+       "sc": ((7, 12), (5, 10)), "late": (1, 1), "halves": (1,), "hand": 1, "ways": 1, "first": "codes", "each": (1, 1),
+       "hint": 8, "paces": ((1.0, 1.0, 1.0, 225.0), (1.3, 1.0, 1.0, 250.0)), "least": 0.0, "turn": 0.0, "give": 2000.0,
+       "more": (2, 2500, 300.0, ((1.0, 1.0, 1.0, 205.0), (1.0, 1.0, 1.0, 235.0), (1.25, 1.1, 1.1, 280.0), (1.45, 1.0, 1.0, 235.0))), "cy": 0.83, "ga": 1.5,
+       "far": ((1900.0, 1700.0), (3700.0, 3300.0)), "apart": 600.0, "issue": 250.0, "sweeps": 4, "wide": 80, "tries": 8000, "slack": 300.0, "seed": 1}
 ORDERS = {}
 
 
@@ -20,42 +27,41 @@ def _sb(n, d):
 
 
 SCRATCH = {
-    "X0": _sb(768, BF), "X1": _sb(768, BF), "X2": _sb(768, BF), "XH": _sb(768, BF),
+    "X0": _sb(768, BF), "X1": _sb(1024, BF), "X2": _sb(1024, BF), "XH": _sb(768, BF),
     "ut": _sb(512, BF), "vt": _sb(512, BF),
     "uq": _sb(128, MX), "us": _sb(128, U8), "vq": _sb(128, MX), "vs": _sb(128, U8),
     "usq": _sb(128, MX), "uss": _sb(128, U8), "ukq": _sb(128, MX), "uks": _sb(128, U8),
     "wq": _sb(512, MX), "wp": _sb(512, U8),
-    "xq0": _sb(192, MX), "xs0": _sb(192, U8), "xq1": _sb(192, MX), "xs1": _sb(192, U8), "xq2": _sb(192, MX), "xs2": _sb(192, U8),
-    "Za": _sb(768, BF), "Zb": _sb(768, BF), "Ga": _sb(768, BF), "Gb": _sb(768, BF),
-    "zaq": _sb(192, MX), "zas": _sb(192, U8),
-    "zq0": _sb(192, MX), "zs0": _sb(192, U8), "zq1": _sb(192, MX), "zs1": _sb(192, U8),
-    "lq0": _sb(192, MX), "ls0": _sb(192, U8), "lq1": _sb(192, MX), "ls1": _sb(192, U8),
-    "rq": _sb(96, MX), "rs": _sb(192, U8),
-    "HH": _sb(1536, BF), "SQ": _sb(4 * 576, BF), "SO": _sb(4 * 576, BF),
+    "xq0": _sb(192, MX), "xs0": _sb(192, U8), "xq1": _sb(256, MX), "xs1": _sb(256, U8), "xq2": _sb(256, MX), "xs2": _sb(256, U8),
+    "Z": _sb(5 * 768, BF), "GT": _sb(5 * 768, BF),
+    "zq0": _sb(576, MX), "zs0": _sb(576, U8), "zq1": _sb(576, MX), "zs1": _sb(576, U8),
+    "lq0": _sb(PAD + 384, MX), "ls0": _sb(PAD + 384, U8), "lq1": _sb(PAD + 384, MX), "ls1": _sb(PAD + 384, U8),
+    "rq": _sb(192, MX), "rs": _sb(192, U8),
+    "HH": _sb(1536, BF), "SQ0": _sb(4 * 576, BF), "SQ1": _sb(4 * 576, BF), "SQ2": _sb(4 * 576, BF),
     "yo": _sb(192, F32), "fo": _sb(384, F32),
     "ci": _sb(32, I32), "cf": _sb(32, F32), "uo": _sb(16, U16),
     "cmod": _sb(192, F32), "D": _sb(192, F32), "R": _sb(192, F32), "keep": _sb(192, BF), "iof": _sb(192, F32),
     "dn": _sb(192, BF), "lur": _sb(192, BF), "neg": _sb(192, BF), "k3": _sb(576, BF),
-    "thr": _sb(144, F32), "k144": _sb(144, BF), "tmpd": _sb(96, F32), "tmpe": _sb(144, F32),
-    "zero": _sb(48, F32), "cw": _sb(96, F32), "cx": _sb(64, F32),
-    "lun": _sb(192, BF), "D3": _sb(96, F32), "R3": _sb(72, F32),
+    "ea": _sb(296, BF), "eb": _sb(296, BF), "es": _sb(296, BF), "tmpd": _sb(96, F32), "tmpe": _sb(148, F32),
+    "zero": _sb(48, F32), "cw": _sb(96, F32), "lun": _sb(192, BF), "D3": _sb(96, F32), "R3": _sb(72, F32),
     "nr": _sb(192, BF), "M1": _sb(192, F32), "x3": _sb(96, F32), "sA": _sb(56, F32), "sB": _sb(96, F32),
     "cu": _sb(24, F32), "f0": _sb(72, F32), "f1": _sb(72, F32), "f2": _sb(72, F32),
-    "g0": _sb(144, F32), "g1": _sb(144, F32), "g2": _sb(144, F32),
+    "gg": _sb(640, F32), "g2": _sb(192, F32),
     "sm": _sb(192, F32), "hold": _sb(192, F32), "eq": _sb(192, BF), "ne": _sb(192, BF),
-    "TT": _sb(12 * 192, BF), "SUM": _sb(12 * 96, BF), "SG": _sb(6 * 200, BF), "junk": _sb(14 * 200, BF), "acc": _sb(48, F32),
+    "TT": _sb(12 * 192, BF), "SUM": _sb(12 * 96, BF), "SG": _sb(12 * 200, BF), "junk": _sb(16 * 200, BF), "acc": _sb(48, F32),
     "RK": _sb(12, U16), "aS": _sb(192, F32), "r": _sb(192, BF), "tid": _sb(192, BF),
     "FW": _sb(400, F32), "rec": _sb(192, BF), "ev": _sb(192, BF), "KW": _sb(592, BF), "OE": _sb(2, U16),
-    "e": _sb(24 * 72, F32), "d144": _sb(144, F32), "c144": _sb(144, BF), "s144": _sb(144, BF), "RE": _sb(4, U16),
+    "ka": _sb(200, F32), "kb": _sb(200, F32), "ko": _sb(144, F32), "e": _sb(24 * 72, F32), "RE": _sb(4, U16),
     "srt": _sb(3 * 56, F32), "bm": _sb(48, F32), "OL": _sb(2, U16),
     "XW": _sb(112, F32), "MW": _sb(112, F32), "GW": _sb(80, F32), "VV": _sb(64, I32),
-    "wi": _sb(5 * 64, I32), "wf": _sb(10 * 64, F32), "FG": _sb(64, U16),
-    "bI": _sb(48, I32), "bm2": _sb(24, F32), "OP": _sb(2, U16), "ZW": _sb(64, F32), "ZM": _sb(64, F32), "G2": _sb(48, F32),
+    "wi": _sb(3 * 64, I32), "wf": _sb(32, F32), "FG": _sb(64, U16),
+    "tb": _sb(96, F32), "bm2": _sb(24, F32), "OP": _sb(2, U16), "ZW": _sb(64, F32), "ZM": _sb(64, F32), "G2": _sb(48, F32),
     "V2": _sb(32, I32), "pi": _sb(96, I32), "pf": _sb(160, F32), "PQ": _sb(32, U16),
 }
 for _b in range(8):
     SCRATCH["ps%d" % _b] = ("psum", [128, 512], F32)
-SEMAPHORES = ["V", "S", "P", "G", "arr0", "arr1", "sent", "hop"] + ["d%d" % _i for _i in range(16)]
+SEMAPHORES = ["V", "S", "P", "G", "sent"] + ["arr%d" % _i for _i in range(6)] + ["hop%d" % _i for _i in range(3)] + [
+    "d%d" % _i for _i in range(16)]
 
 
 def _routes(T, topo):
@@ -73,7 +79,7 @@ def _routes(T, topo):
             far = [k for k in range(CORES_ALL) if k not in used and topo.mates(k, d) and topo.may_write(c, k)
                    and topo.may_write(k, d) and topo.die(k) == topo.die(c)][:1]
             used.update(far)
-            out[(t, r)] = (d, near + far)
+            out[(t, r)] = (d, near[:1] + far + near[1:] if OPT["ways"] == 2 else near + far)
     return out
 
 
@@ -84,23 +90,40 @@ def _bits(engs):
     return m
 
 
+def _first_hop(core, via, topo):
+    off = min((topo.engines(core, k) for k in via), key=len)
+    rest = [e for e in topo.engines(core, via[0]) if e not in off]
+    return [rest, off, rest if via[2] in topo.cores_of(core) else off]
+
+
+def _scales(t, k):
+    send = OPT["send"][t]
+    if OPT["each"][t]:
+        return send[k][0], "arr%d" % (3 * t + k)
+    return C if k == len(send) - 1 else send[k][1], "arr%d" % (3 * t)
+
+
 def _relay(g, core, T, topo, routes):
     for (t, r), (d, via) in routes.items():
         if via is None or core not in via:
             continue
-        k = via.index(core)
+        j = via.index(core)
         src = T.cores[r]
         rid, pid = topo.addr(d, core)
         en = topo.engines(core, d)[::OPT["hand"]]
-        m, n = _bits(en), len(en)
-        if k < 2:
-            g.wait_ge(T.sem.hop, OPT["near"] // 2)
-            g.remote_dma(T["lq%d" % t][:, 96 * k:96 * k + 96].bitcast(dt.uint8), T.rq[:].bitcast(dt.uint8),
-                         T.sem["arr%d" % t], T.sem.sent, pid, rid, m)
-        else:
-            g.wait_ge(T.sem.hop, len(topo.engines(src, core)))
-            g.remote_dma(T["ls%d" % t][:], T.rs[:], T.sem["arr%d" % t], T.sem.sent, pid, rid, m)
-        g.wait_ge(T.sem.sent, n)
+        calls = 0
+        for k, (a, b) in enumerate(OPT["send"][t]):
+            sa, sem = _scales(t, k)
+            hop, arr, h = T.sem["hop%d" % k], T.sem[sem], (b - a) // 2
+            if j < 2:
+                g.wait_ge(hop, len(_first_hop(src, via, topo)[j]))
+                g.remote_dma(T["lq%d" % t][:, PAD + a + h * j:PAD + a + h * j + h].bitcast(dt.uint8),
+                             T.rq[:, a - C:a - C + h].bitcast(dt.uint8), arr, T.sem.sent, pid, rid, _bits(en))
+            elif sa < b:
+                g.wait_ge(hop, len(_first_hop(src, via, topo)[j]))
+                g.remote_dma(T["ls%d" % t][:, PAD + sa:PAD + b], T.rs[:, sa - C:b - C], arr, T.sem.sent, pid, rid, _bits(en))
+            calls += j < 2 or sa < b
+        g.wait_ge(T.sem.sent, len(en) * calls)
 
 
 def _deps(ops):
@@ -130,114 +153,194 @@ def _deps(ops):
     return deps
 
 
-def _order(ops, deps, rows_of, other):
-    n, wake = len(ops), OPT["wake"]
+def _order(ops, deps, other, hints):
+    n, paces = len(ops), OPT["paces"]
     pre = [set(d) for d in deps]
-    sends = []
+    sends, lands = [], []
+    fixed = {(j, i): w for (j, i, w) in hints if j not in deps[i]}
     for i, o in enumerate(ops):
         if o[4] is not None and o[4][0] == "remote":
-            if sends:
-                pre[i].add(sends[-1])
+            fixed.update({(j, i): 0.0 for j in sends[-1:]})
             sends.append(i)
         if o[4] is not None and o[4][0] == "arrive":
-            pre[i].add(sends[-1])
-    tail = [0.0] * n
-    for i in range(n - 1, -1, -1):
-        tail[i] += ops[i][5]
-        for j in pre[i]:
-            tail[j] = max(tail[j], tail[i] + wake)
-        for (j, k) in rows_of:
-            if k == i:
-                tail[j] = max(tail[j], tail[i])
-
-    def lay(rank, before):
-        busy = {}
-        start, end = [0.0] * n, [0.0] * n
-        for i in sorted(range(n), key=rank):
-            q, kind = ops[i][0], ops[i][4]
-            t = max([0.0] + [end[j] + wake for j in before[i]])
-            hold = 80.0 if kind is not None and kind[0] == "dma" else ops[i][5]
-            slots = busy.setdefault(q, [])
-            for (a, b) in slots:
-                if t + hold <= a:
-                    break
-                t = max(t, b)
-            slots.append((t, t + hold))
-            slots.sort()
-            start[i], end[i] = t, t + ops[i][5]
-        return start, end
-
-    start = lay(lambda k: (-tail[k], k), pre)[0]
-    order = sorted(range(n), key=lambda k: (start[k], k))
-    pre = [sorted(p) for p in pre]
-    dmas = {i for i in range(n) if ops[i][4] is not None and ops[i][4][0] == "dma"}
-
-    def play(order, moved):
-        total, held = 0.0, []
-        for (f, w) in OPT["paces"]:
-            end, why, free, prev = [0.0] * n, [None] * n, {}, {}
-            for i in order:
-                o = other[i] if i in moved else ops[i]
-                q = o[0]
-                t, y = free.get(q, 0.0), (prev.get(q), True)
-                for j in pre[i]:
-                    if end[j] + w > t:
-                        t, y = end[j] + w, (j, False)
-                end[i] = t + (o[5] * f if o[4] is None else o[5])
-                why[i], free[q], prev[q] = y, t + 80.0 if i in dmas else end[i], i
-            i = max(range(n), key=lambda k: end[k])
-            total += end[i]
-            while i is not None:
-                if why[i][1] and why[i][0] is not None:
-                    held.append((why[i][0], i))
-                i = why[i][0]
-        return total, held
-
+            pre[i].update(sends[-1:])
+            fixed.update({(j, i): OPT["apart"] - o[5] for j in lands[-1:]})
+            lands.append(i)
+    for (j, i) in fixed:
+        pre[i].add(j)
     post = [[] for _ in range(n)]
     for i in range(n):
         for j in pre[i]:
             post[j].append(i)
-    moved = frozenset()
-    now, held = play(order, moved)
-    best = (now, order, moved)
-    seed = 1
-    for _ in range(OPT["passes"]):
-        seed = (seed * 1103515245 + 12345) % 2 ** 31
-        j, i = held[(seed >> 8) % len(held)]
-        a, b = order.index(j), order.index(i)
-        between = order[a:b + 1]
-        swap = moved
-        if seed >> 27 & 3 == 0 and (i in other or j in other):
-            swap, trial = moved ^ {i if i in other and (seed >> 26 & 1 or j not in other) else j}, between
-        elif seed >> 29 & 1:
-            group = {i}
-            for k in reversed(between):
-                if k in group:
-                    group.update(pre[k])
-            trial = [k for k in between if k in group] + [k for k in between if k not in group]
-        else:
-            group = {j}
-            for k in between:
-                if k in group:
-                    group.update(post[k])
-            trial = [k for k in between if k not in group] + [k for k in between if k in group]
-        trial = order[:a] + trial + order[b + 1:]
-        t, h = play(trial, swap)
-        if t <= now + OPT["slack"] * (1.0 - _ / OPT["passes"]) * (seed >> 4 & 255) / 255.0:
-            now, held, order, moved = t, h, trial, swap
-            if t < best[0]:
-                best = (t, trial, swap)
-    return best[1:]
+    def paced(o, f, by, prod):
+        if o[4]:
+            return o[0], o[5], o[5] if o[4][0] == "remote" else 80.0
+        listed = any(SCRATCH[r[0]][2] == U16 for r in o[2])
+        c = max(o[5], OPT["least"] if o[0] == "S" and not listed else 0.0) * f * (prod if o[0] == "P" else by if listed else 1.0)
+        return o[0], c, c + OPT["turn"]
+
+    cost = [[[paced(o, *p[:3]) for o in [ops[i]] + ([other[i]] if i in other else [])] for i in range(n)] for p in paces]
+    lag = [[[(j, fixed.get((j, i), p[3])) for j in pre[i]] for i in range(n)] for p in paces]
+
+    tail = [0.0] * n
+    for i in range(n - 1, -1, -1):
+        tail[i] += cost[-1][i][0][1]
+        for (j, w) in lag[-1][i]:
+            tail[j] = max(tail[j], tail[i] + w)
+    busy, start, end, on = {}, [0.0] * n, [0.0] * n, [0] * n
+    for i in sorted(range(n), key=lambda k: (-tail[k], k)):
+        ready = max([0.0] + [end[j] + w for (j, w) in lag[-1][i]])
+        found = []
+        for z, (q, c, hold) in enumerate(cost[-1][i]):
+            t = ready
+            for (a, b) in busy.get(q, []):
+                if t + hold <= a:
+                    break
+                t = max(t, b)
+            found.append((t + c + 100.0 * z, t, z))
+        _, t, on[i] = min(found)
+        q, c, hold = cost[-1][i][on[i]]
+        busy.setdefault(q, []).append((t, t + hold))
+        busy[q].sort()
+        start[i], end[i] = t, t + c
+    order = sorted(range(n), key=lambda k: (start[k], k))
+    names = sorted({o[0] for o in ops})
+
+    def around(p, a, b):
+        end, free, first = [0.0] * n, {}, {}
+        for k, i in enumerate(order[:a]):
+            q, c, hold = cost[p][i][on[i]]
+            t = max([free.get(q, 0.0)] + [end[j] + w for (j, w) in lag[p][i]])
+            end[i], free[q] = t + c, t + hold
+        need = [0.0] * n
+        for i in reversed(order[b:]):
+            q, c, hold = cost[p][i][on[i]]
+            first[q] = max(c + need[i], hold + first.get(q, 0.0))
+            for (j, w) in lag[p][i]:
+                need[j] = max(need[j], first[q] + w)
+        inside = set(order[a:b])
+        calls = {i: [(names.index(q), c, hold, max([0.0] + [end[j] + w for (j, w) in lag[p][i] if j not in inside]),
+                      [(j, w) for (j, w) in lag[p][i] if j in inside], need[i]) for (q, c, hold) in cost[p][i]] for i in inside}
+        return (calls, [free.get(q, 0.0) for q in names], [first.get(q, 0.0) for q in names],
+                max([0.0] + [end[j] + need[j] for j in order[:a]]))
+
+    def replay(win, parts, states, x, room):
+        total = 0.0
+        for (calls, free, first, top), (end, marks, was) in zip(parts, states):
+            end, (free, top) = end[:], marks[x]
+            free = free[:]
+            for i in win[x:]:
+                q, c, hold, t, links, rest = calls[i][on[i]]
+                if free[q] > t:
+                    t = free[q]
+                for (j, w) in links:
+                    if end[j] + w > t:
+                        t = end[j] + w
+                end[i] = t + c
+                free[q] = t + hold
+                if t + c + rest > top:
+                    top = t + c + rest
+                    if top > was + room:
+                        return BIG
+            total += max(top, max(map(sum, zip(free, first))))
+        return total
+
+    def play(win, parts):
+        total, held, states = 0.0, [], []
+        for (calls, free, first, top) in parts:
+            end, why, free, prev, last, marks = [0.0] * n, {}, free[:], [None] * len(names), None, []
+            for i in win:
+                marks.append((free[:], top))
+                q, c, hold, t, links, rest = calls[i][on[i]]
+                y = None
+                for (j, w) in links:
+                    if end[j] + w > t:
+                        t, y = end[j] + w, j
+                if free[q] >= t:
+                    t, y = free[q], prev[q]
+                    why[i] = (y, True)
+                else:
+                    why[i] = (y, False)
+                end[i], free[q], prev[q] = t + c, t + hold, i
+                if t + c + rest > top:
+                    top, last = t + c + rest, i
+            for q in range(len(names)):
+                if free[q] + first[q] > top:
+                    top, last = free[q] + first[q], prev[q]
+            total += top
+            states.append((end, marks, top))
+            while last is not None:
+                if why[last][1] and why[last][0] is not None:
+                    held.append((why[last][0], last))
+                last = why[last][0]
+        return total, held, states
+
+    seed, wide = OPT["seed"], OPT["wide"]
+    for sweep in range(OPT["sweeps"] + OPT["more"][0]):
+        tries, slack = OPT["tries"], OPT["slack"] * (1.0 - sweep / OPT["sweeps"])
+        if sweep >= OPT["sweeps"]:
+            tries, slack, paces = OPT["more"][1:]
+            cost[:] = [[[paced(o, *p[:3]) for o in [ops[i]] + ([other[i]] if i in other else [])] for i in range(n)] for p in paces]
+            lag[:] = [[[(j, fixed.get((j, i), p[3])) for j in pre[i]] for i in range(n)] for p in paces]
+        for a in range(-(sweep * 37 % (wide // 2)), n - wide // 2, wide // 2):
+            a, b = max(a, 0), min(a + wide, n)
+            win = order[a:b]
+            parts = [around(p, a, b) for p in range(len(paces))]
+            now, held, states = play(win, parts)
+            best = (now, win, [on[i] for i in win])
+            for k in range(tries if held else 0):
+                seed = (seed * 1103515245 + 12345) % 2 ** 31
+                j, i = held[(seed >> 8) % len(held)]
+                x, y = win.index(j), win.index(i)
+                flip, trial = None, win
+                if seed >> 27 & 3 == 0 and x < y and (i in other or j in other):
+                    flip = i if i in other and (seed >> 26 & 1 or j not in other) else j
+                    on[flip] ^= 1
+                else:
+                    ahead = seed >> 29 & 1
+                    if not ahead:
+                        y = min(len(win) - 1, y + (seed >> 12 & 15) * (seed >> 25 & 1))
+                    between = win[x:y + 1]
+                    group = {i if ahead else j}
+                    for z in reversed(between) if ahead else between:
+                        if z in group:
+                            group.update(pre[z] if ahead else post[z])
+                    trial = (win[:x] + [z for z in between if (z in group) == ahead] + [z for z in between if (z in group) != ahead]
+                             + win[y + 1:])
+                if x > y or trial == win and flip is None:
+                    continue
+                room = slack * (1.0 - k / tries) * (seed >> 4 & 255) / 255.0
+                t = replay(trial, parts, states, x, room + OPT["give"])
+                if t <= now + room:
+                    win = trial
+                    now, h, states = play(win, parts)
+                    held = h or held
+                    if t < best[0]:
+                        best = (t, win, [on[z] for z in win])
+                elif flip is not None:
+                    on[flip] ^= 1
+            for i, z in zip(best[1], best[2]):
+                on[i] = z
+            order[a:b] = best[1]
+    return order, frozenset(i for i in range(n) if on[i])
 
 
-def _emit(g, T, ops, last, rows_of, other):
+def _emit(g, T, ops, last, other, hints):
     queue = {"V": g.vector, "S": g.scalar, "P": g.tensor, "G": g, "Y": g.sync}
     deps = _deps(ops)
     shape = tuple((o[0], o[5]) for o in ops)
     if shape not in ORDERS:
-        ORDERS[shape] = _order(ops, deps, rows_of, other)
+        ORDERS[shape] = _order(ops, deps, other, hints)
     order, moved = ORDERS[shape]
     ops = [other[i] if i in moved else o for i, o in enumerate(ops)]
+    deps = [set(d) for d in deps]
+    readers = {}
+    for i in order:
+        for n in {r[0] for r in ops[i][2] if r[0].startswith("ps")}:
+            deps[i].update(j for j in readers.get(n, []) if ops[j][0] != ops[i][0])
+            readers.setdefault(n, []).append(i)
+        for n in {r[0] for r in ops[i][3] if r[0].startswith("ps")}:
+            readers[n] = []
     pos = {i: k for k, i in enumerate(order)}
     clock = {q: {} for q in queue}
     after, waits, signal = {}, {}, set()
@@ -298,8 +401,8 @@ def rank_program(g, core, T, topo):
     A = AluOpType
     ACT = ActivationFunctionType
     ops = []
-    rows_of = []
     other = {}
+    hints = []
     cy, ga = OPT["cy"], OPT["ga"]
 
     def v(name, a=0, b=None, s=1):
@@ -352,14 +455,23 @@ def rank_program(g, core, T, topo):
         ops.append(("V", lambda: g.vector.tensor_tensor_scan(o[0], d0[0], d1[0], ap(init), op0, op1), regs(d0, d1, init), o[1],
                     None, price(o[2], d0, [o, d0, d1])))
 
-    def fill(o, c):
+    def fill(o, c, first="V"):
         ops.append(("V", lambda: g.vector.memset(o[0], c), [], o[1], None, price(o[2], o, [o])))
+        if first != "V":
+            on_vector = ops.pop()
+            if first == "G":
+                iota(o, [[0, o[2]]], int(c))
+            else:
+                z = v("cmod", 0, o[2])
+                ops.append(("S", lambda: g.scalar.activation(o[0], z[0], ACT.Identity, bias=c, scale=0.0), z[1], o[1], None,
+                            price(o[2], z, [], 1.01)))
+            other[len(ops) - 1] = on_vector
 
     def recip(o, a):
         ops.append(("V", lambda: g.vector.reciprocal(o[0], a[0]), regs(a), o[1], None, 190.0 + 6 * cy * o[2]))
 
     def quant(q, s, a):
-        ops.append(("V", lambda: g.vector.quantize_mx(q[0], s[0], a[0]), regs(a), regs(q, s), None, 12.0 + 0.26 * a[2]))
+        ops.append(("V", lambda: g.vector.quantize_mx(q[0], s[0], a[0]), regs(a), regs(q, s), None, 12.0 + 0.22 * a[2]))
 
     def act(o, a, f=ACT.Copy, bias=None, scale=None, acc=None, first="S"):
         kw = {}
@@ -390,7 +502,7 @@ def rank_program(g, core, T, topo):
 
     def mm(o, lq, ls, rq, rs):
         ops.append(("P", lambda: g.tensor.matmul_mx(o[0], lq[0], ls[0], rq[0], rs[0], True, True), regs(lq, ls, rq, rs), o[1],
-                    None, 170.0))
+                    None, (o[2] + 16) * cy))
 
     def iota(o, pat, base, ch=0):
         c = 130.0 + 2 * cy * o[2]
@@ -399,9 +511,12 @@ def rank_program(g, core, T, topo):
         else:
             ops.append(("G", lambda: g.iota(o[0], pat, base, ch, allow_small_or_imprecise_dtypes=True), [], o[1], None, c))
 
-    def dma(q, o, a, rd, wr):
+    def dma(q, o, a, rd, wr, cost=1500.0):
         e = g.sync if q == "Y" else g.scalar
-        ops.append((q, lambda: e.dma_start(o, a), rd, wr, ("dma",), OPT["load"]))
+        ops.append((q, lambda: e.dma_start(o, a), rd, wr, ("dma",), cost))
+
+    def send(fn, rd):
+        ops.append(("G", fn, rd, [], ("remote",), OPT["issue"]))
 
     def u8(x):
         return x[0].bitcast(dt.uint8)
@@ -415,29 +530,26 @@ def rank_program(g, core, T, topo):
     def srt(k, a=0, b=48):
         return v("srt", 56 * k + a, 56 * k + b)
 
-    def wf(k, a, b):
-        return v("wf", 64 * k + a, 64 * k + b)
+    def g0(k):
+        return v("gg", k, C, 8)
 
-    def wi(k, a=0, b=64):
-        return v("wi", 64 * k + a, 64 * k + b)
+    def g1(k):
+        return v("gg", 448 + k, 640, 8)
 
-    move = {q: lambda o, a, q=q: act(o, a, first=q) for q in "VS"}
-    out_of = {q: lambda o, a, q=q: act(o, a, ACT.Copy, None, 2.0 ** -6, first=q) for q in "VS"}
+    dma("Y", T.ut[:], T.u[:], [], v("ut")[1], 1700.0)
+    dma("Y", T.X0[:], T.x[:], [], v("X0")[1], 2050.0)
+    dma("Y", u8(v("wq")), T.wc[:], v("X0")[1], v("wq")[1], 2500.0)
+    dma("Y", T.wp[:], T.ws[:], v("X0")[1], v("wp")[1], 2500.0)
+    dma("Y", T.vt[:], T.v[:], v("X0")[1], v("vt")[1], 2500.0)
 
-    dma("Y", T.ut[:], T.u[:], [], v("ut")[1])
-    dma("Y", T.X0[:], T.x[:], [], v("X0")[1])
-    dma("Y", u8(v("wq")), T.wc[:], [], v("wq")[1])
-    dma("Y", T.wp[:], T.ws[:], [], v("wp")[1])
-    dma("Y", T.vt[:], T.v[:], [], v("vt")[1])
-
-    s0, s1 = OPT["sc"]
     iota(v("ci", 0, 1), [[0, 1]], 0, 1)
     iota(v("cmod"), [[0, 12], [1, 16]], 0)
     iota(v("ci", 8, 24), [[-1, 2], [16, 8]], 1)
     iota(v("iof"), [[1, 192]], 0)
-    iota(v("tmpe"), [[-16, 3], [1, 48]], 0)
+    iota(v("tmpe", 0, 147), [[-16, 3], [1, 49]], 0)
     iota(v("tmpd", 0, 64), [[0, 2], [16, 32]], -16 - C)
     iota(v("tmpd", 64, 96), [[0, 2], [16, 16]], -16 - 96)
+    iota(v("cf", 24, 26), [[1, 2]], 24)
     pm = col("cf", 0)
     fill(v("TT", 0, 12 * 192, 192), 0.0)
     ts(col("ci", 1), col("ci", 0), 15, A.bitwise_and)
@@ -452,45 +564,57 @@ def rank_program(g, core, T, topo):
     fill(v("R", 16, 192, 16), -BIG)
     fill(col("KW", 15), 256 * U)
     fill(v("neg"), -BIG)
-    for i in range(s0, s1):
-        if 16 * i + 16 < C:
-            fill(col("SG", 200 * (i - s0) + C), -(16.0 * i + 15))
-        else:
-            fill(col("acc", 6 + i - s0), C - 1.0)
+    iota(v("SG", C, 2400, 200), [[-16, 12]], -15)
+    fill(col("acc", 12 + 11), C - 1.0, "S")
     fill(v("lur"), BIG)
     fill(v("lur", 0, 23), -BIG)
     act(v("lun"), v("lur"), ACT.Copy, None, -1.0)
     for w in range(3):
         act(v("D3", w, 96, 3), v("D", min(w, 1), 64, 2))
-    fill(v("R3"), BIG)
-    fill(v("R3", 24, 72, 24), -BIG)
+    fill(v("R3"), BIG, "S")
+    fill(v("R3", 24, 72, 24), -BIG, "S")
     affine(col("cf", 1), pm, -U, (7.5 - C) * U)
-    cp(col("sA", 0), col("cf", 1))
+    act(col("sA", 0), col("cf", 1))
     affine(v("dn"), v("iof"), -U, 256 * U)
-    ts(v("thr"), v("tmpe"), pm, A.is_lt, 1e-30, A.mult)
+    fill(v("ea", 0, 294, 2), -EVEN, "S")
+    fill(v("ea", 0, 294, 98), 0.0, "S")
+    ts(v("ea", 1, 294, 2), v("tmpe", 0, 147), pm, A.is_lt, 0.5, A.add)
+    fill(v("eb", 1, 294, 2), -EVEN, "S")
+    fill(v("eb", 96, 294, 98), 0.0, "S")
+    fill(v("ka", 0, 144, 3), BIG, "S")
+    fill(col("ka", 1), -256 * U, "S")
+    fill(v("kb", 1, 144, 3), 0.0, "S")
+    fill(v("kb", 2, 144, 3), BIG, "S")
     for j in range(2):
         affine(col("cf", 8 + j), pm, 1.0, 16 * j + 1.5)
         affine(col("cf", 16 + j), pm, 16 * U, (256 * j - C - 0.5 + HALF) * U)
     affine(col("cf", 22), pm, 16 * U, -97.5 * U)
-    fill(v("k144"), 1.0)
-    fill(v("k144", 0, 144, 48), 0.0)
-    fill(v("k3"), 1.0)
-    fill(v("k3", 0, 576, 3), 0.0)
+    affine(col("cf", 23), pm, -32 * U, (HALF + 96) * 32 * U)
+    fill(v("k3"), 1.0, "G")
+    fill(v("k3", 0, 576, 3), 0.0, "G")
     affine(v("cw"), v("tmpd"), 1.0, pm)
     act(v("f1", 2, 72, 3), v("cw", 1, 25))
     affine(v("cu"), v("cw", 1, 25), U, U)
-    fill(v("f0"), 1.0)
-    fill(v("f0", 0, 72, 3), 0.0)
-    fill(v("g0"), 1.0)
-    fill(v("g0", 0, 144, 6), 0.0)
-    fill(v("g0", 3, 144, 6), -1.0)
-    fill(v("g1"), WHOLE)
-    fill(v("g1", 1, 144, 6), -0.5)
-    fill(v("zero"), 0.0)
-    fill(e(5, 0, 2), -97 * U)
-    fill(srt(2, 0, 56), (HALF - C) * U)
+    fill(v("f0"), 1.0, "G")
+    fill(v("f0", 0, 72, 3), 0.0, "G")
+    fill(v("gg", 0, C), 1.0, "G")
+    fill(g0(0), 0.0, "G")
+    fill(g0(4), -1.0, "G")
+    fill(v("gg", 448, 640), WHOLE, "G")
+    fill(g1(2), -0.5, "S")
+    fill(v("zero"), 0.0, "G")
+    fill(e(5, 0, 2), -97 * U, "G")
+    fill(srt(2, 0, 56), (HALF - C) * U, "G")
     for name in ("XW", "MW", "GW", "ZW", "ZM", "G2"):
-        fill(v(name), -256 * U)
+        fill(v(name), LOW, "G")
+    for t in range(2):
+        if len(OPT["runs"][t]) > 1:
+            fill(v("X%d" % (t + 1), 768, 1024), 0.0, "G")
+    pieces = [[(a, b, a >= C) for (a, b) in OPT["send"][t] + OPT["own"][t]] for t in range(2)]
+    for k in range(5):
+        short = {(a, b) for p in pieces for (a, b, _) in p[k:k + 1] if b - a < 128}
+        for (a, b) in short:
+            fill(v("Z", 768 * k + 4 * (b - a), 768 * k + 512) if a % C else v("Z", 768 * k, 768 * k + 4 * (128 - b + a)), 0.0, "G")
 
     quant(v("uq"), v("us"), v("ut"))
     quant(v("xq0"), v("xs0"), v("X0"))
@@ -502,37 +626,62 @@ def rank_program(g, core, T, topo):
 
     last = []
     sent = [0]
+    landed = {}
     for t in range(2):
-        X, Xn = "X%d" % t, "X%d" % (t + 1)
-        xq, xs = v("xq%d" % t), v("xs%d" % t)
-        sV, sS, aP = "ps0", "ps1", "ps2"
-        mm(v(sV, 0, C), v("usq"), v("uss"), xq, xs)
-        mm(v(sS, 0, C), v("usq"), v("uss"), xq, xs)
-        mm(v(aP, 0, C), v("ukq"), v("uks"), xq, xs)
-        for (a, b) in OPT["cuts"]:
-            tt(v("sm", a, b), v(sV, a, b), v("D", a, b), A.min)
+        X, Xn, SQ, SO = "X%d" % t, "X%d" % (t + 1), "SQ%d" % t, "SQ%d" % (t + 1)
+        xq, xs = "xq%d" % t, "xs%d" % t
+        aP = "ps2"
+        two = t > 0 and len(OPT["runs"][t - 1]) > 1
+        s0, s1 = OPT["sc"][two]
+
+        def row(q, a, b):
+            if two and b > 128:
+                return v("ps%d" % (3 + q), a - 64, b - 64)
+            return v("ps%d" % q, a, b)
+
+        def spans(a, b):
+            if two and b > 128 and (a < 64 or (a < 128 and b == C)):
+                s = min(128, max(64, b - 64))
+                return [(a, s), (s, b)] if a < s else [(a, b)]
+            return [(a, b)]
+
+        for (a, b, k) in ((0, 128, 0), (64, C, 3)) if two else ((0, C, 0),):
+            for q in range(2):
+                mm(v("ps%d" % (k + q), 0, b - a), v("usq"), v("uss"), v(xq, a, b), v(xs, a, b))
+        mm(v(aP, 0, C), v("ukq"), v("uks"), v(xq, 0, C), v(xs, 0, C))
+        for (a, b) in OPT["cuts"][two]:
+            tt(v("sm", a, b), row(0, a, b), v("D", a, b), A.min)
             scan(v("hold", a, b), v("R", a, b), v("sm", a, b), -BIG if a else col("D", 0), A.min, A.max)
-            tt(v("eq", a, b), v(sV, a, b), v("hold", a, b), A.is_equal)
+            tt(v("eq", a, b), row(0, a, b), v("hold", a, b), A.is_equal)
             scan(v("ne", a, b), v("keep", a, b), v("eq", a, b), 0.0, A.mult, A.subtract)
-        act(v("SG", 0, 200 * (s1 - s0), 200), v("ne", 16 * s0 + 15, 16 * s1, 16), ACT.Copy, None, -1.0, first="V")
+        for (a, b) in ((s0, 8), (8, s1)) if two else ((s0, s1),):
+            act(v("SG", 200 * a, 200 * b, 200), v("ne", 16 * a + 15, 16 * b, 16), ACT.Copy, None, -1.0, first="V")
         for i in range(12):
             m = 16 * i + 16
+            own = col("hold", m - 1)
             if s0 <= i < s1:
-                k = i - s0
-                o = 200 * k
-                act(v("SG", o + 1, o + C), v(sS, 1, C), ACT.Sign, col("hold", m - 1), -1.0)
-                act(v("junk", o, o + m), v("SG", o, o + m), ACT.Relu, None, None, col("acc", k))
+                o = 200 * i
+                for (a, b) in spans(1, C):
+                    act(v("SG", o + a, o + b), row(1, a, b), ACT.Sign, own, -1.0)
+                act(v("junk", o, o + m), v("SG", o, o + m), ACT.Relu, None, None, col("acc", i))
                 if m < C:
-                    act(v("junk", o + m, o + C + 1), v("SG", o + m, o + C + 1), ACT.Relu, None, -1.0, col("acc", 6 + k))
+                    act(v("junk", o + m, o + C + 1), v("SG", o + m, o + C + 1), ACT.Relu, None, -1.0, col("acc", 12 + i))
                 continue
             o = 192 * i
-            ts(v("TT", o + 1, o + m), v(sV, 1, m), col("hold", m - 1), A.is_ge)
+            for (a, b) in spans(1, m):
+                ts(v("TT", o + a, o + b), row(0, a, b), own, A.is_ge)
             if m < C:
-                ts(v("TT", o + m, o + C), v(sV, m, C), col("hold", m - 1), A.is_gt)
+                for (a, b) in spans(m, C) if m < 128 else [(m, C)]:
+                    ts(v("TT", o + a, o + b), row(0, a, b), own, A.is_gt)
             scan(v("SUM", 96 * i, 96 * i + 96), v("TT", o, o + 96), v("TT", o + 96, o + C), col("ne", m - 1), A.add, A.add)
-        for k in range(s1 - s0):
-            ts(col("RK", s0 + k), col("acc", 6 + k), col("acc", k), A.subtract)
-        cp(v("RK", 0, s0), v("SUM", 95, s0 * 96, 96))
+        late = s1 - OPT["late"][two]
+        if late > s0:
+            tt(v("SUM", 96 * s0 + 95, 96 * late, 96), v("acc", 12 + s0, 12 + late), v("acc", s0, late), A.subtract)
+        for i in range(late, s1):
+            ts(col("RK", i), col("acc", 12 + i), col("acc", i), A.subtract)
+        cp(v("RK", 0, late), v("SUM", 95, late * 96, 96))
+        if s1 < 12:
+            cp(v("RK", s1, 12), v("SUM", 96 * s1 + 95, 12 * 96, 96))
         act(v("r", 0, 96), ind(v("lur"), v("RK", 0, 6)), first="V")
         act(v("r", 96, C), ind(v("lur"), v("RK", 6, 12)))
         scan(v("FW", 1, C), v(aP, 0, C - 1), v("r", 1, C), -BIG, A.max, A.min)
@@ -542,14 +691,14 @@ def rank_program(g, core, T, topo):
         scan(v("M1"), v("r"), v(aP, 0, C), -BIG, A.min, A.max)
         tt(v("aS"), v(aP, 0, C), v("nr"), A.min)
         for j in range(2):
-            act(v("junk", 200 * (6 + j), 200 * (6 + j) + C), v("tid"), ACT.Sign, col("cf", 8 + j), 0.5 / BIG, col("acc", 18 + j))
+            act(v("junk", 2400 + 200 * j, 2400 + 200 * j + C), v("tid"), ACT.Sign, col("cf", 8 + j), 0.5 / BIG, col("acc", 24 + j))
         for b in range(4):
-            act(v("XH", C * b, C * b + C), v(X, b, 768, 4), ACT.Copy, None, 0.5)
+            act(v("XH", C * b, C * b + C), v(X, b, 768, 4) if t == 0 else v(SQ, 576 * b + 2, 576 * b + 576, 3), ACT.Copy, None, 0.5)
         tt(v("rec"), v(aP, 0, C), v("FW", 0, C), A.is_le)
         tt(v("ev"), v(aP, 0, C), v("FW", 207, 399), A.is_le)
         scan(v("KW", 16, 208), v("rec"), v("dn"), 0.0, A.mult, A.max)
         on = v("OE")
-        ts(on, v("acc", 18, 20), 0.5, A.mult, 95.0, A.add)
+        ts(on, v("acc", 24, 26), 0.5, A.mult, 95.0, A.add)
         scan(v("KW", 208, 400), v("ev"), v("dn"), 0.0, A.mult, A.max)
         scan(v("KW", 400, 592), v("ev"), v("KW", 15, 207), 0.0, A.mult, A.max)
         rows = (v("M1"), v("FW", 208, 400), v("aS"))
@@ -560,123 +709,130 @@ def rank_program(g, core, T, topo):
         tt(e(2, 1, 64, 2), ind(rows[1], on), e(1, 0, 32), A.max)
         scan(e(21, 0, 72), v("R3"), v("x3", 0, 72), -BIG, A.min, A.max)
         for j in range(3):
-            dj, own = v("d144", 48 * j, 48 * j + 48), e(21, 24 * j + 23, 24 * j + 24)
-            act(dj, e(2), ACT.Identity, own, -1.0, first="S" if j else "V")
-            tt(v("c144", 48 * j, 48 * j + 48), dj, v("thr", 48 * j, 48 * j + 48), A.is_lt)
-        scan(v("s144"), v("k144"), v("c144"), 0.0, A.mult, A.add)
+            o = 98 * j
+            act(v("eb", o, o + 96, 2), e(2), ACT.Sign, e(21, 24 * j + 23, 24 * j + 24), -1.0)
+            scan(v("es", o, o + 97), v("ea", o, o + 97), v("eb", o, o + 97), 0.0, A.add, A.subtract)
         re = v("RE", 0, 3)
-        cp(re, v("s144", 47, 144, 48))
+        ts(re, v("es", 96, 294, 98), 0.5, A.mult)
         for w in range(2):
             affine(e(5, 2 + w, 66, 2), ind(v("iof"), on), U, -96 * U)
-        act(e(6, 0, 64, 2), ind(v("KW", 16, 208), on))
+        affine(v("ka", 7, 199, 6), ind(v("iof"), on), U, -255 * U)
+        act(v("kb", 0, 192, 6), ind(v("KW", 16, 208), on))
+        act(v("kb", 3, 195, 6), ind(v("KW", 208, 400), on))
         tt(e(8), e(5), e(5, 2, 50), A.subtract)
-        tt(e(7, 0, 32), ind(v("KW", 400, 592), on), e(6, 0, 64, 2), A.subtract)
-        tt(e(6, 1, 64, 2), ind(v("KW", 208, 400), on), e(7, 0, 32), A.add)
-        affine(e(9), e(5), 1.0, -159 * U)
+        tt(e(7, 0, 32), ind(v("KW", 16, 208), on), v("ka", 1, 193, 6), A.subtract)
+        tt(v("ka", 4, 196, 6), ind(v("KW", 400, 592), on), e(7, 0, 32), A.subtract)
         act(e(10), e(5, 2, 50), ACT.Copy, None, 1.0 / U)
         affine(e(11), e(5), 255.0 / U, 97.0 * 256 - HALF * U)
-        tt(e(12), e(6), e(9), A.add)
-        tt(e(15), e(10), e(11), A.add)
-        act(e(13), e(12), ACT.Relu, None, -1.0)
-        tt(e(14), e(15), e(13), A.subtract)
+        tt(v("ka", 2, 144, 3), e(10), e(11), A.add)
+        scan(v("ko"), v("ka", 0, 144), v("kb", 0, 144), 0.0, A.add, A.min)
         scatter(srt(0), re, e(8))
         scan(srt(2, 1, 49), v("zero"), srt(0), (HALF - C) * U, A.add, A.subtract)
         scan(v("sA", 1, 48), v("zero", 0, 47), srt(0, 0, 47), col("cf", 1), A.add, A.subtract)
-        scatter(srt(1), re, e(14))
+        scatter(srt(1), re, v("ko", 2, 144, 3))
         act(v("sB", 0, 48), srt(2), ACT.Identity, ROUND, 32.0, first="V")
         act(v("sB", 48, 96), v("sA", 0, 48), ACT.Identity, ROUND, 32.0, first="V")
         tt(v("bm"), v("sB", 0, 48), v("sB", 48, 96), A.subtract)
         for j in range(2):
-            act(v("junk", 1800 + 56 * j, 1848 + 56 * j), srt(2), ACT.Sign, col("cf", 16 + j), -1.0, col("acc", 22 + j))
+            act(v("junk", 2800 + 56 * j, 2848 + 56 * j), srt(2), ACT.Sign, col("cf", 16 + j), -1.0, col("acc", 26 + j))
         tt(v("XW", 1, 49), srt(2, 1, 49), srt(1), A.add)
         affine(v("XW", 57, 104), v("XW", 2, 49), 1.0, srt(0, 0, 1))
         affine(col("XW", 104), srt(1, 0, 1), 1.0, (C + HALF) * U)
-        affine(col("acc", 30), srt(0, 0, 1), 1.0 / U, 0.5)
-        affine(v("cx", 32, 64), v("cw", 32, 64), 1.0, col("acc", 30))
-        ts(v("OL"), v("acc", 22, 24), 0.5, A.mult, 24.0, A.add)
+        for w in range(2):
+            affine(col("acc", 30 + w), srt(0, 0, 1), 1.0 / U, 0.5 - 0.5 * w)
+            affine(g1(1 + 6 * w), v("cw", 33, 57), 1.0, col("acc", 30 + w))
+        ts(v("OL"), v("acc", 26, 28), 0.5, A.mult, 24.0, A.add)
         for a in range(2):
-            scan(v("MW", 56 * a + 1, 56 * a + 49), v("bm"), v("XW", 56 * a + 1, 56 * a + 49), -256 * U, A.add, A.min)
+            scan(v("MW", 56 * a + 1, 56 * a + 49), v("bm"), v("XW", 56 * a + 1, 56 * a + 49), LOW, A.add, A.min)
             act(v("GW", 40 * a + 1, 40 * a + 33), ind(v("XW", 56 * a, 56 * a + 56), v("OL")))
             tt(v("VV", 32 * a, 32 * a + 32), ind(v("MW", 56 * a, 56 * a + 56), v("OL")), v("GW", 40 * a, 40 * a + 32), A.max)
 
-        ts(wi(0), v("VV"), 255, A.bitwise_and)
-        ts(wi(1), v("VV"), 16, A.arith_shift_right)
-        cp(v("g0", 4, 144, 6), wi(0, 33, 57))
-        recip(v("g0", 1, 144, 6), wi(0, 33, 57) if OPT["irec"] else v("g0", 4, 144, 6))
-        ts(wi(2), v("VV"), 8, A.logical_shift_right, 255, A.bitwise_and)
-        tt(wf(3, 1, 25), v("VV", 1, 25), v("cu"), A.is_ge)
-        tt(v("f1", 0, 72, 3), wf(3, 1, 25), wi(0, 1, 25), A.mult)
-        tt(v("f1", 1, 72, 3), wi(2, 1, 25), wi(1, 1, 25), A.subtract)
+        vv = v("VV", 1, 57)
+        ts(v("wi", 1, 57), vv, 255, A.bitwise_and)
+        ts(v("wi", 129, 185), vv, 16, A.arith_shift_right)
+        ts(v("wi", 57, 113), vv, 8, A.logical_shift_right, 255, A.bitwise_and)
+        recip(g0(2), v("wi", 33, 57))
+        tt(v("wf", 0, 24), v("VV", 1, 25), v("cu"), A.is_ge)
+        tt(v("f1", 0, 72, 3), v("wf", 0, 24), v("wi", 1, 25), A.mult)
+        tt(v("f1", 1, 72, 3), v("wi", 57, 81), v("wi", 129, 153), A.subtract)
         scan(v("f2"), v("f0"), v("f1"), 0.0, A.mult, A.add)
         cp(v("FG", 32, 56), v("f2", 2, 72, 3))
-        tt(wf(2, 33, 57), v("cx", 33, 57), wi(1, 33, 57), A.subtract)
-        ts(v("g1", 4, 144, 6), wi(2, 33, 57), -0.5, A.add)
-        for k in (0, 5):
-            tt(v("g1", k, 144, 6), wf(2, 33, 57), wi(0, 1, 25), A.add)
-        scan(v("g2"), v("g0"), v("g1"), 0.0, A.mult, A.add)
-        cp(v("FG", 0, 24), v("g2", 5, 144, 6))
+        cp(v("gg", 5, 640, 8), v("wi", 33, 113))
+        for k in (0, 6):
+            tt(g1(k), v("wi", 1, 25), v("wi", 161, 185), A.subtract)
+        scan(v("g2"), v("gg", 0, C), v("gg", 448, 640), 0.0, A.mult, A.add)
+        cp(v("FG", 0, 24), v("g2", 7, C, 8))
 
-        def zhalf(Z, Gt, o):
-            for b in range(4):
-                w = v("XH", C * b, C * b + C)
-                move[OPT["zf"][b] if o else "S"](v(Gt, C * b, C * b + C), ind(w, v("FG", 32 + o, 44 + o)))
-                tt(v(Z, b, 768, 4), ind(w, v("FG", o, o + 12)), v(Gt, C * b, C * b + C), A.add)
-                if b:
-                    rows_of.extend([(len(ops) - 4, len(ops) - 2), (len(ops) - 3, len(ops) - 1)])
+        def lists(w, a, b):
+            return v("FG", 32 * w + a // 16, 32 * w + b // 16)
 
-        zhalf("Zb", "Gb", 12)
-        zq, zs = "zq%d" % t, "zs%d" % t
-        quant(v(zq), v(zs), v("Zb"))
         d, via = routes[(t, rank)]
-        arr = T.sem["arr%d" % t]
-        if via is None:
-            rid, pid = topo.addr(d, core)
-            m, n = topo.mask(core, d), len(topo.engines(core, d))
-            ops.append(("G", lambda zq=zq, t=t, rid=rid, pid=pid, m=m, arr=arr: g.remote_dma(
-                u8(v("lq%d" % t)), u8(v(zq)), arr, T.sem.sent, pid, rid, m), v(zq)[1], [], ("remote",), 500.0))
-            ops.append(("G", lambda zs=zs, t=t, rid=rid, pid=pid, m=m, arr=arr: g.remote_dma(
-                T["ls%d" % t][:], T[zs][:], arr, T.sem.sent, pid, rid, m), v(zs)[1], [], ("remote",), 500.0))
-            sent[0] += 2 * n
-        else:
-            en = topo.engines(core, via[0])[:OPT["near"]]
-            h = len(en) // 2
-            trs = []
-            for k in range(2):
-                rid, pid = topo.addr(via[k], core)
-                trs.append(RemoteDMATransfer(dst_ids=[DstId(rid=rid, pnc=pid)], dma_engine_mask=_bits(en[h * k:h * k + h]),
-                                             remote_sem=T.sem.hop, src=u8(v(zq, 96 * k, 96 * k + 96)), dst=u8(v("rq"))))
-            rid, pid = topo.addr(via[2], core)
-            m = topo.mask(core, via[2])
-            ops.append(("G", lambda trs=trs: g.remote_dma_fused(trs, local_sem=T.sem.sent), v(zq)[1], [], ("remote",), 500.0))
-            ops.append(("G", lambda zs=zs, rid=rid, pid=pid, m=m: g.remote_dma(
-                T.rs[:], T[zs][:], T.sem.hop, T.sem.sent, pid, rid, m), v(zs)[1], [], ("remote",), 500.0))
-            sent[0] += 2 * h + len(topo.engines(core, via[2]))
         back = routes[(t, rank ^ STEP[t])][1]
-        total = 2 * len(topo.engines(d, core)) if back is None else sum(len(topo.engines(k, core)[::OPT["hand"]]) for k in back)
-        ops.append(("X", None, [], v("lq%d" % t)[1] + v("ls%d" % t)[1], ("arrive", "arr%d" % t, total), OPT["far"][t]))
-
-        zhalf("Za", "Ga", 0)
-        quant(v("zaq"), v("zas"), v("Za"))
-        for b in range(4):
-            mm(v("ps%d" % b, 0, C), v("wq", 128 * b, 128 * b + 128), v("wp", 128 * b, 128 * b + 128), v("zaq"), v("zas"))
-            out_of[OPT["own"][b]](v("HH", 384 * b, 384 * b + C), v("ps%d" % b, 0, C))
+        lq, ls, zq, zs = "lq%d" % t, "ls%d" % t, "zq%d" % t, "zs%d" % t
+        for k, (a, b, away) in enumerate(pieces[t]):
+            n, o = b - a, 768 * k
+            wide = max(n, 128)
+            z = o + 4 * (wide - n) if a % C == 0 else o
+            for p in range(4):
+                w = v("XH", C * p, C * p + C)
+                gt = v("GT", o + C * p, o + C * p + n)
+                act(gt, ind(w, lists(1, a, b)))
+                tt(v("Z", z + p, z + 4 * n, 4), ind(w, lists(0, a, b)), gt, A.add)
+            if not away:
+                quant(v(lq, PAD + b - wide, PAD + b), v(ls, PAD + b - wide, PAD + b), v("Z", o, o + 4 * wide))
+                continue
+            lo = a - 64 - (wide - n if a == C else 0)
+            quant(v(zq, lo, lo + wide), v(zs, lo, lo + wide), v("Z", o, o + 4 * wide))
+            sa, sem = _scales(t, k)
+            codes, scales = v(zq, a - 64, b - 64), v(zs, sa - 64, b - 64)
+            arr, hop = T.sem[sem], T.sem["hop%d" % k]
+            if via is None:
+                rid, pid = topo.addr(d, core)
+                m = topo.mask(core, d)
+                calls = [(lambda x=(u8(v(lq, PAD + a, PAD + b)), u8(codes), arr, T.sem.sent, pid, rid, m): g.remote_dma(*x), codes[1]),
+                         (lambda x=(v(ls, PAD + sa, PAD + b)[0], scales[0], arr, T.sem.sent, pid, rid, m): g.remote_dma(*x), scales[1])]
+                counts = [len(topo.engines(core, d))] * 2
+            else:
+                en = _first_hop(core, via, topo)
+                trs = []
+                for j in range(2):
+                    rid, pid = topo.addr(via[j], core)
+                    trs.append(RemoteDMATransfer(dst_ids=[DstId(rid=rid, pnc=pid)], dma_engine_mask=_bits(en[j]), remote_sem=hop,
+                                                 src=u8(v(zq, a - 64 + n // 2 * j, a - 64 + n // 2 * (j + 1))),
+                                                 dst=u8(v("rq", a - C, a - C + n // 2))))
+                rid, pid = topo.addr(via[2], core)
+                calls = [(lambda x=trs: g.remote_dma_fused(x, local_sem=T.sem.sent), codes[1]),
+                         (lambda x=(v("rs", sa - C, b - C)[0], scales[0], hop, T.sem.sent, pid, rid, _bits(en[2])): g.remote_dma(*x),
+                          scales[1])]
+                counts = [len(en[0] + en[1]), len(en[2])]
+            if sa == b:
+                calls, counts = calls[:1], counts[:1]
+            sent[0] += sum(counts)
+            for fn, rd in calls if OPT["first"] == "codes" else calls[::-1]:
+                send(fn, rd)
+            for j, c in enumerate([d, d] if back is None else back):
+                if j < (1 if back is None else 2) or sa < b:
+                    landed[sem] = landed.get(sem, 0) + len(topo.engines(c, core)[::1 if back is None else OPT["hand"]])
+            if sa < b:
+                ops.append(("X%d" % k, None, [], v(lq, PAD + sa, PAD + b)[1] + v(ls, PAD + sa, PAD + b)[1],
+                            ("arrive", sem, landed[sem]), OPT["far"][t][min(k, 1)]))
 
         affine(e(16), ind(srt(2, 0, 56), re), 256.0 / U, (C - HALF) * 256.0)
         affine(e(17), e(5), 2.0 - 1.0 / U, 2 * U)
-        act(e(18), e(12), ACT.Relu, None, -2.0)
+        act(e(18), v("ko", 1, 144, 3), ACT.Copy, None, -2.0)
         tt(e(19), e(10), e(17), A.add)
         tt(e(20), e(19), e(18), A.add)
-        ts(v("bI", 0, 24), e(5, 0, 48, 2), 1.0 / U, A.mult, 97.0, A.add)
-        ts(v("bI", 24, 48), v("bI", 0, 24), 15, A.bitwise_and)
-        ts(v("bm2"), v("bI", 24, 48), pm, A.is_le, 512 * U, A.mult)
-        act(v("junk", 2100, 2124), e(5, 0, 48, 2), ACT.Sign, col("cf", 22), -1.0, col("acc", 26))
-        op = v("OP", 0, 1)
-        ts(op, col("acc", 26), 0.5, A.mult, 12.0, A.add)
+        affine(v("tb", 0, 24), e(5, 0, 48, 2), 32.0, (HALF + 97) * 32 * U)
+        affine(v("tb", 24, 48), e(5, 0, 48, 2), 32.0, col("cf", 23))
+        affine(v("tb", 48, 96), v("tb", 0, 48), 1.0, ROUND)
+        tt(v("bm2"), v("tb", 48, 72), v("tb", 72, 96), A.subtract)
+        act(v("junk", 3000, 3024), e(5, 0, 48, 2), ACT.Sign, col("cf", 22), -1.0, col("acc", 28))
+        ts(v("OP"), v("cf", 24, 26), col("acc", 28), A.add)
+        tt(v("ZW", 2, 50), e(20), e(16), A.add)
+        act(v("G2", 1, 33), ind(v("ZW"), v("OP")))
         for w in range(2):
-            tt(v("ZW", 32 * w + 1, 32 * w + 25), e(20, w, 48, 2), e(16, w, 48, 2), A.add)
-            act(v("G2", 24 * w + 1, 24 * w + 17), ind(v("ZW", 32 * w, 32 * w + 32), op))
-            scan(v("ZM", 32 * w + 1, 32 * w + 25), v("bm2"), v("ZW", 32 * w + 1, 32 * w + 25), -256 * U, A.add, A.min)
-            tt(v("V2", 16 * w, 16 * w + 16), ind(v("ZM", 32 * w, 32 * w + 32), op), v("G2", 24 * w, 24 * w + 16), A.max)
+            scan(v("ZM", 2 + w, 50, 2), v("bm2"), v("ZW", 2 + w, 50, 2), LOW, A.add, A.min)
+        tt(v("V2"), ind(v("ZM"), v("OP")), v("G2", 0, 32), A.max)
         ts(v("pi", 0, 32), v("V2"), 17, A.arith_shift_right)
         ts(v("pi", 32, 64), v("V2"), 255, A.bitwise_and)
         ts(v("pi", 64, 96), v("V2"), 8, A.logical_shift_right, 511, A.bitwise_and)
@@ -687,35 +843,45 @@ def rank_program(g, core, T, topo):
         tt(v("pf", 128, 160), v("pf", 64, 96), v("pf", 96, 128), A.add)
         cp(v("PQ", 0, 28), v("pf", 129, 157))
         if t == 1:
-            act(v("fo"), ind(v("iof"), v("FG", 32, 56)))
+            act(v("fo"), ind(v("iof"), lists(1, 0, 2 * C)))
             dma("Y", T.ol[:], T.fo[0:128:16, :], v("fo")[1], [])
 
-        for b in range(4):
-            mm(v("ps%d" % (4 + b), 0, C), v("wq", 128 * b, 128 * b + 128), v("wp", 128 * b, 128 * b + 128),
-               v("lq%d" % t), v("ls%d" % t))
-            hw = v("HH", 384 * b, 384 * b + 384)
-            how = OPT["state"][b]
-            out_of[how[0]](v("HH", 384 * b + C, 384 * b + 384), v("ps%d" % (4 + b), 0, C))
-            o = 576 * b
-            act(v("SQ", o + 2, o + 576, 3), v(X, b, 768, 4))
-            for w in range(2):
-                if how[1 + w] == "H":
-                    for k, q in enumerate("VS"):
-                        move[q](v("SQ", o + w + 288 * k, o + 288 * k + 288, 3), ind(hw, v("PQ", 16 * w + 6 * k, 16 * w + 6 * k + 6)))
-                else:
-                    move[how[1 + w]](v("SQ", o + w, o + 576, 3), ind(hw, v("PQ", 16 * w, 16 * w + 12)))
-            parts = 2 if len(how) > 4 else 1
-            for k in range(parts):
-                a, n = 576 * k // parts, 576 // parts
-                scan(v("SO", o + a, o + a + n), v("k3", 0, n), v("SQ", o + a, o + a + n), 0.0, A.mult, A.add)
-                move[how[3]](v(Xn, b + 4 * a // 3, 4 * (a + n) // 3, 4), v("SO", o + a + 2, o + a + n, 3))
-        quant(v("xq%d" % (t + 1)), v("xs%d" % (t + 1)), v(Xn))
+        turn = list(OPT["own"][t]) + [(_scales(t, k)[0], b) for k, (a, b) in enumerate(OPT["send"][t]) if _scales(t, k)[0] < b]
+        for i, (a, b) in enumerate(turn):
+            lo = b - max(b - a, 128)
+            for p in range(4):
+                bank = "ps%d" % (4 * ((len(turn) - i) % 2) + p)
+                mm(v(bank, 0, b - lo), v("wq", 128 * p, 128 * p + 128), v("wp", 128 * p, 128 * p + 128),
+                   v(lq, PAD + lo, PAD + b), v(ls, PAD + lo, PAD + b))
+                act(v("HH", 384 * p + a, 384 * p + b), v(bank, a - lo, b - lo), ACT.Copy, None, 2.0 ** -6, first="VS"[p % 2])
+        if t == 0:
+            for p in range(4):
+                act(v(SQ, 576 * p + 2, 576 * p + 576, 3), v(X, p, 768, 4))
+        picks = {}
+        for (a, b) in OPT["runs"][t]:
+            for p in range(4):
+                hw = v("HH", 384 * p, 384 * p + 384)
+                o = 576 * p
+                cut = [(a, (a + b) // 2), ((a + b) // 2, b)] if p in OPT["halves"] and b - a == C else [(a, b)]
+                for w in range(2):
+                    for (i, j) in cut if w == 0 else [(a, b)]:
+                        act(v(SQ, o + 3 * i + w, o + 3 * j, 3), ind(hw, v("PQ", 16 * w + i // 16, 16 * w + j // 16)), first="VS"[w])
+                        picks.setdefault(a, []).append(len(ops) - 1)
+                        if a and OPT["hint"]:
+                            hints.extend((k, len(ops) - 1, 0.0) for k in picks[0][:OPT["hint"]])
+                for (i, j) in cut:
+                    scan(v(SO, o + 3 * i, o + 3 * j), v("k3", 0, 3 * (j - i)), v(SQ, o + 3 * i, o + 3 * j), 0.0, A.mult, A.add)
+                    act(v(Xn, 4 * i + p, 4 * j, 4), v(SO, o + 3 * i + 2, o + 3 * j, 3), first="V")
+            n = max(b, a + 128)
+            quant(v("xq%d" % (t + 1), a, n), v("xs%d" % (t + 1), a, n), v(Xn, 4 * a, 4 * n))
 
-    mm(v("ps0", 0, C), v("vq"), v("vs"), v("xq2"), v("xs2"))
-    dma("Y", T.oc[:], u8(v("xq2")), v("xq2")[1], [])
-    act(v("yo"), v("ps0", 0, C), first="V")
+    for k, (a, b) in enumerate(OPT["runs"][1]):
+        lo = b - max(b - a, 128)
+        mm(v("ps%d" % k, 0, b - lo), v("vq"), v("vs"), v("xq2", lo, b), v("xs2", lo, b))
+        dma("Y", T.oc[:, 4 * a:4 * b], u8(v("xq2", a, b)), v("xq2", a, b)[1], [])
+        act(v("yo", a, b), v("ps%d" % k, a - lo, b - lo), first="V")
+        dma("Y", T.y[:, a:b], T.yo[:, a:b], v("yo", a, b)[1], [])
     for k in range(4):
-        dma("S", T.osc[4 * k:4 * k + 4, :], T.xs2[32 * k:32 * k + 4, :], v("xs2")[1], [])
-    dma("Y", T.y[:], T.yo[:], v("yo")[1], [])
+        dma("S", T.osc[4 * k:4 * k + 4, :], T.xs2[32 * k:32 * k + 4, 0:C], v("xs2", 0, C)[1], [])
     last.append(("sent", sent[0]))
-    _emit(g, T, ops, last, rows_of, other)
+    _emit(g, T, ops, last, other, hints)

from concourse.bass import DstId, RemoteDMATransfer
from concourse.mybir import dt, AluOpType, ActivationFunctionType

C = 192
STEP = [4, 3]
CORES_ALL = 256
BIG = 2.0 ** 96
U = 65536.0
HALF = 8.5
ROUND = 1.5 * 2.0 ** 48
WHOLE = 1.5 * 2.0 ** 23
EVEN = 1.5 * 2.0 ** 24
LOW = -200 * U
PAD = 64
F32, BF, I32, U16, U8, MX = "float32", "bfloat16", "int32", "uint16", "uint8", "float8_e4m3fn_x4"
OPT = {"send": (((192, 256), (256, 384)), ((192, 256), (256, 384))), "own": (((0, 192),), ((0, 192),)),
       "runs": (((0, 128), (128, 192)), ((0, 192),)), "cuts": (((112, 192), (0, 112)), ((80, 128), (0, 80), (128, 192))),
       "sc": ((7, 12), (5, 10)), "late": (1, 1), "halves": (1,), "hand": 1, "ways": 1, "first": "codes", "each": (1, 1),
       "hint": 8, "paces": ((1.0, 1.0, 1.0, 225.0), (1.3, 1.0, 1.0, 250.0)), "least": 0.0, "turn": 0.0, "give": 2000.0,
       "more": (2, 2500, 300.0, ((1.0, 1.0, 1.0, 205.0), (1.0, 1.0, 1.0, 235.0), (1.25, 1.1, 1.1, 280.0), (1.45, 1.0, 1.0, 235.0))), "cy": 0.83, "ga": 1.5,
       "far": ((1900.0, 1700.0), (3700.0, 3300.0)), "apart": 600.0, "issue": 250.0, "sweeps": 4, "wide": 80, "tries": 8000, "slack": 300.0, "seed": 1}
ORDERS = {}


def _sb(n, d):
    return ("sbuf", [128, n], d)


SCRATCH = {
    "X0": _sb(768, BF), "X1": _sb(1024, BF), "X2": _sb(1024, BF), "XH": _sb(768, BF),
    "ut": _sb(512, BF), "vt": _sb(512, BF),
    "uq": _sb(128, MX), "us": _sb(128, U8), "vq": _sb(128, MX), "vs": _sb(128, U8),
    "usq": _sb(128, MX), "uss": _sb(128, U8), "ukq": _sb(128, MX), "uks": _sb(128, U8),
    "wq": _sb(512, MX), "wp": _sb(512, U8),
    "xq0": _sb(192, MX), "xs0": _sb(192, U8), "xq1": _sb(256, MX), "xs1": _sb(256, U8), "xq2": _sb(256, MX), "xs2": _sb(256, U8),
    "Z": _sb(5 * 768, BF), "GT": _sb(5 * 768, BF),
    "zq0": _sb(576, MX), "zs0": _sb(576, U8), "zq1": _sb(576, MX), "zs1": _sb(576, U8),
    "lq0": _sb(PAD + 384, MX), "ls0": _sb(PAD + 384, U8), "lq1": _sb(PAD + 384, MX), "ls1": _sb(PAD + 384, U8),
    "rq": _sb(192, MX), "rs": _sb(192, U8),
    "HH": _sb(1536, BF), "SQ0": _sb(4 * 576, BF), "SQ1": _sb(4 * 576, BF), "SQ2": _sb(4 * 576, BF),
    "yo": _sb(192, F32), "fo": _sb(384, F32),
    "ci": _sb(32, I32), "cf": _sb(32, F32), "uo": _sb(16, U16),
    "cmod": _sb(192, F32), "D": _sb(192, F32), "R": _sb(192, F32), "keep": _sb(192, BF), "iof": _sb(192, F32),
    "dn": _sb(192, BF), "lur": _sb(192, BF), "neg": _sb(192, BF), "k3": _sb(576, BF),
    "ea": _sb(296, BF), "eb": _sb(296, BF), "es": _sb(296, BF), "tmpd": _sb(96, F32), "tmpe": _sb(148, F32),
    "zero": _sb(48, F32), "cw": _sb(96, F32), "lun": _sb(192, BF), "D3": _sb(96, F32), "R3": _sb(72, F32),
    "nr": _sb(192, BF), "M1": _sb(192, F32), "x3": _sb(96, F32), "sA": _sb(56, F32), "sB": _sb(96, F32),
    "cu": _sb(24, F32), "f0": _sb(72, F32), "f1": _sb(72, F32), "f2": _sb(72, F32),
    "gg": _sb(640, F32), "g2": _sb(192, F32),
    "sm": _sb(192, F32), "hold": _sb(192, F32), "eq": _sb(192, BF), "ne": _sb(192, BF),
    "TT": _sb(12 * 192, BF), "SUM": _sb(12 * 96, BF), "SG": _sb(12 * 200, BF), "junk": _sb(16 * 200, BF), "acc": _sb(48, F32),
    "RK": _sb(12, U16), "aS": _sb(192, F32), "r": _sb(192, BF), "tid": _sb(192, BF),
    "FW": _sb(400, F32), "rec": _sb(192, BF), "ev": _sb(192, BF), "KW": _sb(592, BF), "OE": _sb(2, U16),
    "ka": _sb(200, F32), "kb": _sb(200, F32), "ko": _sb(144, F32), "e": _sb(24 * 72, F32), "RE": _sb(4, U16),
    "srt": _sb(3 * 56, F32), "bm": _sb(48, F32), "OL": _sb(2, U16),
    "XW": _sb(112, F32), "MW": _sb(112, F32), "GW": _sb(80, F32), "VV": _sb(64, I32),
    "wi": _sb(3 * 64, I32), "wf": _sb(32, F32), "FG": _sb(64, U16),
    "tb": _sb(96, F32), "bm2": _sb(24, F32), "OP": _sb(2, U16), "ZW": _sb(64, F32), "ZM": _sb(64, F32), "G2": _sb(48, F32),
    "V2": _sb(32, I32), "pi": _sb(96, I32), "pf": _sb(160, F32), "PQ": _sb(32, U16),
}
for _b in range(8):
    SCRATCH["ps%d" % _b] = ("psum", [128, 512], F32)
SEMAPHORES = ["V", "S", "P", "G", "sent"] + ["arr%d" % _i for _i in range(6)] + ["hop%d" % _i for _i in range(3)] + [
    "d%d" % _i for _i in range(16)]


def _routes(T, topo):
    cores = list(T.cores)
    used = set(cores)
    out = {}
    for t, s in enumerate(STEP):
        for r, c in enumerate(cores):
            d = cores[r ^ s]
            if topo.may_write(c, d):
                out[(t, r)] = (d, None)
                continue
            near = [k for k in topo.cores_of(c) if k not in used and topo.may_write(k, d) and topo.die(k) == topo.die(c)][:2]
            used.update(near)
            far = [k for k in range(CORES_ALL) if k not in used and topo.mates(k, d) and topo.may_write(c, k)
                   and topo.may_write(k, d) and topo.die(k) == topo.die(c)][:1]
            used.update(far)
            out[(t, r)] = (d, near[:1] + far + near[1:] if OPT["ways"] == 2 else near + far)
    return out


def _bits(engs):
    m = 0
    for e in engs:
        m |= 1 << e
    return m


def _first_hop(core, via, topo):
    off = min((topo.engines(core, k) for k in via), key=len)
    rest = [e for e in topo.engines(core, via[0]) if e not in off]
    return [rest, off, rest if via[2] in topo.cores_of(core) else off]


def _scales(t, k):
    send = OPT["send"][t]
    if OPT["each"][t]:
        return send[k][0], "arr%d" % (3 * t + k)
    return C if k == len(send) - 1 else send[k][1], "arr%d" % (3 * t)


def _relay(g, core, T, topo, routes):
    for (t, r), (d, via) in routes.items():
        if via is None or core not in via:
            continue
        j = via.index(core)
        src = T.cores[r]
        rid, pid = topo.addr(d, core)
        en = topo.engines(core, d)[::OPT["hand"]]
        calls = 0
        for k, (a, b) in enumerate(OPT["send"][t]):
            sa, sem = _scales(t, k)
            hop, arr, h = T.sem["hop%d" % k], T.sem[sem], (b - a) // 2
            if j < 2:
                g.wait_ge(hop, len(_first_hop(src, via, topo)[j]))
                g.remote_dma(T["lq%d" % t][:, PAD + a + h * j:PAD + a + h * j + h].bitcast(dt.uint8),
                             T.rq[:, a - C:a - C + h].bitcast(dt.uint8), arr, T.sem.sent, pid, rid, _bits(en))
            elif sa < b:
                g.wait_ge(hop, len(_first_hop(src, via, topo)[j]))
                g.remote_dma(T["ls%d" % t][:, PAD + sa:PAD + b], T.rs[:, sa - C:b - C], arr, T.sem.sent, pid, rid, _bits(en))
            calls += j < 2 or sa < b
        g.wait_ge(T.sem.sent, len(en) * calls)


def _deps(ops):
    seen = {}
    deps = []
    for i, (q, fn, rd, wr, kind, cost) in enumerate(ops):
        d = set()
        rd = [(n, _bits(range(lo, hi, s))) for (n, lo, hi, s) in rd]
        wr = [(n, _bits(range(lo, hi, s))) for (n, lo, hi, s) in wr]
        for (n, m) in rd:
            for (j, m2, w) in seen.get(n, []):
                if n.startswith("ps"):
                    if w or ops[j][0] != q:
                        d.add(j)
                elif w and m & m2:
                    d.add(j)
        for (n, m) in wr:
            for (j, m2, w) in seen.get(n, []):
                if n.startswith("ps") or m & m2:
                    d.add(j)
        for (n, m) in wr:
            seen[n] = [e for e in seen.get(n, []) if e[1] & ~m] + [(i, m, True)]
        for (n, m) in rd:
            seen.setdefault(n, []).append((i, m, False))
        d.discard(i)
        deps.append(d)
    return deps


def _order(ops, deps, other, hints):
    n, paces = len(ops), OPT["paces"]
    pre = [set(d) for d in deps]
    sends, lands = [], []
    fixed = {(j, i): w for (j, i, w) in hints if j not in deps[i]}
    for i, o in enumerate(ops):
        if o[4] is not None and o[4][0] == "remote":
            fixed.update({(j, i): 0.0 for j in sends[-1:]})
            sends.append(i)
        if o[4] is not None and o[4][0] == "arrive":
            pre[i].update(sends[-1:])
            fixed.update({(j, i): OPT["apart"] - o[5] for j in lands[-1:]})
            lands.append(i)
    for (j, i) in fixed:
        pre[i].add(j)
    post = [[] for _ in range(n)]
    for i in range(n):
        for j in pre[i]:
            post[j].append(i)
    def paced(o, f, by, prod):
        if o[4]:
            return o[0], o[5], o[5] if o[4][0] == "remote" else 80.0
        listed = any(SCRATCH[r[0]][2] == U16 for r in o[2])
        c = max(o[5], OPT["least"] if o[0] == "S" and not listed else 0.0) * f * (prod if o[0] == "P" else by if listed else 1.0)
        return o[0], c, c + OPT["turn"]

    cost = [[[paced(o, *p[:3]) for o in [ops[i]] + ([other[i]] if i in other else [])] for i in range(n)] for p in paces]
    lag = [[[(j, fixed.get((j, i), p[3])) for j in pre[i]] for i in range(n)] for p in paces]

    tail = [0.0] * n
    for i in range(n - 1, -1, -1):
        tail[i] += cost[-1][i][0][1]
        for (j, w) in lag[-1][i]:
            tail[j] = max(tail[j], tail[i] + w)
    busy, start, end, on = {}, [0.0] * n, [0.0] * n, [0] * n
    for i in sorted(range(n), key=lambda k: (-tail[k], k)):
        ready = max([0.0] + [end[j] + w for (j, w) in lag[-1][i]])
        found = []
        for z, (q, c, hold) in enumerate(cost[-1][i]):
            t = ready
            for (a, b) in busy.get(q, []):
                if t + hold <= a:
                    break
                t = max(t, b)
            found.append((t + c + 100.0 * z, t, z))
        _, t, on[i] = min(found)
        q, c, hold = cost[-1][i][on[i]]
        busy.setdefault(q, []).append((t, t + hold))
        busy[q].sort()
        start[i], end[i] = t, t + c
    order = sorted(range(n), key=lambda k: (start[k], k))
    names = sorted({o[0] for o in ops})

    def around(p, a, b):
        end, free, first = [0.0] * n, {}, {}
        for k, i in enumerate(order[:a]):
            q, c, hold = cost[p][i][on[i]]
            t = max([free.get(q, 0.0)] + [end[j] + w for (j, w) in lag[p][i]])
            end[i], free[q] = t + c, t + hold
        need = [0.0] * n
        for i in reversed(order[b:]):
            q, c, hold = cost[p][i][on[i]]
            first[q] = max(c + need[i], hold + first.get(q, 0.0))
            for (j, w) in lag[p][i]:
                need[j] = max(need[j], first[q] + w)
        inside = set(order[a:b])
        calls = {i: [(names.index(q), c, hold, max([0.0] + [end[j] + w for (j, w) in lag[p][i] if j not in inside]),
                      [(j, w) for (j, w) in lag[p][i] if j in inside], need[i]) for (q, c, hold) in cost[p][i]] for i in inside}
        return (calls, [free.get(q, 0.0) for q in names], [first.get(q, 0.0) for q in names],
                max([0.0] + [end[j] + need[j] for j in order[:a]]))

    def replay(win, parts, states, x, room):
        total = 0.0
        for (calls, free, first, top), (end, marks, was) in zip(parts, states):
            end, (free, top) = end[:], marks[x]
            free = free[:]
            for i in win[x:]:
                q, c, hold, t, links, rest = calls[i][on[i]]
                if free[q] > t:
                    t = free[q]
                for (j, w) in links:
                    if end[j] + w > t:
                        t = end[j] + w
                end[i] = t + c
                free[q] = t + hold
                if t + c + rest > top:
                    top = t + c + rest
                    if top > was + room:
                        return BIG
            total += max(top, max(map(sum, zip(free, first))))
        return total

    def play(win, parts):
        total, held, states = 0.0, [], []
        for (calls, free, first, top) in parts:
            end, why, free, prev, last, marks = [0.0] * n, {}, free[:], [None] * len(names), None, []
            for i in win:
                marks.append((free[:], top))
                q, c, hold, t, links, rest = calls[i][on[i]]
                y = None
                for (j, w) in links:
                    if end[j] + w > t:
                        t, y = end[j] + w, j
                if free[q] >= t:
                    t, y = free[q], prev[q]
                    why[i] = (y, True)
                else:
                    why[i] = (y, False)
                end[i], free[q], prev[q] = t + c, t + hold, i
                if t + c + rest > top:
                    top, last = t + c + rest, i
            for q in range(len(names)):
                if free[q] + first[q] > top:
                    top, last = free[q] + first[q], prev[q]
            total += top
            states.append((end, marks, top))
            while last is not None:
                if why[last][1] and why[last][0] is not None:
                    held.append((why[last][0], last))
                last = why[last][0]
        return total, held, states

    seed, wide = OPT["seed"], OPT["wide"]
    for sweep in range(OPT["sweeps"] + OPT["more"][0]):
        tries, slack = OPT["tries"], OPT["slack"] * (1.0 - sweep / OPT["sweeps"])
        if sweep >= OPT["sweeps"]:
            tries, slack, paces = OPT["more"][1:]
            cost[:] = [[[paced(o, *p[:3]) for o in [ops[i]] + ([other[i]] if i in other else [])] for i in range(n)] for p in paces]
            lag[:] = [[[(j, fixed.get((j, i), p[3])) for j in pre[i]] for i in range(n)] for p in paces]
        for a in range(-(sweep * 37 % (wide // 2)), n - wide // 2, wide // 2):
            a, b = max(a, 0), min(a + wide, n)
            win = order[a:b]
            parts = [around(p, a, b) for p in range(len(paces))]
            now, held, states = play(win, parts)
            best = (now, win, [on[i] for i in win])
            for k in range(tries if held else 0):
                seed = (seed * 1103515245 + 12345) % 2 ** 31
                j, i = held[(seed >> 8) % len(held)]
                x, y = win.index(j), win.index(i)
                flip, trial = None, win
                if seed >> 27 & 3 == 0 and x < y and (i in other or j in other):
                    flip = i if i in other and (seed >> 26 & 1 or j not in other) else j
                    on[flip] ^= 1
                else:
                    ahead = seed >> 29 & 1
                    if not ahead:
                        y = min(len(win) - 1, y + (seed >> 12 & 15) * (seed >> 25 & 1))
                    between = win[x:y + 1]
                    group = {i if ahead else j}
                    for z in reversed(between) if ahead else between:
                        if z in group:
                            group.update(pre[z] if ahead else post[z])
                    trial = (win[:x] + [z for z in between if (z in group) == ahead] + [z for z in between if (z in group) != ahead]
                             + win[y + 1:])
                if x > y or trial == win and flip is None:
                    continue
                room = slack * (1.0 - k / tries) * (seed >> 4 & 255) / 255.0
                t = replay(trial, parts, states, x, room + OPT["give"])
                if t <= now + room:
                    win = trial
                    now, h, states = play(win, parts)
                    held = h or held
                    if t < best[0]:
                        best = (t, win, [on[z] for z in win])
                elif flip is not None:
                    on[flip] ^= 1
            for i, z in zip(best[1], best[2]):
                on[i] = z
            order[a:b] = best[1]
    return order, frozenset(i for i in range(n) if on[i])


def _emit(g, T, ops, last, other, hints):
    queue = {"V": g.vector, "S": g.scalar, "P": g.tensor, "G": g, "Y": g.sync}
    deps = _deps(ops)
    shape = tuple((o[0], o[5]) for o in ops)
    if shape not in ORDERS:
        ORDERS[shape] = _order(ops, deps, other, hints)
    order, moved = ORDERS[shape]
    ops = [other[i] if i in moved else o for i, o in enumerate(ops)]
    deps = [set(d) for d in deps]
    readers = {}
    for i in order:
        for n in {r[0] for r in ops[i][2] if r[0].startswith("ps")}:
            deps[i].update(j for j in readers.get(n, []) if ops[j][0] != ops[i][0])
            readers.setdefault(n, []).append(i)
        for n in {r[0] for r in ops[i][3] if r[0].startswith("ps")}:
            readers[n] = []
    pos = {i: k for k, i in enumerate(order)}
    clock = {q: {} for q in queue}
    after, waits, signal = {}, {}, set()
    for i in order:
        q, kind = ops[i][0], ops[i][4]
        if kind is not None and kind[0] == "arrive":
            after[i] = {}
            continue
        ck = clock[q]
        w = []
        for j in sorted(deps[i], key=lambda k: -pos[k]):
            key = ops[j][0] if ops[j][4] is None else ("x", j)
            if ck.get(key, -1) >= pos[j]:
                continue
            w.append(j)
            signal.add(j)
            for k2, v2 in after[j].items():
                if ck.get(k2, -1) < v2:
                    ck[k2] = v2
            ck[key] = pos[j]
        waits[i] = w
        after[i] = dict(ck)
    count = {q: 0 for q in queue}
    mark = {}
    ndma = 0
    for i in order:
        q, fn, kind = ops[i][0], ops[i][1], ops[i][4]
        if kind is not None and kind[0] == "arrive":
            mark[i] = (kind[1], kind[2])
            continue
        for j in waits[i]:
            queue[q].wait_ge(T.sem[mark[j][0]], mark[j][1])
        ins = fn()
        if kind is None:
            if i in signal:
                count[q] += 1
                mark[i] = (q, count[q])
                ins.then_inc(T.sem[q], 1)
        elif kind[0] == "dma":
            mark[i] = ("d%d" % ndma, 16)
            ins.then_inc(T.sem["d%d" % ndma], 16)
            ndma += 1
    for q in ("V", "S", "P", "G"):
        if count[q]:
            g.wait_ge(T.sem[q], count[q])
    for s, n in last:
        g.wait_ge(T.sem[s], n)
    for k in range(ndma):
        g.wait_ge(T.sem["d%d" % k], 16)


def rank_program(g, core, T, topo):
    routes = _routes(T, topo)
    rank = T.rank_of(core)
    if rank is None:
        _relay(g, core, T, topo, routes)
        return
    A = AluOpType
    ACT = ActivationFunctionType
    ops = []
    other = {}
    hints = []
    cy, ga = OPT["cy"], OPT["ga"]

    def v(name, a=0, b=None, s=1):
        if b is None:
            b = SCRATCH[name][1][1]
        ap = T[name][:, a:b] if s == 1 else T[name][:, a:b:s]
        return (ap, [(name, a, b, s)], len(range(a, b, s)), SCRATCH[name][2], False)

    def col(name, j):
        return v(name, j, j + 1)

    def ind(w, o):
        return (w[0].indirect(o[0]), w[1] + o[1], 16 * o[2], w[3], True)

    def ap(x):
        return x[0] if isinstance(x, tuple) else x

    def regs(*xs):
        out = []
        for x in xs:
            if isinstance(x, tuple):
                out += x[1]
        return out

    def price(n, first, sides, full=1.0):
        if first[4]:
            return 50.0 + n * ga * cy
        if full == 1.0 and all(s[3] in (BF, U16) for s in sides):
            full = 0.5
        return max(64.0, n * full) * cy

    def tt(o, a, b, op):
        two = 1.01 if a[1][0][0].startswith("ps") else 2.0
        ops.append(("V", lambda: g.vector.tensor_tensor(o[0], a[0], b[0], op), regs(a, b), o[1], None, price(o[2], a, [], two)))

    def ts(o, a, s1, op0, s2=None, op1=None):
        c = price(o[2], a, [o, a])
        if op1 is None:
            ops.append(("V", lambda: g.vector.tensor_scalar(o[0], a[0], ap(s1), None, op0), regs(a, s1), o[1], None, c))
        else:
            ops.append(("V", lambda: g.vector.tensor_scalar(o[0], a[0], ap(s1), ap(s2), op0, op1), regs(a, s1, s2), o[1], None, c))

    def cp(o, a):
        ops.append(("V", lambda: g.vector.tensor_copy(o[0], a[0]), regs(a), o[1], None, price(o[2], a, [o, a])))

    def scatter(w, off, a):
        ops.append(("V", lambda: g.vector.tensor_copy(w[0].indirect(off[0]), a[0]), regs(a, off), w[1], None, 50.0 + 3.5 * cy * a[2]))

    def scan(o, d0, d1, init, op0, op1):
        ops.append(("V", lambda: g.vector.tensor_tensor_scan(o[0], d0[0], d1[0], ap(init), op0, op1), regs(d0, d1, init), o[1],
                    None, price(o[2], d0, [o, d0, d1])))

    def fill(o, c, first="V"):
        ops.append(("V", lambda: g.vector.memset(o[0], c), [], o[1], None, price(o[2], o, [o])))
        if first != "V":
            on_vector = ops.pop()
            if first == "G":
                iota(o, [[0, o[2]]], int(c))
            else:
                z = v("cmod", 0, o[2])
                ops.append(("S", lambda: g.scalar.activation(o[0], z[0], ACT.Identity, bias=c, scale=0.0), z[1], o[1], None,
                            price(o[2], z, [], 1.01)))
            other[len(ops) - 1] = on_vector

    def recip(o, a):
        ops.append(("V", lambda: g.vector.reciprocal(o[0], a[0]), regs(a), o[1], None, 190.0 + 6 * cy * o[2]))

    def quant(q, s, a):
        ops.append(("V", lambda: g.vector.quantize_mx(q[0], s[0], a[0]), regs(a), regs(q, s), None, 12.0 + 0.22 * a[2]))

    def act(o, a, f=ACT.Copy, bias=None, scale=None, acc=None, first="S"):
        kw = {}
        if bias is not None:
            kw["bias"] = ap(bias)
        if scale is not None:
            kw["scale"] = scale
        if acc is not None:
            kw["accum_out"] = acc[0]
        c = price(o[2], a, [], 1.01) + (20.0 if acc is not None else 0.0) + (15.0 if a[4] else 0.0)
        if acc is None and f != ACT.Sign:
            if f == ACT.Relu:
                ts(o, a, scale, A.mult, 0.0, A.max)
            elif bias is not None:
                ts(o, a, scale, A.mult, bias, A.add)
            elif scale is not None:
                ts(o, a, scale, A.mult)
            else:
                cp(o, a)
            on_vector = ops.pop()
            other[len(ops)] = on_vector
        ops.append(("S", lambda: g.scalar.activation(o[0], a[0], f, **kw), regs(a, bias), regs(o, acc), None, c))
        if first == "V":
            other[len(ops) - 1], ops[-1] = ops[-1], other[len(ops) - 1]

    def affine(o, a, scale, bias):
        act(o, a, ACT.Identity, bias, scale)

    def mm(o, lq, ls, rq, rs):
        ops.append(("P", lambda: g.tensor.matmul_mx(o[0], lq[0], ls[0], rq[0], rs[0], True, True), regs(lq, ls, rq, rs), o[1],
                    None, (o[2] + 16) * cy))

    def iota(o, pat, base, ch=0):
        c = 130.0 + 2 * cy * o[2]
        if o[3] == I32:
            ops.append(("G", lambda: g.iota(o[0], pat, base, ch), [], o[1], None, c))
        else:
            ops.append(("G", lambda: g.iota(o[0], pat, base, ch, allow_small_or_imprecise_dtypes=True), [], o[1], None, c))

    def dma(q, o, a, rd, wr, cost=1500.0):
        e = g.sync if q == "Y" else g.scalar
        ops.append((q, lambda: e.dma_start(o, a), rd, wr, ("dma",), cost))

    def send(fn, rd):
        ops.append(("G", fn, rd, [], ("remote",), OPT["issue"]))

    def u8(x):
        return x[0].bitcast(dt.uint8)

    def u32(x):
        return (x[0].bitcast(dt.uint32), x[1], x[2], x[3], False)

    def e(k, a=0, b=48, s=1):
        return v("e", 72 * k + a, 72 * k + b, s)

    def srt(k, a=0, b=48):
        return v("srt", 56 * k + a, 56 * k + b)

    def g0(k):
        return v("gg", k, C, 8)

    def g1(k):
        return v("gg", 448 + k, 640, 8)

    dma("Y", T.ut[:], T.u[:], [], v("ut")[1], 1700.0)
    dma("Y", T.X0[:], T.x[:], [], v("X0")[1], 2050.0)
    dma("Y", u8(v("wq")), T.wc[:], v("X0")[1], v("wq")[1], 2500.0)
    dma("Y", T.wp[:], T.ws[:], v("X0")[1], v("wp")[1], 2500.0)
    dma("Y", T.vt[:], T.v[:], v("X0")[1], v("vt")[1], 2500.0)

    iota(v("ci", 0, 1), [[0, 1]], 0, 1)
    iota(v("cmod"), [[0, 12], [1, 16]], 0)
    iota(v("ci", 8, 24), [[-1, 2], [16, 8]], 1)
    iota(v("iof"), [[1, 192]], 0)
    iota(v("tmpe", 0, 147), [[-16, 3], [1, 49]], 0)
    iota(v("tmpd", 0, 64), [[0, 2], [16, 32]], -16 - C)
    iota(v("tmpd", 64, 96), [[0, 2], [16, 16]], -16 - 96)
    iota(v("cf", 24, 26), [[1, 2]], 24)
    pm = col("cf", 0)
    fill(v("TT", 0, 12 * 192, 192), 0.0)
    ts(col("ci", 1), col("ci", 0), 15, A.bitwise_and)
    fill(v("FW", 0, 400, 207), -BIG)
    cp(pm, col("ci", 1))
    cp(v("uo"), v("ci", 8, 24))
    ts(v("D"), v("cmod"), pm, A.is_equal, 2 * BIG, A.mult)
    ts(v("D"), v("D"), -BIG, A.add)
    fill(v("keep"), 1.0)
    fill(v("keep", 0, 192, 16), 0.0)
    fill(v("R"), BIG)
    fill(v("R", 16, 192, 16), -BIG)
    fill(col("KW", 15), 256 * U)
    fill(v("neg"), -BIG)
    iota(v("SG", C, 2400, 200), [[-16, 12]], -15)
    fill(col("acc", 12 + 11), C - 1.0, "S")
    fill(v("lur"), BIG)
    fill(v("lur", 0, 23), -BIG)
    act(v("lun"), v("lur"), ACT.Copy, None, -1.0)
    for w in range(3):
        act(v("D3", w, 96, 3), v("D", min(w, 1), 64, 2))
    fill(v("R3"), BIG, "S")
    fill(v("R3", 24, 72, 24), -BIG, "S")
    affine(col("cf", 1), pm, -U, (7.5 - C) * U)
    act(col("sA", 0), col("cf", 1))
    affine(v("dn"), v("iof"), -U, 256 * U)
    fill(v("ea", 0, 294, 2), -EVEN, "S")
    fill(v("ea", 0, 294, 98), 0.0, "S")
    ts(v("ea", 1, 294, 2), v("tmpe", 0, 147), pm, A.is_lt, 0.5, A.add)
    fill(v("eb", 1, 294, 2), -EVEN, "S")
    fill(v("eb", 96, 294, 98), 0.0, "S")
    fill(v("ka", 0, 144, 3), BIG, "S")
    fill(col("ka", 1), -256 * U, "S")
    fill(v("kb", 1, 144, 3), 0.0, "S")
    fill(v("kb", 2, 144, 3), BIG, "S")
    for j in range(2):
        affine(col("cf", 8 + j), pm, 1.0, 16 * j + 1.5)
        affine(col("cf", 16 + j), pm, 16 * U, (256 * j - C - 0.5 + HALF) * U)
    affine(col("cf", 22), pm, 16 * U, -97.5 * U)
    affine(col("cf", 23), pm, -32 * U, (HALF + 96) * 32 * U)
    fill(v("k3"), 1.0, "G")
    fill(v("k3", 0, 576, 3), 0.0, "G")
    affine(v("cw"), v("tmpd"), 1.0, pm)
    act(v("f1", 2, 72, 3), v("cw", 1, 25))
    affine(v("cu"), v("cw", 1, 25), U, U)
    fill(v("f0"), 1.0, "G")
    fill(v("f0", 0, 72, 3), 0.0, "G")
    fill(v("gg", 0, C), 1.0, "G")
    fill(g0(0), 0.0, "G")
    fill(g0(4), -1.0, "G")
    fill(v("gg", 448, 640), WHOLE, "G")
    fill(g1(2), -0.5, "S")
    fill(v("zero"), 0.0, "G")
    fill(e(5, 0, 2), -97 * U, "G")
    fill(srt(2, 0, 56), (HALF - C) * U, "G")
    for name in ("XW", "MW", "GW", "ZW", "ZM", "G2"):
        fill(v(name), LOW, "G")
    for t in range(2):
        if len(OPT["runs"][t]) > 1:
            fill(v("X%d" % (t + 1), 768, 1024), 0.0, "G")
    pieces = [[(a, b, a >= C) for (a, b) in OPT["send"][t] + OPT["own"][t]] for t in range(2)]
    for k in range(5):
        short = {(a, b) for p in pieces for (a, b, _) in p[k:k + 1] if b - a < 128}
        for (a, b) in short:
            fill(v("Z", 768 * k + 4 * (b - a), 768 * k + 512) if a % C else v("Z", 768 * k, 768 * k + 4 * (128 - b + a)), 0.0, "G")

    quant(v("uq"), v("us"), v("ut"))
    quant(v("xq0"), v("xs0"), v("X0"))
    quant(v("vq"), v("vs"), v("vt"))
    cp(u32(v("usq")), ind(u32(v("uq")), v("uo", 0, 8)))
    act(v("uss"), ind(v("us"), v("uo", 0, 8)))
    cp(u32(v("ukq")), ind(u32(v("uq")), v("uo", 8, 16)))
    act(v("uks"), ind(v("us"), v("uo", 8, 16)))

    last = []
    sent = [0]
    landed = {}
    for t in range(2):
        X, Xn, SQ, SO = "X%d" % t, "X%d" % (t + 1), "SQ%d" % t, "SQ%d" % (t + 1)
        xq, xs = "xq%d" % t, "xs%d" % t
        aP = "ps2"
        two = t > 0 and len(OPT["runs"][t - 1]) > 1
        s0, s1 = OPT["sc"][two]

        def row(q, a, b):
            if two and b > 128:
                return v("ps%d" % (3 + q), a - 64, b - 64)
            return v("ps%d" % q, a, b)

        def spans(a, b):
            if two and b > 128 and (a < 64 or (a < 128 and b == C)):
                s = min(128, max(64, b - 64))
                return [(a, s), (s, b)] if a < s else [(a, b)]
            return [(a, b)]

        for (a, b, k) in ((0, 128, 0), (64, C, 3)) if two else ((0, C, 0),):
            for q in range(2):
                mm(v("ps%d" % (k + q), 0, b - a), v("usq"), v("uss"), v(xq, a, b), v(xs, a, b))
        mm(v(aP, 0, C), v("ukq"), v("uks"), v(xq, 0, C), v(xs, 0, C))
        for (a, b) in OPT["cuts"][two]:
            tt(v("sm", a, b), row(0, a, b), v("D", a, b), A.min)
            scan(v("hold", a, b), v("R", a, b), v("sm", a, b), -BIG if a else col("D", 0), A.min, A.max)
            tt(v("eq", a, b), row(0, a, b), v("hold", a, b), A.is_equal)
            scan(v("ne", a, b), v("keep", a, b), v("eq", a, b), 0.0, A.mult, A.subtract)
        for (a, b) in ((s0, 8), (8, s1)) if two else ((s0, s1),):
            act(v("SG", 200 * a, 200 * b, 200), v("ne", 16 * a + 15, 16 * b, 16), ACT.Copy, None, -1.0, first="V")
        for i in range(12):
            m = 16 * i + 16
            own = col("hold", m - 1)
            if s0 <= i < s1:
                o = 200 * i
                for (a, b) in spans(1, C):
                    act(v("SG", o + a, o + b), row(1, a, b), ACT.Sign, own, -1.0)
                act(v("junk", o, o + m), v("SG", o, o + m), ACT.Relu, None, None, col("acc", i))
                if m < C:
                    act(v("junk", o + m, o + C + 1), v("SG", o + m, o + C + 1), ACT.Relu, None, -1.0, col("acc", 12 + i))
                continue
            o = 192 * i
            for (a, b) in spans(1, m):
                ts(v("TT", o + a, o + b), row(0, a, b), own, A.is_ge)
            if m < C:
                for (a, b) in spans(m, C) if m < 128 else [(m, C)]:
                    ts(v("TT", o + a, o + b), row(0, a, b), own, A.is_gt)
            scan(v("SUM", 96 * i, 96 * i + 96), v("TT", o, o + 96), v("TT", o + 96, o + C), col("ne", m - 1), A.add, A.add)
        late = s1 - OPT["late"][two]
        if late > s0:
            tt(v("SUM", 96 * s0 + 95, 96 * late, 96), v("acc", 12 + s0, 12 + late), v("acc", s0, late), A.subtract)
        for i in range(late, s1):
            ts(col("RK", i), col("acc", 12 + i), col("acc", i), A.subtract)
        cp(v("RK", 0, late), v("SUM", 95, late * 96, 96))
        if s1 < 12:
            cp(v("RK", s1, 12), v("SUM", 96 * s1 + 95, 12 * 96, 96))
        act(v("r", 0, 96), ind(v("lur"), v("RK", 0, 6)), first="V")
        act(v("r", 96, C), ind(v("lur"), v("RK", 6, 12)))
        scan(v("FW", 1, C), v(aP, 0, C - 1), v("r", 1, C), -BIG, A.max, A.min)
        scan(v("tid"), v("r"), v("neg"), 0.0, A.add, A.add)
        scan(v("FW", 208, 400), v(aP, 0, C), v("FW", 0, C), -BIG, A.max, A.min)
        act(v("nr"), ind(v("lun"), v("RK")))
        scan(v("M1"), v("r"), v(aP, 0, C), -BIG, A.min, A.max)
        tt(v("aS"), v(aP, 0, C), v("nr"), A.min)
        for j in range(2):
            act(v("junk", 2400 + 200 * j, 2400 + 200 * j + C), v("tid"), ACT.Sign, col("cf", 8 + j), 0.5 / BIG, col("acc", 24 + j))
        for b in range(4):
            act(v("XH", C * b, C * b + C), v(X, b, 768, 4) if t == 0 else v(SQ, 576 * b + 2, 576 * b + 576, 3), ACT.Copy, None, 0.5)
        tt(v("rec"), v(aP, 0, C), v("FW", 0, C), A.is_le)
        tt(v("ev"), v(aP, 0, C), v("FW", 207, 399), A.is_le)
        scan(v("KW", 16, 208), v("rec"), v("dn"), 0.0, A.mult, A.max)
        on = v("OE")
        ts(on, v("acc", 24, 26), 0.5, A.mult, 95.0, A.add)
        scan(v("KW", 208, 400), v("ev"), v("dn"), 0.0, A.mult, A.max)
        scan(v("KW", 400, 592), v("ev"), v("KW", 15, 207), 0.0, A.mult, A.max)
        rows = (v("M1"), v("FW", 208, 400), v("aS"))
        act(e(1, 0, 32), ind(rows[2], on))
        act(e(2, 0, 64, 2), ind(rows[0], on))
        for w in range(3):
            tt(v("x3", w, 96, 3), ind(rows[w], on), v("D3", w, 96, 3), A.min)
        tt(e(2, 1, 64, 2), ind(rows[1], on), e(1, 0, 32), A.max)
        scan(e(21, 0, 72), v("R3"), v("x3", 0, 72), -BIG, A.min, A.max)
        for j in range(3):
            o = 98 * j
            act(v("eb", o, o + 96, 2), e(2), ACT.Sign, e(21, 24 * j + 23, 24 * j + 24), -1.0)
            scan(v("es", o, o + 97), v("ea", o, o + 97), v("eb", o, o + 97), 0.0, A.add, A.subtract)
        re = v("RE", 0, 3)
        ts(re, v("es", 96, 294, 98), 0.5, A.mult)
        for w in range(2):
            affine(e(5, 2 + w, 66, 2), ind(v("iof"), on), U, -96 * U)
        affine(v("ka", 7, 199, 6), ind(v("iof"), on), U, -255 * U)
        act(v("kb", 0, 192, 6), ind(v("KW", 16, 208), on))
        act(v("kb", 3, 195, 6), ind(v("KW", 208, 400), on))
        tt(e(8), e(5), e(5, 2, 50), A.subtract)
        tt(e(7, 0, 32), ind(v("KW", 16, 208), on), v("ka", 1, 193, 6), A.subtract)
        tt(v("ka", 4, 196, 6), ind(v("KW", 400, 592), on), e(7, 0, 32), A.subtract)
        act(e(10), e(5, 2, 50), ACT.Copy, None, 1.0 / U)
        affine(e(11), e(5), 255.0 / U, 97.0 * 256 - HALF * U)
        tt(v("ka", 2, 144, 3), e(10), e(11), A.add)
        scan(v("ko"), v("ka", 0, 144), v("kb", 0, 144), 0.0, A.add, A.min)
        scatter(srt(0), re, e(8))
        scan(srt(2, 1, 49), v("zero"), srt(0), (HALF - C) * U, A.add, A.subtract)
        scan(v("sA", 1, 48), v("zero", 0, 47), srt(0, 0, 47), col("cf", 1), A.add, A.subtract)
        scatter(srt(1), re, v("ko", 2, 144, 3))
        act(v("sB", 0, 48), srt(2), ACT.Identity, ROUND, 32.0, first="V")
        act(v("sB", 48, 96), v("sA", 0, 48), ACT.Identity, ROUND, 32.0, first="V")
        tt(v("bm"), v("sB", 0, 48), v("sB", 48, 96), A.subtract)
        for j in range(2):
            act(v("junk", 2800 + 56 * j, 2848 + 56 * j), srt(2), ACT.Sign, col("cf", 16 + j), -1.0, col("acc", 26 + j))
        tt(v("XW", 1, 49), srt(2, 1, 49), srt(1), A.add)
        affine(v("XW", 57, 104), v("XW", 2, 49), 1.0, srt(0, 0, 1))
        affine(col("XW", 104), srt(1, 0, 1), 1.0, (C + HALF) * U)
        for w in range(2):
            affine(col("acc", 30 + w), srt(0, 0, 1), 1.0 / U, 0.5 - 0.5 * w)
            affine(g1(1 + 6 * w), v("cw", 33, 57), 1.0, col("acc", 30 + w))
        ts(v("OL"), v("acc", 26, 28), 0.5, A.mult, 24.0, A.add)
        for a in range(2):
            scan(v("MW", 56 * a + 1, 56 * a + 49), v("bm"), v("XW", 56 * a + 1, 56 * a + 49), LOW, A.add, A.min)
            act(v("GW", 40 * a + 1, 40 * a + 33), ind(v("XW", 56 * a, 56 * a + 56), v("OL")))
            tt(v("VV", 32 * a, 32 * a + 32), ind(v("MW", 56 * a, 56 * a + 56), v("OL")), v("GW", 40 * a, 40 * a + 32), A.max)

        vv = v("VV", 1, 57)
        ts(v("wi", 1, 57), vv, 255, A.bitwise_and)
        ts(v("wi", 129, 185), vv, 16, A.arith_shift_right)
        ts(v("wi", 57, 113), vv, 8, A.logical_shift_right, 255, A.bitwise_and)
        recip(g0(2), v("wi", 33, 57))
        tt(v("wf", 0, 24), v("VV", 1, 25), v("cu"), A.is_ge)
        tt(v("f1", 0, 72, 3), v("wf", 0, 24), v("wi", 1, 25), A.mult)
        tt(v("f1", 1, 72, 3), v("wi", 57, 81), v("wi", 129, 153), A.subtract)
        scan(v("f2"), v("f0"), v("f1"), 0.0, A.mult, A.add)
        cp(v("FG", 32, 56), v("f2", 2, 72, 3))
        cp(v("gg", 5, 640, 8), v("wi", 33, 113))
        for k in (0, 6):
            tt(g1(k), v("wi", 1, 25), v("wi", 161, 185), A.subtract)
        scan(v("g2"), v("gg", 0, C), v("gg", 448, 640), 0.0, A.mult, A.add)
        cp(v("FG", 0, 24), v("g2", 7, C, 8))

        def lists(w, a, b):
            return v("FG", 32 * w + a // 16, 32 * w + b // 16)

        d, via = routes[(t, rank)]
        back = routes[(t, rank ^ STEP[t])][1]
        lq, ls, zq, zs = "lq%d" % t, "ls%d" % t, "zq%d" % t, "zs%d" % t
        for k, (a, b, away) in enumerate(pieces[t]):
            n, o = b - a, 768 * k
            wide = max(n, 128)
            z = o + 4 * (wide - n) if a % C == 0 else o
            for p in range(4):
                w = v("XH", C * p, C * p + C)
                gt = v("GT", o + C * p, o + C * p + n)
                act(gt, ind(w, lists(1, a, b)))
                tt(v("Z", z + p, z + 4 * n, 4), ind(w, lists(0, a, b)), gt, A.add)
            if not away:
                quant(v(lq, PAD + b - wide, PAD + b), v(ls, PAD + b - wide, PAD + b), v("Z", o, o + 4 * wide))
                continue
            lo = a - 64 - (wide - n if a == C else 0)
            quant(v(zq, lo, lo + wide), v(zs, lo, lo + wide), v("Z", o, o + 4 * wide))
            sa, sem = _scales(t, k)
            codes, scales = v(zq, a - 64, b - 64), v(zs, sa - 64, b - 64)
            arr, hop = T.sem[sem], T.sem["hop%d" % k]
            if via is None:
                rid, pid = topo.addr(d, core)
                m = topo.mask(core, d)
                calls = [(lambda x=(u8(v(lq, PAD + a, PAD + b)), u8(codes), arr, T.sem.sent, pid, rid, m): g.remote_dma(*x), codes[1]),
                         (lambda x=(v(ls, PAD + sa, PAD + b)[0], scales[0], arr, T.sem.sent, pid, rid, m): g.remote_dma(*x), scales[1])]
                counts = [len(topo.engines(core, d))] * 2
            else:
                en = _first_hop(core, via, topo)
                trs = []
                for j in range(2):
                    rid, pid = topo.addr(via[j], core)
                    trs.append(RemoteDMATransfer(dst_ids=[DstId(rid=rid, pnc=pid)], dma_engine_mask=_bits(en[j]), remote_sem=hop,
                                                 src=u8(v(zq, a - 64 + n // 2 * j, a - 64 + n // 2 * (j + 1))),
                                                 dst=u8(v("rq", a - C, a - C + n // 2))))
                rid, pid = topo.addr(via[2], core)
                calls = [(lambda x=trs: g.remote_dma_fused(x, local_sem=T.sem.sent), codes[1]),
                         (lambda x=(v("rs", sa - C, b - C)[0], scales[0], hop, T.sem.sent, pid, rid, _bits(en[2])): g.remote_dma(*x),
                          scales[1])]
                counts = [len(en[0] + en[1]), len(en[2])]
            if sa == b:
                calls, counts = calls[:1], counts[:1]
            sent[0] += sum(counts)
            for fn, rd in calls if OPT["first"] == "codes" else calls[::-1]:
                send(fn, rd)
            for j, c in enumerate([d, d] if back is None else back):
                if j < (1 if back is None else 2) or sa < b:
                    landed[sem] = landed.get(sem, 0) + len(topo.engines(c, core)[::1 if back is None else OPT["hand"]])
            if sa < b:
                ops.append(("X%d" % k, None, [], v(lq, PAD + sa, PAD + b)[1] + v(ls, PAD + sa, PAD + b)[1],
                            ("arrive", sem, landed[sem]), OPT["far"][t][min(k, 1)]))

        affine(e(16), ind(srt(2, 0, 56), re), 256.0 / U, (C - HALF) * 256.0)
        affine(e(17), e(5), 2.0 - 1.0 / U, 2 * U)
        act(e(18), v("ko", 1, 144, 3), ACT.Copy, None, -2.0)
        tt(e(19), e(10), e(17), A.add)
        tt(e(20), e(19), e(18), A.add)
        affine(v("tb", 0, 24), e(5, 0, 48, 2), 32.0, (HALF + 97) * 32 * U)
        affine(v("tb", 24, 48), e(5, 0, 48, 2), 32.0, col("cf", 23))
        affine(v("tb", 48, 96), v("tb", 0, 48), 1.0, ROUND)
        tt(v("bm2"), v("tb", 48, 72), v("tb", 72, 96), A.subtract)
        act(v("junk", 3000, 3024), e(5, 0, 48, 2), ACT.Sign, col("cf", 22), -1.0, col("acc", 28))
        ts(v("OP"), v("cf", 24, 26), col("acc", 28), A.add)
        tt(v("ZW", 2, 50), e(20), e(16), A.add)
        act(v("G2", 1, 33), ind(v("ZW"), v("OP")))
        for w in range(2):
            scan(v("ZM", 2 + w, 50, 2), v("bm2"), v("ZW", 2 + w, 50, 2), LOW, A.add, A.min)
        tt(v("V2"), ind(v("ZM"), v("OP")), v("G2", 0, 32), A.max)
        ts(v("pi", 0, 32), v("V2"), 17, A.arith_shift_right)
        ts(v("pi", 32, 64), v("V2"), 255, A.bitwise_and)
        ts(v("pi", 64, 96), v("V2"), 8, A.logical_shift_right, 511, A.bitwise_and)
        tt(v("pf", 0, 32), v("cw", 64, 96), v("pi", 0, 32), A.subtract)
        act(v("pf", 32, 64), v("pf", 0, 32), ACT.Relu, None, -512.0)
        tt(v("pf", 64, 96), v("pf", 0, 32), v("pi", 64, 96), A.add)
        tt(v("pf", 96, 128), v("pf", 32, 64), v("pi", 32, 64), A.min)
        tt(v("pf", 128, 160), v("pf", 64, 96), v("pf", 96, 128), A.add)
        cp(v("PQ", 0, 28), v("pf", 129, 157))
        if t == 1:
            act(v("fo"), ind(v("iof"), lists(1, 0, 2 * C)))
            dma("Y", T.ol[:], T.fo[0:128:16, :], v("fo")[1], [])

        turn = list(OPT["own"][t]) + [(_scales(t, k)[0], b) for k, (a, b) in enumerate(OPT["send"][t]) if _scales(t, k)[0] < b]
        for i, (a, b) in enumerate(turn):
            lo = b - max(b - a, 128)
            for p in range(4):
                bank = "ps%d" % (4 * ((len(turn) - i) % 2) + p)
                mm(v(bank, 0, b - lo), v("wq", 128 * p, 128 * p + 128), v("wp", 128 * p, 128 * p + 128),
                   v(lq, PAD + lo, PAD + b), v(ls, PAD + lo, PAD + b))
                act(v("HH", 384 * p + a, 384 * p + b), v(bank, a - lo, b - lo), ACT.Copy, None, 2.0 ** -6, first="VS"[p % 2])
        if t == 0:
            for p in range(4):
                act(v(SQ, 576 * p + 2, 576 * p + 576, 3), v(X, p, 768, 4))
        picks = {}
        for (a, b) in OPT["runs"][t]:
            for p in range(4):
                hw = v("HH", 384 * p, 384 * p + 384)
                o = 576 * p
                cut = [(a, (a + b) // 2), ((a + b) // 2, b)] if p in OPT["halves"] and b - a == C else [(a, b)]
                for w in range(2):
                    for (i, j) in cut if w == 0 else [(a, b)]:
                        act(v(SQ, o + 3 * i + w, o + 3 * j, 3), ind(hw, v("PQ", 16 * w + i // 16, 16 * w + j // 16)), first="VS"[w])
                        picks.setdefault(a, []).append(len(ops) - 1)
                        if a and OPT["hint"]:
                            hints.extend((k, len(ops) - 1, 0.0) for k in picks[0][:OPT["hint"]])
                for (i, j) in cut:
                    scan(v(SO, o + 3 * i, o + 3 * j), v("k3", 0, 3 * (j - i)), v(SQ, o + 3 * i, o + 3 * j), 0.0, A.mult, A.add)
                    act(v(Xn, 4 * i + p, 4 * j, 4), v(SO, o + 3 * i + 2, o + 3 * j, 3), first="V")
            n = max(b, a + 128)
            quant(v("xq%d" % (t + 1), a, n), v("xs%d" % (t + 1), a, n), v(Xn, 4 * a, 4 * n))

    for k, (a, b) in enumerate(OPT["runs"][1]):
        lo = b - max(b - a, 128)
        mm(v("ps%d" % k, 0, b - lo), v("vq"), v("vs"), v("xq2", lo, b), v("xs2", lo, b))
        dma("Y", T.oc[:, 4 * a:4 * b], u8(v("xq2", a, b)), v("xq2", a, b)[1], [])
        act(v("yo", a, b), v("ps%d" % k, a - lo, b - lo), first="V")
        dma("Y", T.y[:, a:b], T.yo[:, a:b], v("yo", a, b)[1], [])
    for k in range(4):
        dma("S", T.osc[4 * k:4 * k + 4, :], T.xs2[32 * k:32 * k + 4, 0:C], v("xs2", 0, C)[1], [])
    last.append(("sent", sent[0]))
    _emit(g, T, ops, last, other, hints)
